import numpy as np, ml_dtypes
CORES = [13,21,141,149]
N = 4
BF = ml_dtypes.bfloat16
W, L, OR, ST, NEED = 2048, 256, 4, 3, 9
def forest(rng):
    o = np.argsort(rng.random((N, 8, 16, L, OR)), axis=2); k = np.arange(16).reshape(1, 1, 16, 1, 1)
    q = (rng.random(o.shape) * k).astype(np.int64); p = np.zeros_like(o)
    np.put_along_axis(p, o, np.take_along_axis(o, q, 2), 2)
    return np.where(rng.random(p.shape) < 0.1, k, p)
def limits(rng, lo, n):
    base = np.argsort(rng.random((N, 8, 1, L)), axis=-1) % n + lo
    return np.clip(base + rng.integers(-2, 3, (N, 8, 16, L)), 0, 15)
def parts(rng):
    x = rng.integers(0, 16, (N, 8, 16, W)); c = rng.integers(0, W, (N, 8, 16, L, OR)); p = forest(rng); a = limits(rng, 3, 8)
    v = rng.integers(0, 33, (N, 8, OR, L))
    o = np.arange(OR).reshape(1, 1, OR, 1); fav = rng.integers(0, OR, (1, 8, 1, L)); stick = rng.random((1, 8, 1, L)) < 0.5
    v = np.where(stick, np.where(o == fav, rng.integers(20, 33, v.shape), rng.integers(0, 7, v.shape)), v)
    return x, c, p, a, v
def bf(a): return np.ascontiguousarray(a).astype(np.float32).astype(BF)
def pack(x, c, p, a, v):
    return {"xt": bf(x.reshape(N, 128, W)), "pg": np.ascontiguousarray(c.reshape(N, 128, L * OR)).astype(np.int32), "pre": bf(p.reshape(N, 128, L * OR)),
            "lim": bf(a.reshape(N, 128, L)), "vv": np.ascontiguousarray(v.reshape(N, 8 * OR, L)).astype(np.int32)}
def setup_inputs(rng):
    return pack(*parts(rng))
def setup_inputs_ties(rng):
    x, c, p, a, v = parts(rng)
    dl = rng.integers(1, 8, (1, 8, 1, 1)); x = rng.integers(0, 9, (N, 8, 16, 1)) + dl * rng.integers(0, 2, x.shape)
    k = np.argsort(rng.random((N, 8, 1, L)), axis=-1) % 5; n = np.array([0, 2 * NEED - 16, 2 * NEED - 15, NEED - 1, 16])[k]
    a = np.where(np.argsort(rng.random(a.shape), axis=2) < n, dl, dl - 1)
    t = rng.choice(np.array([0, 1, 16, 31, 32]), (N, 8, 1, L))
    v = np.where(np.argsort(rng.random(v.shape), axis=2) < 2, t, np.minimum(rng.integers(0, 33, v.shape), t))
    return pack(x, c, p, a, v)
def setup_inputs_ends(rng):
    x, c, p, a, v = parts(rng)
    x = 15 * rng.integers(0, 2, x.shape); x[..., 0] = 0; x[..., W - 1] = 15
    e = rng.choice(np.array([0, 1, W // 2, W - 2, W - 1]), c.shape); c = np.where(rng.random((N, 8, 1, L, 1)) < 0.5, e, c)
    T = np.arange(16).reshape(1, 1, 16, 1, 1); k = rng.integers(0, 6, (N, 8, 1, L, 1))
    q = np.where(k == 0, T, np.where(k == 1, np.maximum(T - 1, 0), np.where(k == 2, 0, np.where(k == 3, 15, (T + 1) % 16))))
    p = np.where(k == 5, rng.integers(0, 16, p.shape), q)
    k = np.argsort(rng.random((N, 8, 1, L)), axis=-1) % 5; pos = np.argsort(rng.random(a.shape), axis=2)
    a = np.where(k == 0, 0, np.where(k == 1, 15, np.where(k == 2, 14, np.where(pos < np.where(k == 3, NEED, NEED - 1), 15, 0))))
    o = np.arange(OR).reshape(1, 1, OR, 1); k = rng.integers(0, 5, (N, 8, 1, L))
    v = np.where(k == 0, 0, np.where(k == 1, 32, np.where(k == 2, 32 * (o == 0), np.where(k == 3, 32 * (o == OR - 1), v))))
    z = int(rng.integers(0, 8)); w = np.argsort(rng.random(L)) % 4; x[:, z] = 15 * (np.arange(W) & 1)
    tt = T[0]; ring = (w == 0).reshape(1, 1, L, 1); climb = (w == 1).reshape(1, 1, L, 1)
    par = rng.integers(0, 2, (N, 1, L, OR)); even = c[:, z] - (c[:, z] & 1)
    c[:, z] = np.where(ring, even + ((par + tt) & 1), np.where(climb, even + ((par + (tt == 15)) & 1), c[:, z]))
    p[:, z] = np.where(ring, (tt + 1) % 16, np.where(climb, 0, p[:, z]))
    a = np.where(w == 1, 15, a); a[:, z] = np.where(w <= 1, 14 * rng.integers(0, 2, (N, 16, L)), a[:, z])
    v[:, z] = np.where(w == 1, 32 * (o[0] < 5) - 1 * (o[0] == 3), v[:, z])
    return pack(x, c, p, a, v)
def setup_inputs_alike(rng):
    x, c, p, a, v = parts(rng)
    x[:, ::2] = x[:, ::2][..., rng.integers(0, 8, W)]
    few = rng.integers(0, W, 5); few[0] = 0; few[1] = W - 1; c = few[rng.integers(0, 5, c.shape)]
    m = (rng.random((N, 8, 1, L, 1)) < 0.3) | (rng.random((N, 1, 1, L, 1)) < 0.3)
    c = np.where(m, c[:, :, :1], c); a[:, rng.integers(0, 8)] = 0
    return pack(x, c, p, a, v)
def setup_inputs_same(rng):
    x, c, p, a, v = parts(rng)
    o = np.arange(OR).reshape(1, 1, OR, 1); fav = rng.integers(0, OR, (1, 8, 1, L))
    v = np.where(o == fav, 32, rng.integers(0, 3, v.shape)); a = limits(rng, 5, 6)
    a[:, rng.integers(0, 8)] = rng.integers(0, 5, (N, 16, L))
    return pack(x, c, p, a, v)
def setup_inputs_spread(rng):
    x, c, p, a, v = parts(rng); E = np.array([0.25, 0.5, 1.0, 2.0, 4.0])
    def un(n, shape, by): return np.minimum((n * rng.random(shape) ** rng.choice(E, by)).astype(np.int64), n - 1)
    x = un(16, x.shape, (N, 8, 16, 1)); c = un(W, c.shape, (N, 8, 1, L, OR)); a = un(16, a.shape, (N, 8, 1, L)); v = un(33, v.shape, (N, 8, OR, 1))
    return pack(x, c, p, a, v)
def check_inputs(d):
    bad = []
    for k, hi in (("xt", 15), ("pg", W - 1), ("pre", 15), ("lim", 15), ("vv", 32)):
        b = np.asarray(d[k]).astype(np.float64)
        if not (np.min(b) >= 0 and np.max(b) <= hi and np.all(b == np.floor(b))): bad.append("range of " + k)
    return bad
def reference(xt, pg, pre, lim, vv):
    xs = np.ascontiguousarray(xt.astype(np.int32).reshape(N, 8, 16, W).transpose(0, 1, 3, 2))
    cur = np.ascontiguousarray(pg.astype(np.int64).reshape(N, 8, 16, L, OR).transpose(0, 1, 3, 4, 2))
    prd = np.ascontiguousarray(pre.astype(np.int64).reshape(N, 8, 16, L, OR).transpose(0, 1, 3, 4, 2))
    a = np.ascontiguousarray(lim.astype(np.int32).reshape(N, 8, 16, L).transpose(0, 1, 3, 2))
    v = np.ascontiguousarray(vv.astype(np.int64).reshape(N, 8, OR, L).transpose(0, 1, 3, 2))
    m = np.zeros((N, 8, L), np.int64)
    g0 = np.arange(8).reshape(1, 8, 1); l0 = np.arange(L).reshape(1, 1, L)
    for s in range(N):
        h = ((np.arange(N) + s) % N).reshape(N, 1, 1)
        o = np.argmax(v, axis=3)
        c = cur[h, g0, l0, o]; p = prd[h, g0, l0, o]
        got = np.zeros((N, 8, L), np.int64)
        for t in range(ST):
            F = xs[h[..., None], g0[..., None], c]
            G = np.take_along_axis(F, p[..., None], 3)
            D = np.abs(F - G)
            ok = np.add.reduce((D <= a[:, :, :, None, :]).astype(np.int64), axis=4) >= NEED
            full = np.all(ok, axis=3)
            got = got + full
            c = np.where(full[..., None], (5 * c + 1) & (W - 1), np.where(ok, c, (5 * c + np.add.reduce(D, axis=4) + 1) & (W - 1)))
        cur[h, g0, l0, o] = c
        m = m + got
        odd = np.add.reduce(got, axis=1, keepdims=True) & 1
        v = v + 1 + odd[..., None]
        np.put_along_axis(v, o[..., None], np.add.reduce(ok.astype(np.int64), axis=3)[..., None], 3)
    return {"yg": np.ascontiguousarray(cur.transpose(0, 1, 4, 2, 3)).reshape(N, 128, L * OR).astype(np.float32),
            "yv": np.ascontiguousarray(v.transpose(0, 1, 3, 2)).reshape(N, 8 * OR, L).astype(np.float32), "ym": m.astype(np.float32)}

@@ -1,0 +1,465 @@
+from concourse.mybir import AluOpType, ActivationFunctionType
+
+OP, AF = AluOpType, ActivationFunctionType
+NCH, CN, NB = 4, 64, 4
+SUB, HW = 2, 32
+NSL, NST = 4, 3
+BIG = 2 ** 17
+HPW = 40
+TB = 512 // NCH
+
+PER = {"PGI": (256, "int32"), "PGB": (256, "int32"), "PRE": (256, "bfloat16"), "PW0": (256, "int32"), "PW": (256, "int32"), "CW": (256, "int32"),
+       "VI": (16, "int32"), "VB": (16, "bfloat16"), "KS": (28, "float32"), "KM": (20, "float32"), "KN": (16, "int32"), "LI": (4, "int32"), "LU": (4, "uint16"),
+       "E": (16, "bfloat16"), "EN": (16, "bfloat16"), "CB": (64, "int32"), "OFF": (64, "uint16"), "C16": (64, "float16"), "PO": (64, "uint16"),
+       "O1": (64, "int32"), "O2": (64, "int32"), "NS": (192, "bfloat16"), "FM": (12, "bfloat16"), "CNT": (4, "bfloat16"), "MI": (4, "int32"), "OD": (4, "bfloat16"),
+       "OUTF": (256, "float32"), "YV": (16, "float32"), "YM": (4, "float32"), "F": (1024, "bfloat16"), "F2": (1024, "bfloat16"), "D": (1024, "bfloat16"),
+       "C": (1024, "bfloat16"), "HP": (HPW * NSL, "bfloat16"), "HL": (HPW * NSL, "bfloat16")}
+ONE = {"XB": (2064, "bfloat16"), "LIM": (256, "bfloat16"), "LIMP": (256, "bfloat16"), "LS1": (256, "bfloat16"), "LS2": (256, "bfloat16"), "LS3": (256, "bfloat16"),
+       "ONES": (128, "bfloat16"), "BO": (128, "bfloat16"), "BO0": (128, "bfloat16"), "ID": (128, "bfloat16"), "WB": (144, "bfloat16"), "RI": (128, "int32"),
+       "RH": (128, "bfloat16"), "BIGI": (128, "bfloat16"), "NBO": (128, "bfloat16"), "IM64": (128, "bfloat16"), "IM32": (128, "bfloat16"), "IMV": (128, "bfloat16"),
+       "I16": (128, "float16"), "I5": (128, "float16"), "BI": (16, "int32"), "B16": (16, "float16")}
+SCRATCH = {}
+for _n in PER:
+    SCRATCH[_n] = ("sbuf", [128, PER[_n][0] * NCH], PER[_n][1])
+for _n in ONE:
+    SCRATCH[_n] = ("sbuf", [128, ONE[_n][0]], ONE[_n][1])
+for _n in ["lim", "tiny", "c0", "c1"] + ["ab%d" % _k for _k in range(NCH)]:
+    SCRATCH["P_" + _n] = ("psum", [128, 512], "float32")
+SEMAPHORES = ["v", "s", "t", "gc", "loc", "lh"] + ["ls%d" % _s for _s in range(1, NSL)]
+SEMAPHORES += ["%s_%d_%d" % (_b, _k, _s) for _b in ("hr", "hl") for _k in range(NCH) for _s in range(NSL)]
+
+
+def X(T, name, k, a=0, b=None, step=1):
+    w = PER[name][0]
+    return T[name][:, w * k + a:w * k + (w if b is None else b):step]
+
+
+GA, TC, HOP, GC = 1.15, 0.5, 5000, 1000
+SHORT, LAG, SEM = 150, 3000.0, 60.0
+AMP, SEED = 1000.0, 984
+
+
+def build():
+    ops = []
+
+    def op(q, fn, r=(), w=(), bank=None, cost=80.0, k=0, sem=None):
+        ops.append({"q": q, "fn": fn, "r": list(r), "w": list(w), "bank": bank, "cost": cost, "k": k, "sem": sem, "i": len(ops)})
+
+    def V(fn, r, w, n, k=0, bank=None):
+        op("v", fn, r, w, bank, max(64, n) + 15, k)
+
+    def S(fn, r, w, n, k=0, bank=None):
+        op("s", fn, r, w, bank, max(64, n) + 40, k)
+
+    def TE(fn, r, w, n, k=0, bank=None):
+        op("t", fn, r, w, bank, n * TC, k)
+
+    def dma(q, out, in_, r, w, cost=3000.0, k=0):
+        sem = "d%d" % sum(1 for o in ops if o["q"] in ("qs", "qa"))
+        if sem not in SEMAPHORES:
+            SEMAPHORES.append(sem)
+        op(q, (out, in_), r, w, None, cost, k, sem)
+
+    for k in range(NCH):
+        lo = CN * k
+        for o in range(4):
+            dma("qs" if o < 2 or k else "qa", lambda T, k=k, o=o: X(T, "VI", k, NB * o, NB * (o + 1)), lambda T, o=o, lo=lo: T.vv[o::4, lo:lo + CN], [], ["VI%d.%d" % (k, o)], 2500, k)
+        dma("qa" if k else "qs", lambda T, k=k: X(T, "PGI", k), lambda T, lo=lo: T.pg[:, 4 * lo:4 * (lo + CN)], [], ["PGI%d" % k], 3500, k)
+        dma("qa", lambda T, k=k: X(T, "PRE", k), lambda T, lo=lo: T.pre[:, 4 * lo:4 * (lo + CN)], [], ["PRE%d" % k], 3500, k)
+        if k == 0:
+            dma("qs", lambda T: T.XB[:, 0:2048], lambda T: T.xt[:], [], ["XBa"], 6000, k)
+            dma("qa", lambda T: T.XB[:, 2048:2064], lambda T: T.xt[:, 0:16], [], ["XBb"], 5000, k)
+            dma("qa", lambda T: T.LIM[:], lambda T: T.lim[:], [], ["LIM"], 4500, k)
+    op("g", lambda g, T: g.iota(T.BI[:], [[1, 4], [4, NB]], 0, 4 * NB), [], ["BI"], None, 250)
+    V(lambda g, T: g.vector.memset(T.ONES[:], 1.0), [], ["ONES"], 128)
+    V(lambda g, T: g.vector.memset(T.WB[:], 0.0), [], ["WB"], 144)
+    op("g", lambda g, T: g.affine_select(T.ID[:], T.ONES[:], [[-1, 128]], OP.is_equal, 0.0, 0, 1), ["ONES"], ["ID"], None, 500)
+    op("g", lambda g, T: g.iota(X(T, "PW0", 0), [[16, 16], [256, NB], [0, 4]], 0, 0), [], ["PW0"], None, 700)
+    op("g", lambda g, T: g.affine_select(T.BO0[:], T.ONES[:], [[-16, 8], [0, 16]], OP.is_ge, 0.0, 0, 1), ["ONES"], ["BO0"], None, 500)
+    op("g", lambda g, T: g.affine_select(T.BO[:], T.BO0[:], [[16, 8], [0, 16]], OP.is_ge, 0.0, 15, -1), ["BO0"], ["BO"], None, 500)
+    op("g", lambda g, T: g.iota(T.RI[:], [[1, 128]], 0, -1), [], ["RI"], None, 400)
+
+    def scaled(name, src, f):
+        V(lambda g, T: g.vector.tensor_scalar(T[name][:], T[src][:], float(f), None, OP.mult), [src], [name], 128)
+
+    V(lambda g, T: g.vector.tensor_scalar(T.BI[:], T.BI[:], 4 * CN - 1, None, OP.bitwise_and), ["BI"], ["BI"], 16)
+    V(lambda g, T: g.vector.tensor_copy(T.B16[:], T.BI[:]), ["BI"], ["B16"], 16)
+    scaled("IMV", "ID", -4 * CN)
+    scaled("I16", "ID", 1)
+    V(lambda g, T: g.vector.tensor_scalar(X(T, "PW0", 0), X(T, "PW0", 0), 16 * HW - 1, None, OP.bitwise_and), ["PW0"], ["PW0"], 256)
+    V(lambda g, T: g.vector.tensor_copy(T.WB[:, 15:143:16], T.BO[:, 0:128:16]), ["BO", "WB"], ["WBB"], 8)
+    scaled("I5", "ID", 5)
+    scaled("BIGI", "ID", BIG)
+    scaled("NBO", "BO", -(BIG // 16))
+    scaled("IM64", "ID", -64)
+    scaled("IM32", "ID", -32)
+    V(lambda g, T: g.vector.tensor_scalar(T.RI[:], T.RI[:], 15, None, OP.bitwise_and), ["RI"], ["RI"], 128)
+    V(lambda g, T: g.vector.tensor_scalar(T.RH[:], T.RI[:], 0, 0.5, OP.is_equal, OP.mult), ["RI"], ["RH"], 128)
+    for k in range(NCH):
+        V(lambda g, T, k=k: g.vector.tensor_copy(X(T, "VB", k), X(T, "VI", k)), ["VI%d.%d" % (k, o) for o in range(4)], ["VB%d" % k], 32, k)
+        V(lambda g, T, k=k: g.vector.tensor_scalar(X(T, "PGB", k), X(T, "PGI", k), BIG + 2047, None, OP.add), ["PGI%d" % k], ["PGB%d" % k], 256, k)
+        V(lambda g, T, k=k: g.vector.tensor_scalar(X(T, "CW", k), X(T, "PGB", k), BIG | 2047, None, OP.bitwise_and), ["PGB%d" % k], ["CW%d" % k], 256, k)
+        V(lambda g, T, k=k: g.vector.tensor_tensor(X(T, "PW", k), X(T, "PRE", k), X(T, "PW0", 0), OP.add), ["PRE%d" % k, "PW0"], ["PW%d" % k], 512, k)
+        for c in range(NB):
+            V(lambda g, T, k=k, c=c: g.vector.tensor_copy(T.LIMP[:, CN * k + 16 * c:CN * k + 16 * c + 16], T.LIM[:, CN * k + c:CN * k + CN:NB]),
+              ["LIM"], ["LIMP%d.%d" % (k, c)], 16, k)
+    op("g", "limsend", ["LIMP%d.%d" % (k, c) for k in range(NCH) for c in range(NB)], ["limsent"], None, 2000)
+    for s in range(1, NSL):
+        op("hop", "lim%d" % s, ["limsent"], ["LS%d" % s], None, 9000, 0, "ls%d" % s)
+    for s in range(NSL):
+        for k in range(NCH):
+            one_slice(s, k, op, V, S, TE, dma)
+    return ops
+
+
+def one_slice(s, k, op, V, S, TE, dma):
+    kt = lambda b: "%s%d" % (b, k)
+    lo, tb = CN * k, TB * k
+    ltags = ["LIMP%d.%d" % (k, c) for c in range(NB)] if s == 0 else ["LS%d" % s]
+    lname = "LIMP" if s == 0 else "LS%d" % s
+    st = "HL%d.%d" % (k, s - 1)
+    h0 = HPW * (s - 1)
+    V4 = 4 * NB
+    cb, ab = "c%d" % (k % 2), "ab%d" % k
+    cc = CN * k
+
+    def tiny(T, a, b):
+        return T.P_tiny[:, tb + a:tb + b]
+
+    def kmm(g, T):
+        g.tensor.matmul(tiny(T, 0, V4), T.I16[:], T.B16[:], True, False)
+        if s == 0:
+            return g.tensor.matmul(tiny(T, 0, V4), T.IMV[:], X(T, "VB", k), False, True)
+        g.tensor.matmul(tiny(T, 0, V4), T.IMV[:], X(T, "HL", k, h0, h0 + V4), False, False)
+        return g.tensor.matmul(tiny(T, 0, V4), T.IMV[:], X(T, "HL", k, h0 + V4, h0 + 2 * V4), False, True)
+    TE(kmm, ["IMV", "I16", "B16", st if s else kt("VB")], [kt("PSK")], 192, k, "tiny")
+    S(lambda g, T: g.scalar.activation(X(T, "KS", k, 0, V4), tiny(T, 0, V4), AF.Copy), [kt("PSK")], [kt("KSa")], V4, k, "tiny")
+    S(lambda g, T: g.scalar.activation(X(T, "KS", k, V4, 7 * NB), tiny(T, 0, 3 * NB), AF.Copy), [kt("PSK")], [kt("KSb")], V4, k, "tiny")
+    V(lambda g, T: g.vector.tensor_tensor(X(T, "KM", k), X(T, "KS", k, 0, 5 * NB), X(T, "KS", k, 2 * NB, 7 * NB), OP.min), [kt("KSa"), kt("KSb")], [kt("KM")], 40, k)
+    V(lambda g, T: g.vector.tensor_tensor(X(T, "KN", k), X(T, "KM", k, 0, V4), X(T, "KM", k, NB, 5 * NB), OP.min), [kt("KM")], [kt("KN")], 32, k)
+    V(lambda g, T: g.vector.tensor_scalar(X(T, "LI", k), X(T, "KN", k, 0, NB), 4 * CN - 1, None, OP.bitwise_and), [kt("KN")], [kt("LI")], NB, k)
+    V(lambda g, T: g.vector.tensor_copy(X(T, "LU", k), X(T, "LI", k)), [kt("LI")], [kt("LU")], NB, k)
+    V(lambda g, T: g.vector.tensor_copy(X(T, "CB", k), X(T, "CW", k).indirect(X(T, "LU", k))), [kt("CW"), kt("LU")], [kt("CB")], GA * CN + 60, k)
+    V(lambda g, T: g.vector.tensor_scalar(X(T, "OFF", k), X(T, "CB", k), 1 - BIG, None, OP.add), [kt("CB")], [kt("OFF")], CN, k)
+    V(lambda g, T: g.vector.tensor_copy(X(T, "PO", k), X(T, "PW", k).indirect(X(T, "LU", k))), [kt("PW"), kt("LU")], [kt("PO")], GA * CN + 60, k)
+    V(lambda g, T: g.vector.tensor_scalar(X(T, "C16", k), X(T, "CB", k), 1 - BIG, None, OP.add), [kt("CB")], [kt("C16")], CN, k)
+    for e in range(2):
+        V(lambda g, T, e=e: g.vector.tensor_copy(T.P_lim[:, 2 * lo + e:2 * (lo + CN):2], T[lname][:, lo:lo + CN]), ltags, ["PL%d.%d" % (k, e)], CN, k, "lim")
+    V(lambda g, T: g.vector.tensor_tensor(X(T, "E", k), X(T, "KS", k, 0, V4), X(T, "KN", k), OP.is_equal), [kt("KSa"), kt("KN")], [kt("E")], 32, k)
+    S(lambda g, T: g.scalar.activation(X(T, "EN", k), X(T, "E", k), AF.Identity, bias=1.0, scale=-1.0), [kt("E")], [kt("EN")], V4, k)
+
+    for t in range(NST):
+        last_step = s == NSL - 1 and t == NST - 1
+        for u in range(SUB):
+            f0, f1, y0, y1 = 16 * HW * u, 16 * HW * (u + 1), HW * u, HW * (u + 1)
+            fu, gu = "F%d.%d" % (k, u), "G%d.%d" % (k, u)
+            S(lambda g, T, y0=y0, y1=y1, f0=f0, f1=f1: g.scalar.activation(X(T, "F", k, f0, f1), T.XB[:].indirect(X(T, "OFF", k, y0, y1)), AF.Copy),
+              ["XBa", "XBb", kt("OFF")], [fu], GA * 16 * HW + 25, k)
+            op("g", lambda g, T, f0=f0, f1=f1: g.affine_select(X(T, "F2", k, f0, f1), X(T, "F", k, f0, f1), [[0, 16 * HW]], OP.is_ge, 0.0, 0, 0), [fu], [gu], None, GC, k)
+        for u in range(SUB):
+            f0, f1, y0, y1 = 16 * HW * u, 16 * HW * (u + 1), HW * u, HW * (u + 1)
+            fu, gu, du, cu = "F%d.%d" % (k, u), "G%d.%d" % (k, u), "D%d.%d" % (k, u), "C%d.%d" % (k, u)
+            V(lambda g, T, y0=y0, y1=y1, f0=f0, f1=f1: g.vector.tensor_tensor(X(T, "D", k, f0, f1), X(T, "F", k, f0, f1).indirect(X(T, "PO", k, y0, y1)), X(T, "F2", k, f0, f1), OP.subtract),
+              [fu, gu, kt("PO")], [du], GA * 16 * HW + 35, k)
+            S(lambda g, T, f0=f0, f1=f1: g.scalar.activation(X(T, "D", k, f0, f1), X(T, "D", k, f0, f1), AF.Abs), [du], [du], 16 * HW, k)
+
+            def cmp(g, T, u=u, f0=f0, f1=f1):
+                for q in range(8):
+                    c0 = 2 * CN * q + 2 * HW * u
+                    last = g.vector.tensor_tensor(X(T, "C", k, c0, c0 + 2 * HW), X(T, "D", k, f0 + q, f1, 8), T.P_lim[:, 2 * (lo + HW * u):2 * (lo + HW * (u + 1))], OP.is_gt)
+                return last
+            V(cmp, [du, "PL%d.0" % k, "PL%d.1" % k], [cu], 16 * HW, k, "lim")
+        dts, cts = ["D%d.%d" % (k, u) for u in range(SUB)], ["C%d.%d" % (k, u) for u in range(SUB)]
+
+        def ssum(g, T):
+            A = T["P_" + ab][:, 0:CN]
+            g.tensor.matmul(A, T.I5[:], X(T, "C16", k), True, False)
+            for a in range(16):
+                last = g.tensor.matmul(A, T.WB[:, 15 - a:143 - a], X(T, "D", k, a, None, 16), False, False)
+            return last
+        TE(ssum, dts + ["WBB", "I5", kt("C16")], [kt("PA")], 17 * CN, k, ab)
+
+        def csum(g, T):
+            A = T["P_" + cb][:, cc:cc + CN]
+            for a in range(16):
+                c0 = 2 * CN * (a % 8)
+                last = g.tensor.matmul(A, T.WB[:, 15 - a:143 - a], X(T, "C", k, c0 + a // 8, c0 + 2 * CN, 2), a == 0, a == 15)
+            return last
+        TE(csum, cts + ["WBB"], [kt("PC")], 16 * CN, k, cb)
+        S(lambda g, T, t=t: g.scalar.activation(X(T, "NS", k, CN * t, CN * (t + 1)), T["P_" + cb][:, cc:cc + CN], AF.Sign, bias=-7.5),
+          [kt("PC")], ["NS%d.%d" % (k, t)], CN, k, cb)
+
+        def absum(g, T, t=t):
+            s_ = X(T, "NS", k, CN * t, CN * (t + 1))
+            g.tensor.matmul(T["P_" + ab][:, 0:CN], T.BIGI[:], s_, False, True)
+            g.tensor.matmul(T["P_" + ab][:, CN:2 * CN], T.I5[:], X(T, "C16", k), True, False)
+            return g.tensor.matmul(T["P_" + ab][:, CN:2 * CN], T.NBO[:], s_, False, True)
+        TE(absum, ["NS%d.%d" % (k, t), "BIGI", "I5", "NBO", kt("C16"), kt("PA")], [kt("PA"), kt("PB")], 3 * CN, k, ab)
+        V(lambda g, T: g.vector.tensor_tensor(X(T, "O1", k), T["P_" + ab][:, 0:CN], X(T, "CB", k), OP.max), [kt("PA"), kt("CB")], [kt("O1")], CN, k, ab)
+        V(lambda g, T: g.vector.tensor_tensor(X(T, "O2", k), T["P_" + ab][:, CN:2 * CN], X(T, "O1", k), OP.max), [kt("PB"), kt("O1")], [kt("O2")], CN, k, ab)
+        if last_step:
+            V(lambda g, T: g.vector.tensor_scalar(X(T, "O1", k), X(T, "O2", k), 1, None, OP.add), [kt("O2")], [kt("O1")], CN, k)
+            V(lambda g, T: g.vector.tensor_scalar(X(T, "CB", k), X(T, "O1", k), 2047, None, OP.bitwise_and), [kt("O1")], [kt("CB")], CN, k)
+        else:
+            V(lambda g, T: g.vector.tensor_scalar(X(T, "CB", k), X(T, "O2", k), BIG | 2047, None, OP.bitwise_and), [kt("O2")], [kt("CB")], CN, k)
+        if t < NST - 1:
+            V(lambda g, T: g.vector.tensor_scalar(X(T, "OFF", k), X(T, "CB", k), 1 - BIG, None, OP.add), [kt("CB")], [kt("OFF")], CN, k)
+            V(lambda g, T: g.vector.tensor_scalar(X(T, "C16", k), X(T, "CB", k), 1 - BIG, None, OP.add), [kt("CB")], [kt("C16")], CN, k)
+
+    PN, PM, PX = V4, 7 * NB, 8 * NB
+
+    def nsum(g, T):
+        for a in range(16):
+            last = g.tensor.matmul(tiny(T, PN, PN + 3 * NB), T.WB[:, 15 - a:143 - a], X(T, "NS", k, a, None, 16), a == 0, a == 15)
+        return last
+    TE(nsum, ["NS%d.%d" % (k, t) for t in range(NST)] + ["WBB"], [kt("PN")], 1024, k, "tiny")
+    S(lambda g, T: g.scalar.activation(X(T, "FM", k), tiny(T, PN, PN + 3 * NB), AF.Relu, bias=-15.0, scale=-1.0), [kt("PN")], [kt("FM")], 3 * NB, k, "tiny")
+    S(lambda g, T: g.scalar.activation(X(T, "CNT", k), tiny(T, PN + 2 * NB, PN + 3 * NB), AF.Identity, bias=8.0, scale=-0.5), [kt("PN")], [kt("CNT")], NB, k, "tiny")
+
+    def msum(g, T):
+        for t in range(NST):
+            last = g.tensor.matmul(tiny(T, PM, PM + NB), T.RH[:], X(T, "FM", k, t * NB, (t + 1) * NB), t == 0, t == NST - 1)
+        return last
+    TE(msum, [kt("FM"), "RH"], [kt("PM")], 192, k, "tiny")
+    V(lambda g, T: g.vector.tensor_copy(X(T, "MI", k), tiny(T, PM, PM + NB)), [kt("PM")], [kt("MI")], NB, k, "tiny")
+    V(lambda g, T: g.vector.tensor_tensor(X(T, "OD", k), tiny(T, PM, PM + NB), X(T, "MI", k), OP.not_equal), [kt("PM"), kt("MI")], [kt("OD")], NB, k, "tiny")
+
+    def bsum(g, T):
+        B = tiny(T, PX + V4, PX + 2 * V4)
+        g.tensor.matmul(B, T.IM32[:], X(T, "EN", k), True, False)
+        for o in range(4):
+            g.tensor.matmul(tiny(T, PX + V4 + o * NB, PX + V4 + (o + 1) * NB), T.ID[:], X(T, "CNT", k), False, False)
+        g.tensor.matmul(B, T.IM32[:], X(T, "EN", k), False, True)
+        M = tiny(T, PX + 2 * V4, PX + 2 * V4 + NB)
+        for t in range(NST):
+            last = g.tensor.matmul(M, T.ID[:], X(T, "FM", k, t * NB, (t + 1) * NB), t == 0, t == NST - 1 and s == 0)
+        if s > 0:
+            last = g.tensor.matmul(M, T.ID[:], X(T, "HL", k, h0 + 2 * V4, h0 + 2 * V4 + NB), False, True)
+        return last
+    TE(bsum, [kt("EN"), kt("CNT"), kt("FM"), "IM32", "ID"] + ([st] if s else []), [kt("PX")], 640, k, "tiny")
+
+    def asum(g, T):
+        A = tiny(T, PX, PX + V4)
+        if s == 0:
+            g.tensor.matmul(A, T.ID[:], X(T, "VB", k), True, False)
+        else:
+            g.tensor.matmul(A, T.ID[:], X(T, "HL", k, h0, h0 + V4), True, False)
+            g.tensor.matmul(A, T.ID[:], X(T, "HL", k, h0 + V4, h0 + 2 * V4), False, False)
+        g.tensor.matmul(A, T.ID[:], X(T, "EN", k), False, False)
+        for o in range(4):
+            g.tensor.matmul(tiny(T, PX + o * NB, PX + (o + 1) * NB), T.ID[:], X(T, "OD", k), False, False)
+        return g.tensor.matmul(A, T.IM64[:], X(T, "E", k), False, True)
+    TE(asum, [kt("E"), kt("EN"), kt("OD"), "IM64", "ID", st if s else kt("VB")], [kt("PY")], 512, k, "tiny")
+    hp, hl = "HP%d.%d" % (k, s), "HL%d.%d" % (k, s)
+    g0 = HPW * s
+    S(lambda g, T: g.scalar.activation(X(T, "HP", k, g0, g0 + 9 * NB), tiny(T, PX, PX + 9 * NB), AF.Relu), [kt("PX"), kt("PY")], [hp], 9 * NB, k, "tiny")
+    op("g", ("send", k, s), [hp], ["snt%d.%d" % (k, s)], None, 1000, k)
+    op("hop", "hop", ["snt%d.%d" % (k, s)], [hl], None, HOP, k, "hl_%d_%d" % (k, s))
+    if s < NSL - 1:
+        V(lambda g, T: g.vector.tensor_copy(X(T, "CW", k).indirect(X(T, "LU", k)), X(T, "CB", k)), [kt("CB"), kt("LU")], [kt("CW")], 4 * CN + 60, k)
+    if s == NSL - 2:
+        V(lambda g, T: g.vector.tensor_scalar(X(T, "PGB", k), X(T, "CW", k), 1, None, OP.add), [kt("CW")], [kt("PGB")], 256, k)
+        V(lambda g, T: g.vector.tensor_scalar(X(T, "PGI", k), X(T, "PGB", k), 2047, None, OP.bitwise_and), [kt("PGB")], [kt("PGI")], 256, k)
+        V(lambda g, T: g.vector.tensor_copy(X(T, "OUTF", k), X(T, "PGI", k)), [kt("PGI")], [kt("OUTF")], 256, k)
+    if s == NSL - 1:
+        V(lambda g, T: g.vector.tensor_copy(X(T, "OUTF", k).indirect(X(T, "LU", k)), X(T, "CB", k)), [kt("CB"), kt("LU"), kt("OUTF")], [kt("OUTF")], 4 * CN + 60, k)
+        dma("qs", lambda T: T.yg[:, 4 * lo:4 * (lo + CN)], lambda T: X(T, "OUTF", k), [kt("OUTF")], [], 3500, k)
+        V(lambda g, T: g.vector.tensor_tensor(X(T, "YV", k), X(T, "HL", k, g0, g0 + V4), X(T, "HL", k, g0 + V4, g0 + 2 * V4), OP.add), [hl], [kt("YV")], 32, k)
+        S(lambda g, T: g.scalar.activation(X(T, "YM", k), X(T, "HL", k, g0 + 2 * V4, g0 + 2 * V4 + NB), AF.Copy), [hl], [kt("YM")], NB, k)
+        for o in range(4):
+            dma("qs", lambda T, o=o: T.yv[o::4, lo:lo + CN], lambda T, o=o: X(T, "YV", k, NB * o, NB * (o + 1)), [kt("YV")], [], 2500, k)
+        dma("qs", lambda T: T.ym[:, lo:lo + CN], lambda T: X(T, "YM", k), [kt("YM")], [], 2500, k)
+
+
+def jitter(n):
+    x, out = SEED, []
+    for _ in range(n):
+        x = (x * 1103515245 + 12345) % 2 ** 31
+        out.append(AMP * (x / 2 ** 31 - 0.5))
+    return out
+
+
+def plan(ops):
+    n = len(ops)
+    lastw, readers = {}, {}
+    deps = [set() for _ in range(n)]
+    for o in ops:
+        i = o["i"]
+        for r in o["r"]:
+            if r in lastw:
+                deps[i].add(lastw[r])
+        for w in o["w"]:
+            if w in lastw:
+                deps[i].add(lastw[w])
+            deps[i].update(readers.get(w, ()))
+        for r in o["r"]:
+            readers.setdefault(r, set()).add(i)
+        for w in o["w"]:
+            lastw[w] = i
+            readers[w] = set()
+        deps[i].discard(i)
+    succ = [[] for _ in range(n)]
+    for i in range(n):
+        for d in deps[i]:
+            succ[d].append(i)
+    tail = [0.0] * n
+    for i in range(n - 1, -1, -1):
+        tail[i] = ops[i]["cost"] + max([tail[j] + SEM for j in succ[i]] + [0.0])
+    nz = jitter(n)
+    prio = [tail[i] - LAG * ops[i]["k"] + nz[i] for i in range(n)]
+    left = [len(d) for d in deps]
+    ready_at, fin = [0.0] * n, [0.0] * n
+    free, bankfree, bankq = {}, {}, {}
+    avail = [i for i in range(n) if left[i] == 0]
+    order = []
+    while len(order) < n:
+        best = None
+        for i in avail:
+            o = ops[i]
+            at = ready_at[i]
+            if o["q"] != "hop":
+                at = max(at, free.get(o["q"], 0.0))
+            b = o["bank"]
+            if b and bankq.get(b) not in (None, o["q"]):
+                at = max(at, bankfree[b] + SEM)
+            key = (at, o["cost"] > SHORT, -prio[i], i)
+            if best is None or key < best:
+                best = key
+        i, at = best[3], best[0]
+        o = ops[i]
+        avail.remove(i)
+        fin[i] = at + o["cost"]
+        if o["q"] != "hop":
+            free[o["q"]] = (at + 120) if o["q"] in ("qs", "qa") else fin[i]
+        if o["bank"]:
+            bankq[o["bank"]] = o["q"]
+            bankfree[o["bank"]] = fin[i]
+        order.append(i)
+        for j in succ[i]:
+            left[j] -= 1
+            ready_at[j] = max(ready_at[j], fin[i] + SEM)
+            if left[j] == 0:
+                avail.append(j)
+    return order, deps, fin
+
+
+_PLAN = []
+
+
+def get_plan():
+    if not _PLAN:
+        ops = build()
+        order, deps, fin = plan(ops)
+        _PLAN.extend([ops, order, deps, fin])
+    return _PLAN
+
+
+get_plan()
+
+
+def helpers(topo, core, nxt, group):
+    return [c for c in topo.cores_of(core) if c not in group and topo.die(c) == topo.die(core) and topo.may_write(c, nxt)]
+
+
+def bits(topo, a, b):
+    return len(topo.engines(a, b))
+
+
+def rank_program(g, core, T, topo):
+    cores = list(T.cores)
+    n = len(cores)
+    rank = T.rank_of(core)
+    if rank is not None:
+        run_rank(g, core, T, topo, cores, rank)
+        return
+    for r in range(n):
+        own, nxt, prv = cores[r], cores[(r + 1) % n], cores[(r + 3) % n]
+        hs = helpers(topo, own, nxt, cores)
+        if core in hs:
+            hand_on(g, core, T, topo, own, nxt, prv, [k for k in range(NCH) if hs[k % len(hs)] == core], hs[0] == core)
+
+
+def hand_on(g, core, T, topo, own, nxt, prv, ks, lims):
+    loc = 0
+
+    def remote(out, in_, sem, dst):
+        rid, pid = topo.addr(dst, core)
+        g.remote_dma(out, in_, T.sem[sem], T.sem.loc, pid, rid, topo.mask(core, dst))
+        return bits(topo, core, dst)
+
+    if lims:
+        g.wait_ge(T.sem.lh, bits(topo, own, core))
+        loc += remote(T.LS1[:], T.LIMP[:], "ls1", nxt)
+        loc += remote(T.LS3[:], T.LIMP[:], "ls3", prv)
+    for s in range(NSL):
+        for k in ks:
+            g.wait_ge(T.sem["hr_%d_%d" % (k, s)], bits(topo, own, core))
+            a, b = HPW * s, HPW * s + 9 * NB
+            loc += remote(X(T, "HL", k, a, b), X(T, "HP", k, a, b), "hl_%d_%d" % (k, s), nxt)
+    if loc:
+        g.wait_ge(T.sem.loc, loc)
+
+
+def run_rank(g, core, T, topo, cores, rank):
+    n = len(cores)
+    nxt, opp, prv = cores[(rank + 1) % n], cores[(rank + 2) % n], cores[(rank + 3) % n]
+    hs, hprev, hnext = helpers(topo, core, nxt, cores), helpers(topo, prv, core, cores), helpers(topo, nxt, opp, cores)
+    ops, order, deps, _f = get_plan()
+    eng = {"v": g.vector, "s": g.scalar, "t": g.tensor, "g": g, "qs": g.sync, "qa": g.scalar}
+    semname = {"v": "v", "s": "s", "t": "t", "g": "gc"}
+    count = {"v": 0, "s": 0, "t": 0, "g": 0}
+    done, waited, banks, loc = {}, {}, {}, [0]
+
+    def queue(q):
+        return "s" if q == "qa" else q
+
+    def wait(q, d):
+        if d in done:
+            sem, val = done[d]
+            key = (queue(q), sem)
+            if waited.get(key, 0) < val:
+                eng[q].wait_ge(T.sem[sem], val)
+                waited[key] = val
+
+    def remote(out, in_, sem, dst):
+        rid, pid = topo.addr(dst, core)
+        g.remote_dma(out, in_, T.sem[sem], T.sem.loc, pid, rid, topo.mask(core, dst))
+        loc[0] += bits(topo, core, dst)
+
+    for i in order:
+        o = ops[i]
+        q = o["q"]
+        if q == "hop":
+            src = hprev[o["k"] % len(hprev)] if o["fn"] == "hop" else {"ls1": hprev[0], "ls2": opp, "ls3": hnext[0]}[o["sem"]]
+            done[i] = (o["sem"], bits(topo, src, core))
+            continue
+        for d in sorted(deps[i], reverse=True):
+            if not (q == "t" and ops[d]["q"] == "t"):
+                wait(q, d)
+        if o["bank"]:
+            for qq, d in banks.get(o["bank"], {}).items():
+                if qq != q:
+                    wait(q, d)
+            banks.setdefault(o["bank"], {})[q] = i
+        if q in ("qs", "qa"):
+            out, in_ = o["fn"]
+            eng[q].dma_start(out(T), in_(T)).then_inc(T.sem[o["sem"]], 16)
+            done[i] = (o["sem"], 16)
+        elif o["fn"] == "limsend":
+            remote(T.LIMP[:], T.LIMP[:], "lh", hs[0])
+            remote(T.LS2[:], T.LIMP[:], "ls2", opp)
+        elif q == "g" and isinstance(o["fn"], tuple):
+            _x, k, s = o["fn"]
+            a, b = HPW * s, HPW * s + 9 * NB
+            remote(X(T, "HP", k, a, b), X(T, "HP", k, a, b), "hr_%d_%d" % (k, s), hs[k % len(hs)])
+        else:
+            ins = o["fn"](g, T)
+            count[q] += 1
+            ins.then_inc(T.sem[semname[q]], 1)
+            done[i] = (semname[q], count[q])
+    for q in ("v", "s", "t", "g"):
+        g.wait_ge(T.sem[semname[q]], count[q])
+    g.wait_ge(T.sem.loc, loc[0])
+    for o in ops:
+        if o["q"] in ("qs", "qa"):
+            g.wait_ge(T.sem[o["sem"]], 16)

@@ -2,31 +2,45 @@ from concourse.mybir import AluOpType, ActivationFunctionType
 
 OP, AF = AluOpType, ActivationFunctionType
 NCH, CN, NB = 4, 64, 4
-SUB, HW = 2, 32
+SUB = 2
+HW = CN // SUB
+REP = 4
+NQ = 16 // REP
+NDB = 2
 NSL, NST = 4, 3
-BIG = 2 ** 17
+BIG = 2 ** 14
+V4 = 4 * NB
 HPW = 40
-TB = 512 // NCH
 
-PER = {"PGI": (256, "int32"), "PGB": (256, "int32"), "PRE": (256, "bfloat16"), "PW0": (256, "int32"), "PW": (256, "int32"), "CW": (256, "int32"),
-       "VI": (16, "int32"), "VB": (16, "bfloat16"), "KS": (28, "float32"), "KM": (20, "float32"), "KN": (16, "int32"), "LI": (4, "int32"), "LU": (4, "uint16"),
-       "E": (16, "bfloat16"), "EN": (16, "bfloat16"), "CB": (64, "int32"), "OFF": (64, "uint16"), "C16": (64, "float16"), "PO": (64, "uint16"),
-       "O1": (64, "int32"), "O2": (64, "int32"), "NS": (192, "bfloat16"), "FM": (12, "bfloat16"), "CNT": (4, "bfloat16"), "MI": (4, "int32"), "OD": (4, "bfloat16"),
-       "OUTF": (256, "float32"), "YV": (16, "float32"), "YM": (4, "float32"), "F": (1024, "bfloat16"), "F2": (1024, "bfloat16"), "D": (1024, "bfloat16"),
+PER = {"PGI": (256, "int32"), "CW": (256, "float32"), "PRE": (256, "bfloat16"), "PW": (256, "int32"),
+       "VI": (16, "int32"), "VB": (16, "bfloat16"), "SC": (16, "bfloat16"), "E": (16, "bfloat16"), "LU": (4, "uint16"),
+       "C32": (64, "float32"), "C16": (64, "float16"), "OFF": (64, "uint16"), "PO": (64, "uint16"),
+       "RL": (64, "float32"), "O2": (64, "int32"), "CI": (64, "int32"), "NS": (192, "bfloat16"), "FM": (16, "bfloat16"), "RR": (16, "bfloat16"),
+       "YV": (16, "float32"), "YM": (4, "float32"), "F": (1024, "bfloat16"), "F2": (1024, "bfloat16"), "D": (1024, "bfloat16"),
        "C": (1024, "bfloat16"), "HP": (HPW * NSL, "bfloat16"), "HL": (HPW * NSL, "bfloat16")}
-ONE = {"XB": (2064, "bfloat16"), "LIM": (256, "bfloat16"), "LIMP": (256, "bfloat16"), "LS1": (256, "bfloat16"), "LS2": (256, "bfloat16"), "LS3": (256, "bfloat16"),
-       "ONES": (128, "bfloat16"), "BO": (128, "bfloat16"), "BO0": (128, "bfloat16"), "ID": (128, "bfloat16"), "WB": (144, "bfloat16"), "RI": (128, "int32"),
-       "RH": (128, "bfloat16"), "BIGI": (128, "bfloat16"), "NBO": (128, "bfloat16"), "IM64": (128, "bfloat16"), "IM32": (128, "bfloat16"), "IMV": (128, "bfloat16"),
-       "I16": (128, "float16"), "I5": (128, "float16"), "BI": (16, "int32"), "B16": (16, "float16")}
+ONE = {"XB": (2048, "bfloat16"), "LIM": (256, "bfloat16"), "LIMP": (256, "bfloat16"), "LS1": (256, "bfloat16"), "LS2": (256, "bfloat16"), "LS3": (256, "bfloat16"),
+       "ONES": (128, "bfloat16"), "BO": (128, "bfloat16"), "BO0": (128, "bfloat16"), "ID": (128, "bfloat16"), "WB": (144, "bfloat16"), "WK": (144, "bfloat16"),
+       "RI": (128, "int32"), "RH": (128, "bfloat16"), "R1": (128, "bfloat16"), "NBO": (128, "bfloat16"), "CST": (128, "bfloat16"),
+       "WS": (128, "bfloat16"), "IDF": (128, "float32"), "I8K": (128, "bfloat16"),
+       "I2": (128, "bfloat16"), "I3": (128, "bfloat16"), "I4": (128, "bfloat16"), "IM1": (128, "bfloat16"), "IM2": (128, "bfloat16"), "IMH": (128, "bfloat16"),
+       "I64": (128, "bfloat16"), "IM64": (128, "bfloat16"), "I5H": (128, "float16"), "I5F": (128, "float32"),
+       "PW0": (256, "int32"), "BI": (4, "int32"), "BL": (4, "int32"), "B4": (4, "bfloat16"), "LL": (4, "uint16"),
+       "KO1": (16, "bfloat16"), "KO2": (16, "bfloat16"), "RST": (16, "bfloat16"), "XYC": (40, "bfloat16")}
 SCRATCH = {}
 for _n in PER:
     SCRATCH[_n] = ("sbuf", [128, PER[_n][0] * NCH], PER[_n][1])
 for _n in ONE:
     SCRATCH[_n] = ("sbuf", [128, ONE[_n][0]], ONE[_n][1])
-for _n in ["lim", "tiny", "c0", "c1"] + ["ab%d" % _k for _k in range(NCH)]:
-    SCRATCH["P_" + _n] = ("psum", [128, 512], "float32")
+for _k in range(NCH):
+    SCRATCH["P_a%d" % _k] = ("psum", [128, 512], "float32")
+for _k in range(2):
+    SCRATCH["P_l%d" % _k] = ("psum", [128, 512], "float32")
+    SCRATCH["P_d%d" % _k] = ("psum", [128, 512], "float32")
 SEMAPHORES = ["v", "s", "t", "gc", "loc", "lh"] + ["ls%d" % _s for _s in range(1, NSL)]
 SEMAPHORES += ["%s_%d_%d" % (_b, _k, _s) for _b in ("hr", "hl") for _k in range(NCH) for _s in range(NSL)]
+SEMAPHORES += ["cp_%d_%d" % (_k, _u) for _k in range(NCH) for _u in range(SUB)]
+PA, PB, PK1, PK2, PLU, PN, PMA, PMB = 0, 64, 128, 144, 160, 164, 176, 180
+PXY = 192
 
 
 def X(T, name, k, a=0, b=None, step=1):
@@ -34,255 +48,255 @@ def X(T, name, k, a=0, b=None, step=1):
     return T[name][:, w * k + a:w * k + (w if b is None else b):step]
 
 
-GA, TC, HOP, GC = 1.15, 0.5, 5000, 1000
-SHORT, LAG, SEM = 150, 3000.0, 60.0
-AMP, SEED = 1000.0, 984
+COST = {"ga": 1.5, "sc": 4.0, "tc": 0.5, "hop": 4000.0, "cp": 2200.0, "cpe": 600.0, "sem": 60.0, "vo": 15.0, "so": 40.0}
+SHORT, LAG = 200, 2000.0
 
 
-def build():
+def f_on_vector(s, k, t, u):
+    return False
+
+
+def route(s, k, t, u):
+    return "g"
+
+
+def build(C):
     ops = []
 
-    def op(q, fn, r=(), w=(), bank=None, cost=80.0, k=0, sem=None):
-        ops.append({"q": q, "fn": fn, "r": list(r), "w": list(w), "bank": bank, "cost": cost, "k": k, "sem": sem, "i": len(ops)})
+    def op(q, fn, r=(), w=(), bank=None, cost=80.0, k=0, sem=None, eng=0.0):
+        ops.append({"q": q, "fn": fn, "r": list(r), "w": list(w), "bank": bank, "cost": cost, "k": k, "sem": sem, "eng": eng, "i": len(ops)})
 
     def V(fn, r, w, n, k=0, bank=None):
-        op("v", fn, r, w, bank, max(64, n) + 15, k)
+        op("v", fn, r, w, bank, max(64, n) + C["vo"], k)
 
     def S(fn, r, w, n, k=0, bank=None):
-        op("s", fn, r, w, bank, max(64, n) + 40, k)
+        op("s", fn, r, w, bank, max(64, n) + C["so"], k)
 
     def TE(fn, r, w, n, k=0, bank=None):
-        op("t", fn, r, w, bank, n * TC, k)
+        op("t", fn, r, w, bank, n * C["tc"] + 30, k)
 
-    def dma(q, out, in_, r, w, cost=3000.0, k=0):
-        sem = "d%d" % sum(1 for o in ops if o["q"] in ("qs", "qa"))
-        if sem not in SEMAPHORES:
-            SEMAPHORES.append(sem)
-        op(q, (out, in_), r, w, None, cost, k, sem)
+    def dma(q, out, in_, r, w, cost=3000.0, k=0, sem=None, eng=100.0):
+        if sem is None:
+            sem = "d%d" % sum(1 for o in ops if o["q"] in ("qs", "qa") and o["sem"][0] == "d")
+            if sem not in SEMAPHORES:
+                SEMAPHORES.append(sem)
+        op(q, (out, in_), r, w, None, cost, k, sem, eng)
 
     for k in range(NCH):
         lo = CN * k
         for o in range(4):
-            dma("qs" if o < 2 or k else "qa", lambda T, k=k, o=o: X(T, "VI", k, NB * o, NB * (o + 1)), lambda T, o=o, lo=lo: T.vv[o::4, lo:lo + CN], [], ["VI%d.%d" % (k, o)], 2500, k)
-        dma("qa" if k else "qs", lambda T, k=k: X(T, "PGI", k), lambda T, lo=lo: T.pg[:, 4 * lo:4 * (lo + CN)], [], ["PGI%d" % k], 3500, k)
-        dma("qa", lambda T, k=k: X(T, "PRE", k), lambda T, lo=lo: T.pre[:, 4 * lo:4 * (lo + CN)], [], ["PRE%d" % k], 3500, k)
+            dma("qs" if o < 2 else "qa", lambda T, k=k, o=o: X(T, "VI", k, NB * o, NB * (o + 1)), lambda T, o=o, lo=lo: T.vv[o::4, lo:lo + CN], [], ["VI%d.%d" % (k, o)], 2000, k)
+        dma("qa" if k else "qs", lambda T, k=k: X(T, "PGI", k), lambda T, lo=lo: T.pg[:, 4 * lo:4 * (lo + CN)], [], ["PGI%d" % k], 2000, k, None, 500)
         if k == 0:
-            dma("qs", lambda T: T.XB[:, 0:2048], lambda T: T.xt[:], [], ["XBa"], 6000, k)
-            dma("qa", lambda T: T.XB[:, 2048:2064], lambda T: T.xt[:, 0:16], [], ["XBb"], 5000, k)
-            dma("qa", lambda T: T.LIM[:], lambda T: T.lim[:], [], ["LIM"], 4500, k)
-    op("g", lambda g, T: g.iota(T.BI[:], [[1, 4], [4, NB]], 0, 4 * NB), [], ["BI"], None, 250)
-    V(lambda g, T: g.vector.memset(T.ONES[:], 1.0), [], ["ONES"], 128)
-    V(lambda g, T: g.vector.memset(T.WB[:], 0.0), [], ["WB"], 144)
-    op("g", lambda g, T: g.affine_select(T.ID[:], T.ONES[:], [[-1, 128]], OP.is_equal, 0.0, 0, 1), ["ONES"], ["ID"], None, 500)
-    op("g", lambda g, T: g.iota(X(T, "PW0", 0), [[16, 16], [256, NB], [0, 4]], 0, 0), [], ["PW0"], None, 700)
-    op("g", lambda g, T: g.affine_select(T.BO0[:], T.ONES[:], [[-16, 8], [0, 16]], OP.is_ge, 0.0, 0, 1), ["ONES"], ["BO0"], None, 500)
-    op("g", lambda g, T: g.affine_select(T.BO[:], T.BO0[:], [[16, 8], [0, 16]], OP.is_ge, 0.0, 15, -1), ["BO0"], ["BO"], None, 500)
-    op("g", lambda g, T: g.iota(T.RI[:], [[1, 128]], 0, -1), [], ["RI"], None, 400)
+            dma("qa", lambda T: T.XB[:], lambda T: T.xt[:], [], ["XB"], 2000, k, None, 2000)
+        dma("qs", lambda T, k=k: X(T, "PRE", k), lambda T, lo=lo: T.pre[:, 4 * lo:4 * (lo + CN)], [], ["PRE%d" % k], 2000, k, None, 300)
+        if k == 0:
+            dma("qs", lambda T: T.LIM[:], lambda T: T.lim[:], [], ["LIM"], 2000, k, None, 300)
 
-    def scaled(name, src, f):
-        V(lambda g, T: g.vector.tensor_scalar(T[name][:], T[src][:], float(f), None, OP.mult), [src], [name], 128)
+    def fill(name, a, b, val, step=1, p0=0, p1=128, r=()):
+        V(lambda g, T: g.vector.memset(T[name][p0:p1, a:b:step], val), r, ["%s.%d.%d" % (name, a, p0)], 32)
+        return "%s.%d.%d" % (name, a, p0)
 
-    V(lambda g, T: g.vector.tensor_scalar(T.BI[:], T.BI[:], 4 * CN - 1, None, OP.bitwise_and), ["BI"], ["BI"], 16)
-    V(lambda g, T: g.vector.tensor_copy(T.B16[:], T.BI[:]), ["BI"], ["B16"], 16)
-    scaled("IMV", "ID", -4 * CN)
-    scaled("I16", "ID", 1)
-    V(lambda g, T: g.vector.tensor_scalar(X(T, "PW0", 0), X(T, "PW0", 0), 16 * HW - 1, None, OP.bitwise_and), ["PW0"], ["PW0"], 256)
-    V(lambda g, T: g.vector.tensor_copy(T.WB[:, 15:143:16], T.BO[:, 0:128:16]), ["BO", "WB"], ["WBB"], 8)
-    scaled("I5", "ID", 5)
-    scaled("BIGI", "ID", BIG)
-    scaled("NBO", "BO", -(BIG // 16))
-    scaled("IM64", "ID", -64)
-    scaled("IM32", "ID", -32)
+    def scaled(name, src, f, n=64):
+        V(lambda g, T: g.vector.tensor_scalar(T[name][:], T[src][:], float(f), None, OP.mult), [src], [name], n)
+
+    def G(fn, r, w, n):
+        op("g", fn, r, w, None, 200 + 2 * n)
+
+    V(lambda g, T: g.vector.memset(T.ONES[:], 1.0), [], ["ONES"], 64)
+    G(lambda g, T: g.affine_select(T.ID[:], T.ONES[:], [[-1, 128]], OP.is_equal, 0.0, 0, 1), ["ONES"], ["ID"], 128)
+    G(lambda g, T: g.iota(T.KO1[:], [[0, NB], [-1, 4]], 0, 0, allow_small_or_imprecise_dtypes=True), [], ["KO1"], 16)
+    G(lambda g, T: g.iota(T.KO2[:], [[-1, 4], [0, NB]], 0, 0, allow_small_or_imprecise_dtypes=True), [], ["KO2"], 16)
+    G(lambda g, T: g.iota(T.BI[:], [[4, NB]], 0, 4 * NB), [], ["BI"], 4)
+    G(lambda g, T: g.iota(T.PW0[:], [[16, 16], [256, NB], [0, 4]], 0, 0), [], ["PW0"], 256)
+    G(lambda g, T: g.affine_select(T.BO0[:], T.ONES[:], [[-16, 8], [0, 16]], OP.is_ge, 0.0, 0, 1), ["ONES"], ["BO0"], 128)
+    G(lambda g, T: g.affine_select(T.BO[:], T.BO0[:], [[16, 8], [0, 16]], OP.is_ge, 0.0, 15, -1), ["BO0"], ["BO"], 128)
+    G(lambda g, T: g.iota(T.RI[:], [[1, 128]], 0, -1), [], ["RI"], 128)
+    V(lambda g, T: g.vector.memset(T.RST[:], 0.0), [], ["RST"], 16)
+    V(lambda g, T: g.vector.memset(T.RST[:, 0:V4:4], -1024.0), [], ["RST"], 16)
+    V(lambda g, T: g.vector.tensor_scalar(T.BI[:], T.BI[:], 4 * CN - 1, None, OP.bitwise_and), ["BI"], ["BI"], 4)
+    V(lambda g, T: g.vector.tensor_copy(T.B4[:], T.BI[:]), ["BI"], ["B4"], 4)
+    V(lambda g, T: g.vector.tensor_scalar(T.BL[:], T.BI[:], 2, None, OP.logical_shift_right), ["BI"], ["BL"], 4)
+    V(lambda g, T: g.vector.tensor_copy(T.LL[:], T.BL[:]), ["BL"], ["LL"], 4)
+    for name, f in (("I4", 4), ("IM1", -1), ("I2", 2), ("I3", 3), ("I5F", 5), ("I5H", 5), ("IM2", -2), ("IMH", -0.5), ("I64", 64), ("IM64", -64), ("I8K", 8 * BIG), ("IDF", 1)):
+        scaled(name, "ID", f, 128 if name[-1] == "F" else 64)
+    if SUB > 1:
+        V(lambda g, T: g.vector.tensor_scalar(T.PW0[:], T.PW0[:], 16 * HW - 1, None, OP.bitwise_and), ["PW0"], ["PW0"], 256)
+    V(lambda g, T: g.vector.memset(T.WB[:], 0.0), [], ["WB"], 72)
+    V(lambda g, T: g.vector.tensor_copy(T.WB[:, 15:143:16], T.BO[:, 0:128:16]), ["BO"], ["WB"], 8)
+    scaled("WK", "WB", BIG, 72)
+    scaled("NBO", "BO", -(BIG // 2))
     V(lambda g, T: g.vector.tensor_scalar(T.RI[:], T.RI[:], 15, None, OP.bitwise_and), ["RI"], ["RI"], 128)
     V(lambda g, T: g.vector.tensor_scalar(T.RH[:], T.RI[:], 0, 0.5, OP.is_equal, OP.mult), ["RI"], ["RH"], 128)
+    scaled("R1", "RH", 2)
+    scaled("CST", "ONES", 1.0 / 128)
+    V(lambda g, T: g.vector.tensor_tensor(T.WS[:], T.NBO[:], T.I8K[:], OP.add), ["NBO", "I8K"], ["WS"], 256)
+    xyc = [fill("XYC", 0, V4, 193.0), fill("XYC", V4, 2 * V4, 40.0), fill("XYC", 2 * V4, 40, 0.0)]
     for k in range(NCH):
-        V(lambda g, T, k=k: g.vector.tensor_copy(X(T, "VB", k), X(T, "VI", k)), ["VI%d.%d" % (k, o) for o in range(4)], ["VB%d" % k], 32, k)
-        V(lambda g, T, k=k: g.vector.tensor_scalar(X(T, "PGB", k), X(T, "PGI", k), BIG + 2047, None, OP.add), ["PGI%d" % k], ["PGB%d" % k], 256, k)
-        V(lambda g, T, k=k: g.vector.tensor_scalar(X(T, "CW", k), X(T, "PGB", k), BIG | 2047, None, OP.bitwise_and), ["PGB%d" % k], ["CW%d" % k], 256, k)
-        V(lambda g, T, k=k: g.vector.tensor_tensor(X(T, "PW", k), X(T, "PRE", k), X(T, "PW0", 0), OP.add), ["PRE%d" % k, "PW0"], ["PW%d" % k], 512, k)
-        for c in range(NB):
-            V(lambda g, T, k=k, c=c: g.vector.tensor_copy(T.LIMP[:, CN * k + 16 * c:CN * k + 16 * c + 16], T.LIM[:, CN * k + c:CN * k + CN:NB]),
-              ["LIM"], ["LIMP%d.%d" % (k, c)], 16, k)
-    op("g", "limsend", ["LIMP%d.%d" % (k, c) for k in range(NCH) for c in range(NB)], ["limsent"], None, 2000)
+        V(lambda g, T, k=k: g.vector.tensor_copy(X(T, "VB", k), X(T, "VI", k)), ["VI%d.%d" % (k, o) for o in range(4)], ["VB%d" % k], 16, k)
+        V(lambda g, T, k=k: g.vector.tensor_copy(X(T, "CW", k), X(T, "PGI", k)), ["PGI%d" % k], ["CW%d" % k], 256, k)
+        V(lambda g, T, k=k: g.vector.tensor_tensor(X(T, "PW", k), X(T, "PRE", k), T.PW0[:], OP.add), ["PRE%d" % k, "PW0"], ["PW%d" % k], 512, k)
+        S(lambda g, T, k=k: g.scalar.activation(T.LIMP[:, CN * k:CN * (k + 1)], T.LIM[:, CN * k:CN * (k + 1)].indirect(T.LL[:]), AF.Copy),
+          ["LIM", "LL"], ["LIMP%d" % k], C["ga"] * CN + 40, k)
+    op("g", "limsend", ["LIMP%d" % k for k in range(NCH)], ["limsent"], None, 2000)
     for s in range(1, NSL):
         op("hop", "lim%d" % s, ["limsent"], ["LS%d" % s], None, 9000, 0, "ls%d" % s)
     for s in range(NSL):
         for k in range(NCH):
-            one_slice(s, k, op, V, S, TE, dma)
+            one_slice(s, k, C, op, V, S, TE, dma, xyc)
     return ops
 
 
-def one_slice(s, k, op, V, S, TE, dma):
+def one_slice(s, k, C, op, V, S, TE, dma, xyc):
     kt = lambda b: "%s%d" % (b, k)
-    lo, tb = CN * k, TB * k
-    ltags = ["LIMP%d.%d" % (k, c) for c in range(NB)] if s == 0 else ["LS%d" % s]
+    lo = CN * k
+    ltag = kt("LIMP") if s == 0 else "LS%d" % s
     lname = "LIMP" if s == 0 else "LS%d" % s
-    st = "HL%d.%d" % (k, s - 1)
+    st = "HL%d.%d" % (k, s - 1) if s else kt("VB")
     h0 = HPW * (s - 1)
-    V4 = 4 * NB
-    cb, ab = "c%d" % (k % 2), "ab%d" % k
-    cc = CN * k
+    ab, lb = "a%d" % k, "l%d" % (k % 2)
+    GA = C["ga"]
 
-    def tiny(T, a, b):
-        return T.P_tiny[:, tb + a:tb + b]
+    def PS(T, a, b, step=1):
+        return T["P_" + ab][:, a:b:step]
 
-    def kmm(g, T):
-        g.tensor.matmul(tiny(T, 0, V4), T.I16[:], T.B16[:], True, False)
+    def PL(T, a, b, step=1):
+        return T["P_" + lb][:, REP * CN * (k // 2) + a:REP * CN * (k // 2) + b:step]
+
+    def old(T, a, b):
         if s == 0:
-            return g.tensor.matmul(tiny(T, 0, V4), T.IMV[:], X(T, "VB", k), False, True)
-        g.tensor.matmul(tiny(T, 0, V4), T.IMV[:], X(T, "HL", k, h0, h0 + V4), False, False)
-        return g.tensor.matmul(tiny(T, 0, V4), T.IMV[:], X(T, "HL", k, h0 + V4, h0 + 2 * V4), False, True)
-    TE(kmm, ["IMV", "I16", "B16", st if s else kt("VB")], [kt("PSK")], 192, k, "tiny")
-    S(lambda g, T: g.scalar.activation(X(T, "KS", k, 0, V4), tiny(T, 0, V4), AF.Copy), [kt("PSK")], [kt("KSa")], V4, k, "tiny")
-    S(lambda g, T: g.scalar.activation(X(T, "KS", k, V4, 7 * NB), tiny(T, 0, 3 * NB), AF.Copy), [kt("PSK")], [kt("KSb")], V4, k, "tiny")
-    V(lambda g, T: g.vector.tensor_tensor(X(T, "KM", k), X(T, "KS", k, 0, 5 * NB), X(T, "KS", k, 2 * NB, 7 * NB), OP.min), [kt("KSa"), kt("KSb")], [kt("KM")], 40, k)
-    V(lambda g, T: g.vector.tensor_tensor(X(T, "KN", k), X(T, "KM", k, 0, V4), X(T, "KM", k, NB, 5 * NB), OP.min), [kt("KM")], [kt("KN")], 32, k)
-    V(lambda g, T: g.vector.tensor_scalar(X(T, "LI", k), X(T, "KN", k, 0, NB), 4 * CN - 1, None, OP.bitwise_and), [kt("KN")], [kt("LI")], NB, k)
-    V(lambda g, T: g.vector.tensor_copy(X(T, "LU", k), X(T, "LI", k)), [kt("LI")], [kt("LU")], NB, k)
-    V(lambda g, T: g.vector.tensor_copy(X(T, "CB", k), X(T, "CW", k).indirect(X(T, "LU", k))), [kt("CW"), kt("LU")], [kt("CB")], GA * CN + 60, k)
-    V(lambda g, T: g.vector.tensor_scalar(X(T, "OFF", k), X(T, "CB", k), 1 - BIG, None, OP.add), [kt("CB")], [kt("OFF")], CN, k)
-    V(lambda g, T: g.vector.tensor_copy(X(T, "PO", k), X(T, "PW", k).indirect(X(T, "LU", k))), [kt("PW"), kt("LU")], [kt("PO")], GA * CN + 60, k)
-    V(lambda g, T: g.vector.tensor_scalar(X(T, "C16", k), X(T, "CB", k), 1 - BIG, None, OP.add), [kt("CB")], [kt("C16")], CN, k)
-    for e in range(2):
-        V(lambda g, T, e=e: g.vector.tensor_copy(T.P_lim[:, 2 * lo + e:2 * (lo + CN):2], T[lname][:, lo:lo + CN]), ltags, ["PL%d.%d" % (k, e)], CN, k, "lim")
-    V(lambda g, T: g.vector.tensor_tensor(X(T, "E", k), X(T, "KS", k, 0, V4), X(T, "KN", k), OP.is_equal), [kt("KSa"), kt("KN")], [kt("E")], 32, k)
-    S(lambda g, T: g.scalar.activation(X(T, "EN", k), X(T, "E", k), AF.Identity, bias=1.0, scale=-1.0), [kt("E")], [kt("EN")], V4, k)
+            return [X(T, "VB", k, a, b)]
+        return [X(T, "HL", k, h0 + a, h0 + b), X(T, "HL", k, h0 + V4 + a, h0 + V4 + b)]
+
+    def group(g, terms):
+        for n, (out, w, x) in enumerate(terms):
+            last = g.tensor.matmul(out, w, x, n == 0, n == len(terms) - 1)
+        return last
+    npart = 1 if s == 0 else 2
+
+    TE(lambda g, T: group(g, [(PS(T, PK1, PK1 + V4), T.ID[:], T.KO1[:])]
+                          + [(PS(T, PK1 + o, PK1 + V4, 4), T.I4[:], x) for o in range(4) for x in old(T, NB * o, NB * (o + 1))]),
+       ["ID", "I4", "KO1", st], [kt("K1")], 64 * (1 + 4 * npart), k, ab)
+    V(lambda g, T: g.vector.tensor_tensor_scan(X(T, "SC", k), T.RST[:], PS(T, PK1, PK1 + V4), 0.0, OP.add, OP.max), [kt("K1"), "RST"], [kt("SC")], V4, k, ab)
+    TE(lambda g, T: group(g, [(PS(T, PK2, PK2 + V4), T.ID[:], T.KO2[:])] + [(PS(T, PK2, PK2 + V4), T.I4[:], x) for x in old(T, 0, V4)]
+                          + [(PS(T, PK2 + NB * o, PK2 + NB * (o + 1)), T.IM1[:], X(T, "SC", k, 3, None, 4)) for o in range(4)]),
+       ["ID", "I4", "IM1", "KO2", st, kt("SC")], [kt("K2")], 64 * (5 + npart), k, ab)
+    S(lambda g, T: g.scalar.activation(X(T, "E", k), PS(T, PK2, PK2 + V4), AF.Relu, bias=1.0), [kt("K2")], [kt("E")], V4, k, ab)
+    TE(lambda g, T: group(g, [(PS(T, PLU, PLU + NB), T.ID[:], T.B4[:])]
+                          + [(PS(T, PLU, PLU + NB), T[w][:], X(T, "E", k, NB * o, NB * (o + 1))) for o, w in ((1, "ID"), (2, "I2"), (3, "I3"))]),
+       ["ID", "I2", "I3", "B4", kt("E")], [kt("PLU")], 256, k, ab)
+    V(lambda g, T: g.vector.tensor_copy(X(T, "LU", k), PS(T, PLU, PLU + NB)), [kt("PLU")], [kt("LU")], NB, k, ab)
+    S(lambda g, T: g.scalar.activation(X(T, "C32", k), X(T, "CW", k).indirect(X(T, "LU", k)), AF.Copy), [kt("CW"), kt("LU")], [kt("C32")], GA * CN + 40, k)
+    V(lambda g, T: g.vector.tensor_copy(X(T, "OFF", k), X(T, "C32", k)), [kt("C32")], [kt("OFF")], CN, k)
+    V(lambda g, T: g.vector.tensor_copy(X(T, "PO", k), X(T, "PW", k).indirect(X(T, "LU", k))), [kt("PW"), kt("LU")], [kt("PO")], GA * CN + 45, k)
+
+    def lrep(g, T):
+        for e in range(REP):
+            last = g.tensor.matmul(PL(T, e, REP * CN, REP), T.ID[:], T[lname][:, lo:lo + CN], True, True)
+        return last
+    TE(lrep, [ltag, "ID"], [kt("PL")], REP * CN, k, lb)
 
     for t in range(NST):
-        last_step = s == NSL - 1 and t == NST - 1
+        cur, keep, five = ("C32", "C32", "I5F") if t == 0 else ("C16", "CI", "I5H")
+        mm5 = 4 * CN if t == 0 else CN
         for u in range(SUB):
             f0, f1, y0, y1 = 16 * HW * u, 16 * HW * (u + 1), HW * u, HW * (u + 1)
             fu, gu = "F%d.%d" % (k, u), "G%d.%d" % (k, u)
-            S(lambda g, T, y0=y0, y1=y1, f0=f0, f1=f1: g.scalar.activation(X(T, "F", k, f0, f1), T.XB[:].indirect(X(T, "OFF", k, y0, y1)), AF.Copy),
-              ["XBa", "XBb", kt("OFF")], [fu], GA * 16 * HW + 25, k)
-            op("g", lambda g, T, f0=f0, f1=f1: g.affine_select(X(T, "F2", k, f0, f1), X(T, "F", k, f0, f1), [[0, 16 * HW]], OP.is_ge, 0.0, 0, 0), [fu], [gu], None, GC, k)
+            if f_on_vector(s, k, t, u):
+                V(lambda g, T, y0=y0, y1=y1, f0=f0, f1=f1: g.vector.tensor_copy(X(T, "F", k, f0, f1), T.XB[:].indirect(X(T, "OFF", k, y0, y1))),
+                  ["XB", kt("OFF")], [fu], GA * 16 * HW + 45, k)
+            else:
+                S(lambda g, T, y0=y0, y1=y1, f0=f0, f1=f1: g.scalar.activation(X(T, "F", k, f0, f1), T.XB[:].indirect(X(T, "OFF", k, y0, y1)), AF.Copy),
+                  ["XB", kt("OFF")], [fu], GA * 16 * HW + 40, k)
+            way = route(s, k, t, u)
+            if way == "dma":
+                dma("qs", lambda T, f0=f0, f1=f1: X(T, "F2", k, f0, f1), lambda T, f0=f0, f1=f1: X(T, "F", k, f0, f1), [fu], [gu], C["cp"], k, "cp_%d_%d" % (k, u), C["cpe"] * HW / 32)
+            elif way == "g":
+                op("g", lambda g, T, f0=f0, f1=f1: g.affine_select(X(T, "F2", k, f0, f1), X(T, "F", k, f0, f1), [[0, 16 * HW]], OP.is_ge, 0.0, 0, 0), [fu], [gu], None, 200 + 32 * HW, k)
+        dts = ["D%d.%d" % (k, u) for u in range(SUB)]
         for u in range(SUB):
             f0, f1, y0, y1 = 16 * HW * u, 16 * HW * (u + 1), HW * u, HW * (u + 1)
-            fu, gu, du, cu = "F%d.%d" % (k, u), "G%d.%d" % (k, u), "D%d.%d" % (k, u), "C%d.%d" % (k, u)
-            V(lambda g, T, y0=y0, y1=y1, f0=f0, f1=f1: g.vector.tensor_tensor(X(T, "D", k, f0, f1), X(T, "F", k, f0, f1).indirect(X(T, "PO", k, y0, y1)), X(T, "F2", k, f0, f1), OP.subtract),
-              [fu, gu, kt("PO")], [du], GA * 16 * HW + 35, k)
-            S(lambda g, T, f0=f0, f1=f1: g.scalar.activation(X(T, "D", k, f0, f1), X(T, "D", k, f0, f1), AF.Abs), [du], [du], 16 * HW, k)
+            fu, gu, du = "F%d.%d" % (k, u), "G%d.%d" % (k, u), dts[u]
+            way = route(s, k, t, u)
+            if way in ("ts", "tv"):
+                db = "d%d" % (k % NDB)
+                if way == "ts":
+                    S(lambda g, T, y0=y0, y1=y1, f0=f0, f1=f1: g.scalar.activation(X(T, "F2", k, f0, f1), X(T, "F", k, f0, f1).indirect(X(T, "PO", k, y0, y1)), AF.Copy),
+                      [fu, kt("PO")], [gu], GA * 16 * HW + 40, k)
+                else:
+                    V(lambda g, T, y0=y0, y1=y1, f0=f0, f1=f1: g.vector.tensor_copy(X(T, "F2", k, f0, f1), X(T, "F", k, f0, f1).indirect(X(T, "PO", k, y0, y1))),
+                      [fu, kt("PO")], [gu], GA * 16 * HW + 45, k)
+                TE(lambda g, T, f0=f0, f1=f1, db=db: group(g, [(T["P_" + db][:, 0:16 * HW], T.IM1[:], X(T, "F", k, f0, f1)), (T["P_" + db][:, 0:16 * HW], T.ID[:], X(T, "F2", k, f0, f1))]),
+                   [fu, gu, "ID", "IM1"], ["P" + db], 32 * HW, k, db)
+                S(lambda g, T, f0=f0, f1=f1, db=db: g.scalar.activation(X(T, "D", k, f0, f1), T["P_" + db][:, 0:16 * HW], AF.Abs), ["P" + db], [du], 16 * HW, k, db)
+            else:
+                V(lambda g, T, y0=y0, y1=y1, f0=f0, f1=f1: g.vector.tensor_tensor(X(T, "D", k, f0, f1), X(T, "F", k, f0, f1).indirect(X(T, "PO", k, y0, y1)), X(T, "F2", k, f0, f1), OP.subtract),
+                  [fu, gu, kt("PO")], [du], GA * 16 * HW + 45, k)
+                S(lambda g, T, f0=f0, f1=f1: g.scalar.activation(X(T, "D", k, f0, f1), X(T, "D", k, f0, f1), AF.Abs), [du], [du], 16 * HW, k)
+            for q in range(NQ):
+                V(lambda g, T, f0=f0, f1=f1, y0=y0, y1=y1, q=q: g.vector.tensor_tensor(X(T, "C", k, f0 + q, f1, NQ), X(T, "D", k, f0 + q, f1, NQ), PL(T, REP * y0, REP * y1), OP.is_gt),
+                  [du, kt("PL")], ["C%d.%d.%d" % (k, u, q)], REP * HW, k, lb)
 
-            def cmp(g, T, u=u, f0=f0, f1=f1):
-                for q in range(8):
-                    c0 = 2 * CN * q + 2 * HW * u
-                    last = g.vector.tensor_tensor(X(T, "C", k, c0, c0 + 2 * HW), X(T, "D", k, f0 + q, f1, 8), T.P_lim[:, 2 * (lo + HW * u):2 * (lo + HW * (u + 1))], OP.is_gt)
-                return last
-            V(cmp, [du, "PL%d.0" % k, "PL%d.1" % k], [cu], 16 * HW, k, "lim")
-        dts, cts = ["D%d.%d" % (k, u) for u in range(SUB)], ["C%d.%d" % (k, u) for u in range(SUB)]
-
-        def ssum(g, T):
-            A = T["P_" + ab][:, 0:CN]
-            g.tensor.matmul(A, T.I5[:], X(T, "C16", k), True, False)
-            for a in range(16):
-                last = g.tensor.matmul(A, T.WB[:, 15 - a:143 - a], X(T, "D", k, a, None, 16), False, False)
+        def asum(g, T, w, x, als, first, final):
+            for a in als:
+                last = g.tensor.matmul(PS(T, PA, PA + CN), T[w][:, 15 - a:143 - a], X(T, x, k, a, None, 16), first and a == als[0], final and a == als[-1])
             return last
-        TE(ssum, dts + ["WBB", "I5", kt("C16")], [kt("PA")], 17 * CN, k, ab)
-
-        def csum(g, T):
-            A = T["P_" + cb][:, cc:cc + CN]
-            for a in range(16):
-                c0 = 2 * CN * (a % 8)
-                last = g.tensor.matmul(A, T.WB[:, 15 - a:143 - a], X(T, "C", k, c0 + a // 8, c0 + 2 * CN, 2), a == 0, a == 15)
-            return last
-        TE(csum, cts + ["WBB"], [kt("PC")], 16 * CN, k, cb)
-        S(lambda g, T, t=t: g.scalar.activation(X(T, "NS", k, CN * t, CN * (t + 1)), T["P_" + cb][:, cc:cc + CN], AF.Sign, bias=-7.5),
-          [kt("PC")], ["NS%d.%d" % (k, t)], CN, k, cb)
-
-        def absum(g, T, t=t):
-            s_ = X(T, "NS", k, CN * t, CN * (t + 1))
-            g.tensor.matmul(T["P_" + ab][:, 0:CN], T.BIGI[:], s_, False, True)
-            g.tensor.matmul(T["P_" + ab][:, CN:2 * CN], T.I5[:], X(T, "C16", k), True, False)
-            return g.tensor.matmul(T["P_" + ab][:, CN:2 * CN], T.NBO[:], s_, False, True)
-        TE(absum, ["NS%d.%d" % (k, t), "BIGI", "I5", "NBO", kt("C16"), kt("PA")], [kt("PA"), kt("PB")], 3 * CN, k, ab)
-        V(lambda g, T: g.vector.tensor_tensor(X(T, "O1", k), T["P_" + ab][:, 0:CN], X(T, "CB", k), OP.max), [kt("PA"), kt("CB")], [kt("O1")], CN, k, ab)
-        V(lambda g, T: g.vector.tensor_tensor(X(T, "O2", k), T["P_" + ab][:, CN:2 * CN], X(T, "O1", k), OP.max), [kt("PB"), kt("O1")], [kt("O2")], CN, k, ab)
-        if last_step:
-            V(lambda g, T: g.vector.tensor_scalar(X(T, "O1", k), X(T, "O2", k), 1, None, OP.add), [kt("O2")], [kt("O1")], CN, k)
-            V(lambda g, T: g.vector.tensor_scalar(X(T, "CB", k), X(T, "O1", k), 2047, None, OP.bitwise_and), [kt("O1")], [kt("CB")], CN, k)
-        else:
-            V(lambda g, T: g.vector.tensor_scalar(X(T, "CB", k), X(T, "O2", k), BIG | 2047, None, OP.bitwise_and), [kt("O2")], [kt("CB")], CN, k)
+        TE(lambda g, T: asum(g, T, "WB", "D", range(16), True, False), dts + ["WB"], [kt("PA")], 16 * CN, k, ab)
+        for q in range(NQ):
+            TE(lambda g, T, q=q: asum(g, T, "WK", "C", range(q, 16, NQ), False, q == NQ - 1), ["C%d.%d.%d" % (k, u, q) for u in range(SUB)] + ["WK"], [kt("PA")], REP * CN, k, ab)
+        ns = "NS%d.%d" % (k, t)
+        S(lambda g, T, t=t: g.scalar.activation(X(T, "NS", k, CN * t, CN * (t + 1)), PS(T, PA, PA + CN), AF.Sign, bias=-8.0 * BIG), [kt("PA")], [ns], CN, k, ab)
+        S(lambda g, T: g.scalar.activation(X(T, "RL", k), PS(T, PA, PA + CN), AF.Relu, bias=-8.0 * BIG), [kt("PA")], [kt("RL")], CN, k, ab)
+        TE(lambda g, T, t=t, cur=cur, five=five: group(g, [(PS(T, PB, PB + CN), T.CST[:], T.ONES[:, 0:CN]), (PS(T, PB, PB + CN), T[five][:], X(T, cur, k)),
+                                                           (PS(T, PB, PB + CN), T.WS[:], X(T, "NS", k, CN * t, CN * (t + 1))), (PS(T, PB, PB + CN), T.IDF[:], X(T, "RL", k))]),
+           [ns, kt("RL"), "WS", "IDF", "CST", "ONES", five, kt(cur)], [kt("PB")], 6 * CN + mm5, k, ab)
+        V(lambda g, T, keep=keep: g.vector.tensor_tensor(X(T, "O2", k), PS(T, PB, PB + CN), X(T, keep, k), OP.max), [kt("PB"), kt(keep)], [kt("O2")], CN, k, ab)
+        V(lambda g, T: g.vector.tensor_scalar(X(T, "CI", k), X(T, "O2", k), 2047, None, OP.bitwise_and), [kt("O2")], [kt("CI")], CN, k)
         if t < NST - 1:
-            V(lambda g, T: g.vector.tensor_scalar(X(T, "OFF", k), X(T, "CB", k), 1 - BIG, None, OP.add), [kt("CB")], [kt("OFF")], CN, k)
-            V(lambda g, T: g.vector.tensor_scalar(X(T, "C16", k), X(T, "CB", k), 1 - BIG, None, OP.add), [kt("CB")], [kt("C16")], CN, k)
+            V(lambda g, T: g.vector.tensor_copy(X(T, "OFF", k), X(T, "CI", k)), [kt("CI")], [kt("OFF")], CN, k)
+            V(lambda g, T: g.vector.tensor_copy(X(T, "C16", k), X(T, "CI", k)), [kt("CI")], [kt("C16")], CN, k)
 
-    PN, PM, PX = V4, 7 * NB, 8 * NB
-
-    def nsum(g, T):
-        for a in range(16):
-            last = g.tensor.matmul(tiny(T, PN, PN + 3 * NB), T.WB[:, 15 - a:143 - a], X(T, "NS", k, a, None, 16), a == 0, a == 15)
-        return last
-    TE(nsum, ["NS%d.%d" % (k, t) for t in range(NST)] + ["WBB"], [kt("PN")], 1024, k, "tiny")
-    S(lambda g, T: g.scalar.activation(X(T, "FM", k), tiny(T, PN, PN + 3 * NB), AF.Relu, bias=-15.0, scale=-1.0), [kt("PN")], [kt("FM")], 3 * NB, k, "tiny")
-    S(lambda g, T: g.scalar.activation(X(T, "CNT", k), tiny(T, PN + 2 * NB, PN + 3 * NB), AF.Identity, bias=8.0, scale=-0.5), [kt("PN")], [kt("CNT")], NB, k, "tiny")
+    TE(lambda g, T: group(g, [(PS(T, PN, PN + 3 * NB), T.WB[:, 15 - a:143 - a], X(T, "NS", k, a, None, 16)) for a in range(16)]),
+       ["NS%d.%d" % (k, t) for t in range(NST)] + ["WB"], [kt("PN")], 1024, k, ab)
+    S(lambda g, T: g.scalar.activation(X(T, "FM", k, 0, 3 * NB), PS(T, PN, PN + 3 * NB), AF.Relu, bias=-15.0, scale=-1.0), [kt("PN")], [kt("FM")], 3 * NB, k, ab)
 
     def msum(g, T):
-        for t in range(NST):
-            last = g.tensor.matmul(tiny(T, PM, PM + NB), T.RH[:], X(T, "FM", k, t * NB, (t + 1) * NB), t == 0, t == NST - 1)
+        for at, w in ((PMA, "RH"), (PMB, "R1")):
+            last = group(g, [(PS(T, at, at + NB), T[w][:], X(T, "FM", k, t * NB, (t + 1) * NB)) for t in range(NST)])
         return last
-    TE(msum, [kt("FM"), "RH"], [kt("PM")], 192, k, "tiny")
-    V(lambda g, T: g.vector.tensor_copy(X(T, "MI", k), tiny(T, PM, PM + NB)), [kt("PM")], [kt("MI")], NB, k, "tiny")
-    V(lambda g, T: g.vector.tensor_tensor(X(T, "OD", k), tiny(T, PM, PM + NB), X(T, "MI", k), OP.not_equal), [kt("PM"), kt("MI")], [kt("OD")], NB, k, "tiny")
+    TE(msum, [kt("FM"), "RH", "R1"], [kt("PM")], 384, k, ab)
+    S(lambda g, T: g.scalar.activation(X(T, "RR", k, 0, 3 * NB), PS(T, PN + 2 * NB, PN + 5 * NB), AF.Identity, bias=191.75), [kt("PN"), kt("PM")], [kt("RR")], 3 * NB, k, ab)
 
-    def bsum(g, T):
-        B = tiny(T, PX + V4, PX + 2 * V4)
-        g.tensor.matmul(B, T.IM32[:], X(T, "EN", k), True, False)
+    def newv(g, T):
+        terms = [(PS(T, PXY, PXY + 9 * NB), T.ID[:], T.XYC[:, 0:9 * NB])]
+        terms += [(PS(T, PXY, PXY + V4), T.IM64[:], X(T, "E", k)), (PS(T, PXY + V4, PXY + 2 * V4), T.I64[:], X(T, "E", k))]
+        terms += [(PS(T, PXY, PXY + V4), T.ID[:], x) for x in old(T, 0, V4)]
+        terms += [(PS(T, PXY + 2 * V4, PXY + 9 * NB), T.ID[:], X(T, "FM", k, t * NB, (t + 1) * NB)) for t in range(NST)]
+        if s:
+            terms += [(PS(T, PXY + 2 * V4, PXY + 9 * NB), T.ID[:], X(T, "HL", k, h0 + 2 * V4, h0 + 9 * NB))]
         for o in range(4):
-            g.tensor.matmul(tiny(T, PX + V4 + o * NB, PX + V4 + (o + 1) * NB), T.ID[:], X(T, "CNT", k), False, False)
-        g.tensor.matmul(B, T.IM32[:], X(T, "EN", k), False, True)
-        M = tiny(T, PX + 2 * V4, PX + 2 * V4 + NB)
-        for t in range(NST):
-            last = g.tensor.matmul(M, T.ID[:], X(T, "FM", k, t * NB, (t + 1) * NB), t == 0, t == NST - 1 and s == 0)
-        if s > 0:
-            last = g.tensor.matmul(M, T.ID[:], X(T, "HL", k, h0 + 2 * V4, h0 + 2 * V4 + NB), False, True)
-        return last
-    TE(bsum, [kt("EN"), kt("CNT"), kt("FM"), "IM32", "ID"] + ([st] if s else []), [kt("PX")], 640, k, "tiny")
-
-    def asum(g, T):
-        A = tiny(T, PX, PX + V4)
-        if s == 0:
-            g.tensor.matmul(A, T.ID[:], X(T, "VB", k), True, False)
-        else:
-            g.tensor.matmul(A, T.ID[:], X(T, "HL", k, h0, h0 + V4), True, False)
-            g.tensor.matmul(A, T.ID[:], X(T, "HL", k, h0 + V4, h0 + 2 * V4), False, False)
-        g.tensor.matmul(A, T.ID[:], X(T, "EN", k), False, False)
-        for o in range(4):
-            g.tensor.matmul(tiny(T, PX + o * NB, PX + (o + 1) * NB), T.ID[:], X(T, "OD", k), False, False)
-        return g.tensor.matmul(A, T.IM64[:], X(T, "E", k), False, True)
-    TE(asum, [kt("E"), kt("EN"), kt("OD"), "IM64", "ID", st if s else kt("VB")], [kt("PY")], 512, k, "tiny")
+            x, y = PS(T, PXY + NB * o, PXY + NB * (o + 1)), PS(T, PXY + V4 + NB * o, PXY + V4 + NB * (o + 1))
+            terms += [(y, T.IMH[:], X(T, "RR", k, 0, NB)), (x, T.IM2[:], X(T, "RR", k, NB, 2 * NB)), (x, T.ID[:], X(T, "RR", k, 2 * NB, 3 * NB))]
+        return group(g, terms)
+    TE(newv, xyc + ["ID", "IM64", "I64", "IMH", "IM2", kt("E"), kt("FM"), kt("RR"), st], [kt("XY")], 64 * (17 + 2 * npart), k, ab)
     hp, hl = "HP%d.%d" % (k, s), "HL%d.%d" % (k, s)
     g0 = HPW * s
-    S(lambda g, T: g.scalar.activation(X(T, "HP", k, g0, g0 + 9 * NB), tiny(T, PX, PX + 9 * NB), AF.Relu), [kt("PX"), kt("PY")], [hp], 9 * NB, k, "tiny")
-    op("g", ("send", k, s), [hp], ["snt%d.%d" % (k, s)], None, 1000, k)
-    op("hop", "hop", ["snt%d.%d" % (k, s)], [hl], None, HOP, k, "hl_%d_%d" % (k, s))
-    if s < NSL - 1:
-        V(lambda g, T: g.vector.tensor_copy(X(T, "CW", k).indirect(X(T, "LU", k)), X(T, "CB", k)), [kt("CB"), kt("LU")], [kt("CW")], 4 * CN + 60, k)
-    if s == NSL - 2:
-        V(lambda g, T: g.vector.tensor_scalar(X(T, "PGB", k), X(T, "CW", k), 1, None, OP.add), [kt("CW")], [kt("PGB")], 256, k)
-        V(lambda g, T: g.vector.tensor_scalar(X(T, "PGI", k), X(T, "PGB", k), 2047, None, OP.bitwise_and), [kt("PGB")], [kt("PGI")], 256, k)
-        V(lambda g, T: g.vector.tensor_copy(X(T, "OUTF", k), X(T, "PGI", k)), [kt("PGI")], [kt("OUTF")], 256, k)
+    S(lambda g, T: g.scalar.activation(X(T, "HP", k, g0, g0 + 9 * NB), PS(T, PXY, PXY + 9 * NB), AF.Relu), [kt("XY")], [hp], 9 * NB, k, ab)
+    op("g", ("send", k, s), [hp], ["snt%d.%d" % (k, s)], None, 600, k)
+    op("hop", "hop", ["snt%d.%d" % (k, s)], [hl], None, C["hop"], k, "hl_%d_%d" % (k, s))
+    V(lambda g, T: g.vector.tensor_copy(X(T, "CW", k).indirect(X(T, "LU", k)), X(T, "CI", k)), [kt("CI"), kt("LU")], [kt("CW")], C["sc"] * CN + 45, k)
     if s == NSL - 1:
-        V(lambda g, T: g.vector.tensor_copy(X(T, "OUTF", k).indirect(X(T, "LU", k)), X(T, "CB", k)), [kt("CB"), kt("LU"), kt("OUTF")], [kt("OUTF")], 4 * CN + 60, k)
-        dma("qs", lambda T: T.yg[:, 4 * lo:4 * (lo + CN)], lambda T: X(T, "OUTF", k), [kt("OUTF")], [], 3500, k)
+        dma("qs", lambda T: T.yg[:, 4 * lo:4 * (lo + CN)], lambda T: X(T, "CW", k), [kt("CW")], [], 2500, k, None, 500)
         V(lambda g, T: g.vector.tensor_tensor(X(T, "YV", k), X(T, "HL", k, g0, g0 + V4), X(T, "HL", k, g0 + V4, g0 + 2 * V4), OP.add), [hl], [kt("YV")], 32, k)
         S(lambda g, T: g.scalar.activation(X(T, "YM", k), X(T, "HL", k, g0 + 2 * V4, g0 + 2 * V4 + NB), AF.Copy), [hl], [kt("YM")], NB, k)
         for o in range(4):
-            dma("qs", lambda T, o=o: T.yv[o::4, lo:lo + CN], lambda T, o=o: X(T, "YV", k, NB * o, NB * (o + 1)), [kt("YV")], [], 2500, k)
-        dma("qs", lambda T: T.ym[:, lo:lo + CN], lambda T: X(T, "YM", k), [kt("YM")], [], 2500, k)
+            dma("qa" if k == NCH - 1 and o > 1 else "qs", lambda T, o=o: T.yv[o::4, lo:lo + CN], lambda T, o=o: X(T, "YV", k, NB * o, NB * (o + 1)), [kt("YV")], [], 2000, k)
+        dma("qa" if k == NCH - 1 else "qs", lambda T: T.ym[:, lo:lo + CN], lambda T: X(T, "YM", k), [kt("YM")], [], 2000, k)
 
 
-def jitter(n):
-    x, out = SEED, []
-    for _ in range(n):
-        x = (x * 1103515245 + 12345) % 2 ** 31
-        out.append(AMP * (x / 2 ** 31 - 0.5))
-    return out
-
-
-def plan(ops):
-    n = len(ops)
+def depend(ops):
     lastw, readers = {}, {}
-    deps = [set() for _ in range(n)]
+    deps = [set() for _ in ops]
     for o in ops:
         i = o["i"]
         for r in o["r"]:
@@ -298,15 +312,19 @@ def plan(ops):
             lastw[w] = i
             readers[w] = set()
         deps[i].discard(i)
+    return deps
+
+
+def plan(ops, deps, C):
+    n, sem = len(ops), C["sem"]
     succ = [[] for _ in range(n)]
     for i in range(n):
         for d in deps[i]:
             succ[d].append(i)
     tail = [0.0] * n
     for i in range(n - 1, -1, -1):
-        tail[i] = ops[i]["cost"] + max([tail[j] + SEM for j in succ[i]] + [0.0])
-    nz = jitter(n)
-    prio = [tail[i] - LAG * ops[i]["k"] + nz[i] for i in range(n)]
+        tail[i] = ops[i]["cost"] + ops[i]["eng"] + max([tail[j] + sem for j in succ[i]] + [0.0])
+    prio = [tail[i] - LAG * o["k"] if o["r"] or o["q"] not in ("qs", "qa") else 1e9 - i for i, o in enumerate(ops)]
     left = [len(d) for d in deps]
     ready_at, fin = [0.0] * n, [0.0] * n
     free, bankfree, bankq = {}, {}, {}
@@ -318,29 +336,34 @@ def plan(ops):
             o = ops[i]
             at = ready_at[i]
             if o["q"] != "hop":
-                at = max(at, free.get(o["q"], 0.0))
+                at = max(at, free.get("s" if o["q"] == "qa" else o["q"], 0.0))
             b = o["bank"]
             if b and bankq.get(b) not in (None, o["q"]):
-                at = max(at, bankfree[b] + SEM)
+                at = max(at, bankfree[b] + sem)
             key = (at, o["cost"] > SHORT, -prio[i], i)
             if best is None or key < best:
                 best = key
         i, at = best[3], best[0]
         o = ops[i]
         avail.remove(i)
-        fin[i] = at + o["cost"]
-        if o["q"] != "hop":
-            free[o["q"]] = (at + 120) if o["q"] in ("qs", "qa") else fin[i]
+        if o["q"] in ("qs", "qa"):
+            free["s" if o["q"] == "qa" else "qs"] = at + 100
+            free["dma"] = max(free.get("dma", 0.0), at) + o["eng"]
+            fin[i] = free["dma"] + o["cost"]
+        else:
+            fin[i] = at + o["cost"]
+            if o["q"] != "hop":
+                free[o["q"]] = fin[i]
         if o["bank"]:
             bankq[o["bank"]] = o["q"]
             bankfree[o["bank"]] = fin[i]
         order.append(i)
         for j in succ[i]:
             left[j] -= 1
-            ready_at[j] = max(ready_at[j], fin[i] + SEM)
+            ready_at[j] = max(ready_at[j], fin[i] + sem)
             if left[j] == 0:
                 avail.append(j)
-    return order, deps, fin
+    return order, fin
 
 
 _PLAN = []
@@ -348,8 +371,9 @@ _PLAN = []
 
 def get_plan():
     if not _PLAN:
-        ops = build()
-        order, deps, fin = plan(ops)
+        ops = build(COST)
+        deps = depend(ops)
+        order, fin = plan(ops, deps, COST)
         _PLAN.extend([ops, order, deps, fin])
     return _PLAN
 
@@ -376,10 +400,11 @@ def rank_program(g, core, T, topo):
         own, nxt, prv = cores[r], cores[(r + 1) % n], cores[(r + 3) % n]
         hs = helpers(topo, own, nxt, cores)
         if core in hs:
-            hand_on(g, core, T, topo, own, nxt, prv, [k for k in range(NCH) if hs[k % len(hs)] == core], hs[0] == core)
+            lims = [(name, dst) for name, dst, h in (("1", nxt, hs[0]), ("3", prv, hs[-1])) if h == core]
+            hand_on(g, core, T, topo, own, nxt, [k for k in range(NCH) if hs[k % len(hs)] == core], lims)
 
 
-def hand_on(g, core, T, topo, own, nxt, prv, ks, lims):
+def hand_on(g, core, T, topo, own, nxt, ks, lims):
     loc = 0
 
     def remote(out, in_, sem, dst):
@@ -389,8 +414,8 @@ def hand_on(g, core, T, topo, own, nxt, prv, ks, lims):
 
     if lims:
         g.wait_ge(T.sem.lh, bits(topo, own, core))
-        loc += remote(T.LS1[:], T.LIMP[:], "ls1", nxt)
-        loc += remote(T.LS3[:], T.LIMP[:], "ls3", prv)
+    for name, dst in lims:
+        loc += remote(T["LS" + name][:], T.LIMP[:], "ls" + name, dst)
     for s in range(NSL):
         for k in ks:
             g.wait_ge(T.sem["hr_%d_%d" % (k, s)], bits(topo, own, core))
@@ -408,7 +433,7 @@ def run_rank(g, core, T, topo, cores, rank):
     eng = {"v": g.vector, "s": g.scalar, "t": g.tensor, "g": g, "qs": g.sync, "qa": g.scalar}
     semname = {"v": "v", "s": "s", "t": "t", "g": "gc"}
     count = {"v": 0, "s": 0, "t": 0, "g": 0}
-    done, waited, banks, loc = {}, {}, {}, [0]
+    done, waited, banks, loc, dmas = {}, {}, {}, [0], {}
 
     def queue(q):
         return "s" if q == "qa" else q
@@ -430,7 +455,7 @@ def run_rank(g, core, T, topo, cores, rank):
         o = ops[i]
         q = o["q"]
         if q == "hop":
-            src = hprev[o["k"] % len(hprev)] if o["fn"] == "hop" else {"ls1": hprev[0], "ls2": opp, "ls3": hnext[0]}[o["sem"]]
+            src = hprev[o["k"] % len(hprev)] if o["fn"] == "hop" else {"ls1": hprev[0], "ls2": opp, "ls3": hnext[-1]}[o["sem"]]
             done[i] = (o["sem"], bits(topo, src, core))
             continue
         for d in sorted(deps[i], reverse=True):
@@ -444,9 +469,11 @@ def run_rank(g, core, T, topo, cores, rank):
         if q in ("qs", "qa"):
             out, in_ = o["fn"]
             eng[q].dma_start(out(T), in_(T)).then_inc(T.sem[o["sem"]], 16)
-            done[i] = (o["sem"], 16)
+            dmas[o["sem"]] = dmas.get(o["sem"], 0) + 16
+            done[i] = (o["sem"], dmas[o["sem"]])
         elif o["fn"] == "limsend":
-            remote(T.LIMP[:], T.LIMP[:], "lh", hs[0])
+            for h in sorted({hs[0], hs[-1]}):
+                remote(T.LIMP[:], T.LIMP[:], "lh", h)
             remote(T.LS2[:], T.LIMP[:], "ls2", opp)
         elif q == "g" and isinstance(o["fn"], tuple):
             _x, k, s = o["fn"]
@@ -460,6 +487,5 @@ def run_rank(g, core, T, topo, cores, rank):
     for q in ("v", "s", "t", "g"):
         g.wait_ge(T.sem[semname[q]], count[q])
     g.wait_ge(T.sem.loc, loc[0])
-    for o in ops:
-        if o["q"] in ("qs", "qa"):
-            g.wait_ge(T.sem[o["sem"]], 16)
+    for sem in dmas:
+        g.wait_ge(T.sem[sem], dmas[sem])

@@ -4,28 +4,29 @@ OP, AF = AluOpType, ActivationFunctionType
 NCH, CN, NB = 4, 64, 4
 SUB = 2
 HW = CN // SUB
-REP = 4
+REP = 8
 NQ = 16 // REP
-NDB = 2
 NSL, NST = 4, 3
 BIG = 2 ** 14
 V4 = 4 * NB
 HPW = 40
+CWW = 4 * CN + 8
+TW, TBW = 2048, 3072
 
-PER = {"PGI": (256, "int32"), "CW": (256, "float32"), "PRE": (256, "bfloat16"), "PW": (256, "int32"),
-       "VI": (16, "int32"), "VB": (16, "bfloat16"), "SC": (16, "bfloat16"), "E": (16, "bfloat16"), "LU": (4, "uint16"),
-       "C32": (64, "float32"), "C16": (64, "float16"), "OFF": (64, "uint16"), "PO": (64, "uint16"),
-       "RL": (64, "float32"), "O2": (64, "int32"), "CI": (64, "int32"), "NS": (192, "bfloat16"), "FM": (16, "bfloat16"), "RR": (16, "bfloat16"),
+PER = {"PGI": (256, "int32"), "CW": (CWW * (NSL + 1), "float32"), "SC": (16, "bfloat16"), "E": (16, "bfloat16"), "LU": (4, "uint16"), "LN": (4, "uint16"),
+       "CF": (128, "float32"), "C16": (64, "float16"), "OF": (128, "uint16"),
+       "RL": (64, "float32"), "O2": (64, "int32"), "CI": (64, "int32"), "CO": (64 * NSL, "int32"), "CL": (64 * NSL, "int32"),
+       "NS": (192, "bfloat16"), "FM": (16, "bfloat16"), "RR": (16, "bfloat16"),
        "YV": (16, "float32"), "YM": (4, "float32"), "F": (1024, "bfloat16"), "F2": (1024, "bfloat16"), "D": (1024, "bfloat16"),
-       "C": (1024, "bfloat16"), "HP": (HPW * NSL, "bfloat16"), "HL": (HPW * NSL, "bfloat16")}
-ONE = {"XB": (2048, "bfloat16"), "LIM": (256, "bfloat16"), "LIMP": (256, "bfloat16"), "LS1": (256, "bfloat16"), "LS2": (256, "bfloat16"), "LS3": (256, "bfloat16"),
+       "C": (1024, "bfloat16"), "HP": (HPW * NSL, "bfloat16")}
+ONE = {"TB": (TBW * NSL, "bfloat16"), "LIM": (256, "bfloat16"), "LIMP": (256, "bfloat16"),
        "ONES": (128, "bfloat16"), "BO": (128, "bfloat16"), "BO0": (128, "bfloat16"), "ID": (128, "bfloat16"), "WB": (144, "bfloat16"), "WK": (144, "bfloat16"),
        "RI": (128, "int32"), "RH": (128, "bfloat16"), "R1": (128, "bfloat16"), "NBO": (128, "bfloat16"), "CST": (128, "bfloat16"),
-       "WS": (128, "bfloat16"), "IDF": (128, "float32"), "I8K": (128, "bfloat16"),
+       "WS": (128, "bfloat16"), "I8K": (128, "bfloat16"), "IDF": (128, "float32"),
        "I2": (128, "bfloat16"), "I3": (128, "bfloat16"), "I4": (128, "bfloat16"), "IM1": (128, "bfloat16"), "IM2": (128, "bfloat16"), "IMH": (128, "bfloat16"),
        "I64": (128, "bfloat16"), "IM64": (128, "bfloat16"), "I5H": (128, "float16"), "I5F": (128, "float32"),
-       "PW0": (256, "int32"), "BI": (4, "int32"), "BL": (4, "int32"), "B4": (4, "bfloat16"), "LL": (4, "uint16"),
-       "KO1": (16, "bfloat16"), "KO2": (16, "bfloat16"), "RST": (16, "bfloat16"), "XYC": (40, "bfloat16")}
+       "POS": (64, "bfloat16"), "BI": (16, "int32"), "BL": (4, "int32"), "B4": (16, "bfloat16"), "LL": (4, "uint16"),
+       "KO": (64, "bfloat16"), "RST": (64, "bfloat16"), "XYC": (40, "bfloat16"), "VI": (64, "int32"), "VB": (64, "bfloat16")}
 SCRATCH = {}
 for _n in PER:
     SCRATCH[_n] = ("sbuf", [128, PER[_n][0] * NCH], PER[_n][1])
@@ -33,14 +34,17 @@ for _n in ONE:
     SCRATCH[_n] = ("sbuf", [128, ONE[_n][0]], ONE[_n][1])
 for _k in range(NCH):
     SCRATCH["P_a%d" % _k] = ("psum", [128, 512], "float32")
-for _k in range(2):
     SCRATCH["P_l%d" % _k] = ("psum", [128, 512], "float32")
-    SCRATCH["P_d%d" % _k] = ("psum", [128, 512], "float32")
-SEMAPHORES = ["v", "s", "t", "gc", "loc", "lh"] + ["ls%d" % _s for _s in range(1, NSL)]
-SEMAPHORES += ["%s_%d_%d" % (_b, _k, _s) for _b in ("hr", "hl") for _k in range(NCH) for _s in range(NSL)]
-SEMAPHORES += ["cp_%d_%d" % (_k, _u) for _k in range(NCH) for _u in range(SUB)]
-PA, PB, PK1, PK2, PLU, PN, PMA, PMB = 0, 64, 128, 144, 160, 164, 176, 180
-PXY = 192
+SEMAPHORES = ["v", "s", "t", "gc", "loc"] + ["%s%d" % (_b, _s) for _b in ("tr", "tl") for _s in range(1, NSL)]
+SEMAPHORES += ["%s_%d_%d" % (_b, _k, _s) for _b in ("cr", "cl") for _k in range(NCH) for _s in range(NSL)]
+SEMAPHORES += ["%s_1_%d" % (_b, _s) for _b in ("wr", "wl") for _s in range(NSL)]
+PA, PB, PK1, PLU, PN, PMA, PMB, PK0 = 0, 64, 128, 144, 148, 160, 164, 192
+
+
+def group(g, terms, first=True, final=True):
+    for n, (out, w, x) in enumerate(terms):
+        last = g.tensor.matmul(out, w, x, first and n == 0, final and n == len(terms) - 1)
+    return last
 
 
 def X(T, name, k, a=0, b=None, step=1):
@@ -48,16 +52,20 @@ def X(T, name, k, a=0, b=None, step=1):
     return T[name][:, w * k + a:w * k + (w if b is None else b):step]
 
 
-COST = {"ga": 1.5, "sc": 4.0, "tc": 0.5, "hop": 4000.0, "cp": 2200.0, "cpe": 600.0, "sem": 60.0, "vo": 15.0, "so": 40.0}
-SHORT, LAG = 200, 2000.0
+def cursors(T, s, k, a, b):
+    return T.CW[:, CWW * (NCH * s + k) + a:CWW * (NCH * s + k) + b]
 
 
-def f_on_vector(s, k, t, u):
-    return False
+def message(T, kind, k, s, landed):
+    if kind == "w":
+        return cursors(T, s + landed, 0, 0, CWW * NCH)
+    return X(T, "CL" if landed else "CO", k, CN * s, CN * (s + 1))
 
 
-def route(s, k, t, u):
-    return "g"
+COST = {"ga": 1.4, "sc": 4.0, "tc": 0.45, "hop": 3500.0, "sem": 140.0, "vo": 20.0, "so": 50.0, "pm": 1.0, "send": 500.0}
+AMP, SEED = 0.0, 1
+SHORT, LAG = 600, 1500.0
+ON = {"E": "v", "FM": "v", "RR": "v", "HP": "v", "C32": "s", "LF": "s"}
 
 
 def build(C):
@@ -70,32 +78,31 @@ def build(C):
         op("v", fn, r, w, bank, max(64, n) + C["vo"], k)
 
     def S(fn, r, w, n, k=0, bank=None):
-        op("s", fn, r, w, bank, max(64, n) + C["so"], k)
+        op("s", fn, r, w, bank, max(64, n) * (C["pm"] if bank else 1) + C["so"], k)
 
     def TE(fn, r, w, n, k=0, bank=None):
-        op("t", fn, r, w, bank, n * C["tc"] + 30, k)
+        op("t", fn, r, w, bank, n * C["tc"] + 15, k)
 
-    def dma(q, out, in_, r, w, cost=3000.0, k=0, sem=None, eng=100.0):
-        if sem is None:
-            sem = "d%d" % sum(1 for o in ops if o["q"] in ("qs", "qa") and o["sem"][0] == "d")
-            if sem not in SEMAPHORES:
-                SEMAPHORES.append(sem)
+    def dma(q, out, in_, r, w, cost=3000.0, k=0, eng=100.0):
+        sem = "d%d" % sum(1 for o in ops if o["q"] in ("qs", "qa"))
+        if sem not in SEMAPHORES:
+            SEMAPHORES.append(sem)
         op(q, (out, in_), r, w, None, cost, k, sem, eng)
 
     for k in range(NCH):
-        lo = CN * k
         for o in range(4):
-            dma("qs" if o < 2 else "qa", lambda T, k=k, o=o: X(T, "VI", k, NB * o, NB * (o + 1)), lambda T, o=o, lo=lo: T.vv[o::4, lo:lo + CN], [], ["VI%d.%d" % (k, o)], 2000, k)
-        dma("qa" if k else "qs", lambda T, k=k: X(T, "PGI", k), lambda T, lo=lo: T.pg[:, 4 * lo:4 * (lo + CN)], [], ["PGI%d" % k], 2000, k, None, 500)
+            dma("qs" if o < 2 else "qa", lambda T, k=k, o=o: T.VI[:, V4 * o + NB * k:V4 * o + NB * (k + 1)], lambda T, o=o, k=k: T.vv[o::4, CN * k:CN * (k + 1)],
+                [], ["VI%d.%d" % (k, o)], 2000, k)
+    for k in range(NCH):
+        dma("qa" if k else "qs", lambda T, k=k: X(T, "PGI", k), lambda T, k=k: T.pg[:, 4 * CN * k:4 * CN * (k + 1)], [], ["PGI%d" % k], 2000, k, 500)
         if k == 0:
-            dma("qa", lambda T: T.XB[:], lambda T: T.xt[:], [], ["XB"], 2000, k, None, 2000)
-        dma("qs", lambda T, k=k: X(T, "PRE", k), lambda T, lo=lo: T.pre[:, 4 * lo:4 * (lo + CN)], [], ["PRE%d" % k], 2000, k, None, 300)
-        if k == 0:
-            dma("qs", lambda T: T.LIM[:], lambda T: T.lim[:], [], ["LIM"], 2000, k, None, 300)
+            dma("qa", lambda T: T.TB[:, 0:TW], lambda T: T.xt[:], [], ["XB0"], 2000, k, 2000)
+            dma("qs", lambda T: T.TB[:, TW:TBW], lambda T: T.pre[:], [], ["PRE0"], 2000, k, 1000)
+            dma("qs", lambda T: T.LIM[:], lambda T: T.lim[:], [], ["LIM"], 2000, k, 300)
 
-    def fill(name, a, b, val, step=1, p0=0, p1=128, r=()):
-        V(lambda g, T: g.vector.memset(T[name][p0:p1, a:b:step], val), r, ["%s.%d.%d" % (name, a, p0)], 32)
-        return "%s.%d.%d" % (name, a, p0)
+    def fill(name, a, b, val):
+        V(lambda g, T: g.vector.memset(T[name][:, a:b], val), [], ["%s.%d" % (name, a)], 32)
+        return "%s.%d" % (name, a)
 
     def scaled(name, src, f, n=64):
         V(lambda g, T: g.vector.tensor_scalar(T[name][:], T[src][:], float(f), None, OP.mult), [src], [name], n)
@@ -105,23 +112,20 @@ def build(C):
 
     V(lambda g, T: g.vector.memset(T.ONES[:], 1.0), [], ["ONES"], 64)
     G(lambda g, T: g.affine_select(T.ID[:], T.ONES[:], [[-1, 128]], OP.is_equal, 0.0, 0, 1), ["ONES"], ["ID"], 128)
-    G(lambda g, T: g.iota(T.KO1[:], [[0, NB], [-1, 4]], 0, 0, allow_small_or_imprecise_dtypes=True), [], ["KO1"], 16)
-    G(lambda g, T: g.iota(T.KO2[:], [[-1, 4], [0, NB]], 0, 0, allow_small_or_imprecise_dtypes=True), [], ["KO2"], 16)
-    G(lambda g, T: g.iota(T.BI[:], [[4, NB]], 0, 4 * NB), [], ["BI"], 4)
-    G(lambda g, T: g.iota(T.PW0[:], [[16, 16], [256, NB], [0, 4]], 0, 0), [], ["PW0"], 256)
+    G(lambda g, T: g.iota(T.KO[:], [[0, NB * NCH], [-1, 4]], 0, 0, allow_small_or_imprecise_dtypes=True), [], ["KO"], 64)
+    G(lambda g, T: g.iota(T.BI[:], [[0, NCH], [4, NB]], 0, 4 * NB), [], ["BI"], 16)
+    G(lambda g, T: g.iota(T.POS[:], [[0, SUB], [16, HW]], 0, 0, allow_small_or_imprecise_dtypes=True), [], ["POS"], 64)
     G(lambda g, T: g.affine_select(T.BO0[:], T.ONES[:], [[-16, 8], [0, 16]], OP.is_ge, 0.0, 0, 1), ["ONES"], ["BO0"], 128)
     G(lambda g, T: g.affine_select(T.BO[:], T.BO0[:], [[16, 8], [0, 16]], OP.is_ge, 0.0, 15, -1), ["BO0"], ["BO"], 128)
     G(lambda g, T: g.iota(T.RI[:], [[1, 128]], 0, -1), [], ["RI"], 128)
     V(lambda g, T: g.vector.memset(T.RST[:], 0.0), [], ["RST"], 16)
-    V(lambda g, T: g.vector.memset(T.RST[:, 0:V4:4], -1024.0), [], ["RST"], 16)
+    V(lambda g, T: g.vector.memset(T.RST[:, 0:V4 * NCH:4], -1024.0), [], ["RST"], 16)
     V(lambda g, T: g.vector.tensor_scalar(T.BI[:], T.BI[:], 4 * CN - 1, None, OP.bitwise_and), ["BI"], ["BI"], 4)
     V(lambda g, T: g.vector.tensor_copy(T.B4[:], T.BI[:]), ["BI"], ["B4"], 4)
-    V(lambda g, T: g.vector.tensor_scalar(T.BL[:], T.BI[:], 2, None, OP.logical_shift_right), ["BI"], ["BL"], 4)
+    V(lambda g, T: g.vector.tensor_scalar(T.BL[:], T.BI[:, 0:NB], 2, None, OP.logical_shift_right), ["BI"], ["BL"], 4)
     V(lambda g, T: g.vector.tensor_copy(T.LL[:], T.BL[:]), ["BL"], ["LL"], 4)
     for name, f in (("I4", 4), ("IM1", -1), ("I2", 2), ("I3", 3), ("I5F", 5), ("I5H", 5), ("IM2", -2), ("IMH", -0.5), ("I64", 64), ("IM64", -64), ("I8K", 8 * BIG), ("IDF", 1)):
         scaled(name, "ID", f, 128 if name[-1] == "F" else 64)
-    if SUB > 1:
-        V(lambda g, T: g.vector.tensor_scalar(T.PW0[:], T.PW0[:], 16 * HW - 1, None, OP.bitwise_and), ["PW0"], ["PW0"], 256)
     V(lambda g, T: g.vector.memset(T.WB[:], 0.0), [], ["WB"], 72)
     V(lambda g, T: g.vector.tensor_copy(T.WB[:, 15:143:16], T.BO[:, 0:128:16]), ["BO"], ["WB"], 8)
     scaled("WK", "WB", BIG, 72)
@@ -133,165 +137,203 @@ def build(C):
     V(lambda g, T: g.vector.tensor_tensor(T.WS[:], T.NBO[:], T.I8K[:], OP.add), ["NBO", "I8K"], ["WS"], 256)
     xyc = [fill("XYC", 0, V4, 193.0), fill("XYC", V4, 2 * V4, 40.0), fill("XYC", 2 * V4, 40, 0.0)]
     for k in range(NCH):
-        V(lambda g, T, k=k: g.vector.tensor_copy(X(T, "VB", k), X(T, "VI", k)), ["VI%d.%d" % (k, o) for o in range(4)], ["VB%d" % k], 16, k)
-        V(lambda g, T, k=k: g.vector.tensor_copy(X(T, "CW", k), X(T, "PGI", k)), ["PGI%d" % k], ["CW%d" % k], 256, k)
-        V(lambda g, T, k=k: g.vector.tensor_tensor(X(T, "PW", k), X(T, "PRE", k), T.PW0[:], OP.add), ["PRE%d" % k, "PW0"], ["PW%d" % k], 512, k)
+        V(lambda g, T, k=k: g.vector.memset(cursors(T, 0, k, 4 * CN, CWW), 0.0), [], ["LF%d.0" % k], 8)
+    allk = lambda b: ["%s%d" % (b, k) for k in range(NCH)]
+    W4 = V4 * NCH
+    keys = lambda T: [(T.P_a0[:, PK0:PK0 + W4], T.ID[:], T.KO[:])] + [(T.P_a0[:, PK0 + o:PK0 + W4:4], T.I4[:], T.VB[:, V4 * o:V4 * (o + 1)]) for o in range(4)]
+    V(lambda g, T: g.vector.tensor_copy(T.VB[:], T.VI[:]), ["VI%d.%d" % (k, o) for k in range(NCH) for o in range(4)], ["VB"], W4)
+    TE(lambda g, T: group(g, keys(T)), ["ID", "I4", "KO", "VB"], ["K0"], 64 * 5, 0, "a0")
+    V(lambda g, T: g.vector.tensor_tensor_scan(T.SC[:], T.RST[:], T.P_a0[:, PK0:PK0 + W4], 0.0, OP.add, OP.max), ["K0", "RST"], allk("SC"), W4, 0, "a0")
+    TE(lambda g, T: group(g, keys(T) + [(T.P_a0[:, PK0 + o:PK0 + W4:4], T.IM1[:], T.SC[:, 3:W4:4]) for o in range(4)]), ["IM1"] + allk("SC"), ["K0"], 64 * 9, 0, "a0")
+    V(lambda g, T: g.vector.tensor_scalar(T.E[:], T.P_a0[:, PK0:PK0 + W4], -0.5, None, OP.is_gt), ["K0"], allk("E"), W4, 0, "a0")
+    TE(lambda g, T: group(g, [(T.P_a0[:, PK0:PK0 + V4], T.ID[:], T.B4[:])] + [(T.P_a0[:, PK0:PK0 + V4], T[w][:], T.E[:, o:W4:4]) for o, w in ((1, "ID"), (2, "I2"), (3, "I3"))]),
+       ["I2", "I3", "B4"] + allk("E"), ["K0"], 256, 0, "a0")
+    V(lambda g, T: g.vector.tensor_copy(T.LU[:], T.P_a0[:, PK0:PK0 + V4]), ["K0"], allk("LU"), V4, 0, "a0")
+    for k in range(NCH):
+        S(lambda g, T, k=k: g.scalar.activation(cursors(T, 0, k, 4 * CN, 4 * CN + NB), T.P_a0[:, PK0 + NB * k:PK0 + NB * (k + 1)], AF.Copy), ["K0"], ["LF%d.0" % k], NB, k, "a0")
+        V(lambda g, T, k=k: g.vector.tensor_copy(cursors(T, 0, k, 0, 4 * CN), X(T, "PGI", k)), ["PGI%d" % k], ["CW%d.0" % k], 256, k)
         S(lambda g, T, k=k: g.scalar.activation(T.LIMP[:, CN * k:CN * (k + 1)], T.LIM[:, CN * k:CN * (k + 1)].indirect(T.LL[:]), AF.Copy),
           ["LIM", "LL"], ["LIMP%d" % k], C["ga"] * CN + 40, k)
-    op("g", "limsend", ["LIMP%d" % k for k in range(NCH)], ["limsent"], None, 2000)
-    for s in range(1, NSL):
-        op("hop", "lim%d" % s, ["limsent"], ["LS%d" % s], None, 9000, 0, "ls%d" % s)
     for s in range(NSL):
+        if s < NSL - 1:
+            op("g", ("t", 0, s + 1), ["XB0", "PRE0"] + ["csent%d.%d" % (NCH - 1, s - 1)] * (s > 0), ["tsent%d" % s], None, C["send"])
+            op("hop", "t", ["tsent%d" % s], ["XB%d" % (s + 1), "PRE%d" % (s + 1)], None, 28000, 0, "tl%d" % (s + 1))
         for k in range(NCH):
-            one_slice(s, k, C, op, V, S, TE, dma, xyc)
+            one_slice(s, k, 0, C, op, V, S, TE, dma, xyc)
+        both = lambda at: ["%s%d.%d" % (b, k, at) for b in ("CW", "LF") for k in range(NCH)]
+        op("g", ("w", 1, s), both(s), ["wsent%d" % s], None, C["send"])
+        op("hop", "w", ["wsent%d" % s], both(s + 1), None, 22000, 1, "wl_1_%d" % s)
+        for k in range(NCH):
+            one_slice(s, k, 1, C, op, V, S, TE, dma, xyc)
     return ops
 
 
-def one_slice(s, k, C, op, V, S, TE, dma, xyc):
+def one_slice(s, k, rest, C, op, V, S, TE, dma, xyc):
     kt = lambda b: "%s%d" % (b, k)
+    ks = lambda b, at=s: "%s%d.%d" % (b, k, at)
     lo = CN * k
-    ltag = kt("LIMP") if s == 0 else "LS%d" % s
-    lname = "LIMP" if s == 0 else "LS%d" % s
-    st = "HL%d.%d" % (k, s - 1) if s else kt("VB")
+    st = ks("HP", s - 1) if s else "VB"
     h0 = HPW * (s - 1)
-    ab, lb = "a%d" % k, "l%d" % (k % 2)
+    ab, lb = "a%d" % k, "l%d" % k
     GA = C["ga"]
+    home = s == NSL - 1
 
     def PS(T, a, b, step=1):
         return T["P_" + ab][:, a:b:step]
 
     def PL(T, a, b, step=1):
-        return T["P_" + lb][:, REP * CN * (k // 2) + a:REP * CN * (k // 2) + b:step]
+        return T["P_" + lb][:, a:b:step]
 
-    def old(T, a, b):
+    def saved(T, at):
+        return cursors(T, at, k, 0, 4 * CN)
+
+    def listed(T, at):
+        return cursors(T, at, k, 4 * CN, 4 * CN + NB)
+
+    def one(P, T, at, o, by_order):
+        return P(T, at + NB * o, at + NB * (o + 1)) if by_order else P(T, at + o, at + V4, 4)
+
+    def laid(P, T, at, w, name, a, by_order):
+        if not by_order:
+            return [(P(T, at, at + V4), T[w][:], X(T, name, k, a, a + V4))]
+        return [(one(P, T, at, o, True), T[w][:], X(T, name, k, a + o, a + V4, 4)) for o in range(4)]
+
+    def old(P, T, at, w, by_order=False):
         if s == 0:
-            return [X(T, "VB", k, a, b)]
-        return [X(T, "HL", k, h0 + a, h0 + b), X(T, "HL", k, h0 + V4 + a, h0 + V4 + b)]
+            return [(one(P, T, at, o, by_order), T[w][:], T.VB[:, V4 * o + NB * k:V4 * o + NB * (k + 1)]) for o in range(4)]
+        return laid(P, T, at, w, "HP", h0, by_order) + laid(P, T, at, w, "HP", h0 + V4, by_order)
 
-    def group(g, terms):
-        for n, (out, w, x) in enumerate(terms):
-            last = g.tensor.matmul(out, w, x, n == 0, n == len(terms) - 1)
-        return last
-    npart = 1 if s == 0 else 2
-
-    TE(lambda g, T: group(g, [(PS(T, PK1, PK1 + V4), T.ID[:], T.KO1[:])]
-                          + [(PS(T, PK1 + o, PK1 + V4, 4), T.I4[:], x) for o in range(4) for x in old(T, NB * o, NB * (o + 1))]),
-       ["ID", "I4", "KO1", st], [kt("K1")], 64 * (1 + 4 * npart), k, ab)
-    V(lambda g, T: g.vector.tensor_tensor_scan(X(T, "SC", k), T.RST[:], PS(T, PK1, PK1 + V4), 0.0, OP.add, OP.max), [kt("K1"), "RST"], [kt("SC")], V4, k, ab)
-    TE(lambda g, T: group(g, [(PS(T, PK2, PK2 + V4), T.ID[:], T.KO2[:])] + [(PS(T, PK2, PK2 + V4), T.I4[:], x) for x in old(T, 0, V4)]
-                          + [(PS(T, PK2 + NB * o, PK2 + NB * (o + 1)), T.IM1[:], X(T, "SC", k, 3, None, 4)) for o in range(4)]),
-       ["ID", "I4", "IM1", "KO2", st, kt("SC")], [kt("K2")], 64 * (5 + npart), k, ab)
-    S(lambda g, T: g.scalar.activation(X(T, "E", k), PS(T, PK2, PK2 + V4), AF.Relu, bias=1.0), [kt("K2")], [kt("E")], V4, k, ab)
-    TE(lambda g, T: group(g, [(PS(T, PLU, PLU + NB), T.ID[:], T.B4[:])]
-                          + [(PS(T, PLU, PLU + NB), T[w][:], X(T, "E", k, NB * o, NB * (o + 1))) for o, w in ((1, "ID"), (2, "I2"), (3, "I3"))]),
-       ["ID", "I2", "I3", "B4", kt("E")], [kt("PLU")], 256, k, ab)
-    V(lambda g, T: g.vector.tensor_copy(X(T, "LU", k), PS(T, PLU, PLU + NB)), [kt("PLU")], [kt("LU")], NB, k, ab)
-    S(lambda g, T: g.scalar.activation(X(T, "C32", k), X(T, "CW", k).indirect(X(T, "LU", k)), AF.Copy), [kt("CW"), kt("LU")], [kt("C32")], GA * CN + 40, k)
-    V(lambda g, T: g.vector.tensor_copy(X(T, "OFF", k), X(T, "C32", k)), [kt("C32")], [kt("OFF")], CN, k)
-    V(lambda g, T: g.vector.tensor_copy(X(T, "PO", k), X(T, "PW", k).indirect(X(T, "LU", k))), [kt("PW"), kt("LU")], [kt("PO")], GA * CN + 45, k)
+    if s and not rest:
+        TE(lambda g, T: group(g, [(PS(T, PK1, PK1 + V4), T.ID[:], T.KO[:, 0:V4])] + old(PS, T, PK1, "I4")), ["ID", "I4", "KO", st], [kt("K1")], 64 * 3, k, ab)
+        V(lambda g, T: g.vector.tensor_tensor_scan(X(T, "SC", k), T.RST[:, 0:V4], PS(T, PK1, PK1 + V4), 0.0, OP.add, OP.max), [kt("K1"), "RST"], [kt("SC")], V4, k, ab)
+        TE(lambda g, T: group(g, [(PS(T, PK1, PK1 + V4), T.ID[:], T.KO[:, 0:V4])] + old(PS, T, PK1, "I4")
+                              + [(one(PS, T, PK1, o, False), T.IM1[:], X(T, "SC", k, 3, None, 4)) for o in range(4)]),
+           ["IM1", kt("SC"), st], [kt("K1")], 64 * 7, k, ab)
+        if ON["E"] == "s":
+            S(lambda g, T: g.scalar.activation(X(T, "E", k), PS(T, PK1, PK1 + V4), AF.Relu, bias=1.0), [kt("K1")], [kt("E")], V4, k, ab)
+        else:
+            V(lambda g, T: g.vector.tensor_scalar(X(T, "E", k), PS(T, PK1, PK1 + V4), -0.5, None, OP.is_gt), [kt("K1")], [kt("E")], V4, k, ab)
+        TE(lambda g, T: group(g, [(PS(T, PLU, PLU + NB), T.ID[:], T.B4[:, 0:NB])]
+                              + [(PS(T, PLU, PLU + NB), T[w][:], X(T, "E", k, o, None, 4)) for o, w in ((1, "ID"), (2, "I2"), (3, "I3"))]),
+           ["ID", "I2", "I3", "B4", kt("E")], [kt("PLU")], 256, k, ab)
+        V(lambda g, T: g.vector.tensor_copy(X(T, "LU", k), PS(T, PLU, PLU + NB)), [kt("PLU")], [kt("LU")], NB, k, ab)
+        if ON["LF"] == "s":
+            S(lambda g, T: g.scalar.activation(listed(T, s), PS(T, PLU, PLU + NB), AF.Copy), [kt("PLU")], [ks("LF")], NB, k, ab)
+        else:
+            V(lambda g, T: g.vector.tensor_copy(listed(T, s), PS(T, PLU, PLU + NB)), [kt("PLU")], [ks("LF")], NB, k, ab)
+    if not rest:
+        return
+    if s == 0:
+        V(lambda g, T: g.vector.tensor_copy(X(T, "CF", k, 0, CN), X(T, "PGI", k).indirect(X(T, "LU", k))), [kt("PGI"), kt("LU")], [kt("C32")], GA * CN + 45, k)
+    elif ON["C32"] == "s":
+        S(lambda g, T: g.scalar.activation(X(T, "CF", k, 0, CN), saved(T, s).indirect(X(T, "LU", k)), AF.Copy), [ks("CW"), kt("LU")], [kt("C32")], GA * CN + 40, k)
+    else:
+        V(lambda g, T: g.vector.tensor_copy(X(T, "CF", k, 0, CN), saved(T, s).indirect(X(T, "LU", k))), [ks("CW"), kt("LU")], [kt("C32")], GA * CN + 45, k)
+    p0 = TBW * s + TW + 4 * lo
+    V(lambda g, T: g.vector.tensor_tensor(X(T, "CF", k, CN, 2 * CN), T.TB[:, p0:p0 + 4 * CN].indirect(X(T, "LU", k)), T.POS[:], OP.add),
+      ["PRE%d" % s, kt("LU"), "POS"], [kt("PF")], GA * CN + 45, k)
+    if s == 0:
+        V(lambda g, T: g.vector.tensor_copy(X(T, "OF", k, 0, CN), X(T, "CF", k, 0, CN)), [kt("C32")], [kt("OFF")], CN, k)
+        V(lambda g, T: g.vector.tensor_copy(X(T, "OF", k, CN, 2 * CN), X(T, "CF", k, CN, 2 * CN)), [kt("PF")], [kt("PO")], CN, k)
+    else:
+        V(lambda g, T: g.vector.tensor_copy(X(T, "OF", k), X(T, "CF", k)), [kt("C32"), kt("PF")], [kt("OFF"), kt("PO")], 2 * CN, k)
 
     def lrep(g, T):
         for e in range(REP):
-            last = g.tensor.matmul(PL(T, e, REP * CN, REP), T.ID[:], T[lname][:, lo:lo + CN], True, True)
+            last = g.tensor.matmul(PL(T, e, REP * CN, REP), T.ID[:], T.LIMP[:, lo:lo + CN], True, True)
         return last
-    TE(lrep, [ltag, "ID"], [kt("PL")], REP * CN, k, lb)
+    TE(lrep, [kt("LIMP"), "ID"], [kt("PL")], REP * CN, k, lb)
 
     for t in range(NST):
-        cur, keep, five = ("C32", "C32", "I5F") if t == 0 else ("C16", "CI", "I5H")
-        mm5 = 4 * CN if t == 0 else CN
+        if t == 0:
+            cur, keep, tags, five, mm5 = (lambda T: X(T, "CF", k, 0, CN)), (lambda T: X(T, "CF", k, 0, CN)), ("C32", "C32"), "I5F", 4 * CN
+        else:
+            cur, keep, tags, five, mm5 = (lambda T: X(T, "C16", k)), (lambda T: X(T, "CI", k)), ("C16", "CI"), "I5H", CN
         for u in range(SUB):
             f0, f1, y0, y1 = 16 * HW * u, 16 * HW * (u + 1), HW * u, HW * (u + 1)
             fu, gu = "F%d.%d" % (k, u), "G%d.%d" % (k, u)
-            if f_on_vector(s, k, t, u):
-                V(lambda g, T, y0=y0, y1=y1, f0=f0, f1=f1: g.vector.tensor_copy(X(T, "F", k, f0, f1), T.XB[:].indirect(X(T, "OFF", k, y0, y1))),
-                  ["XB", kt("OFF")], [fu], GA * 16 * HW + 45, k)
-            else:
-                S(lambda g, T, y0=y0, y1=y1, f0=f0, f1=f1: g.scalar.activation(X(T, "F", k, f0, f1), T.XB[:].indirect(X(T, "OFF", k, y0, y1)), AF.Copy),
-                  ["XB", kt("OFF")], [fu], GA * 16 * HW + 40, k)
-            way = route(s, k, t, u)
-            if way == "dma":
-                dma("qs", lambda T, f0=f0, f1=f1: X(T, "F2", k, f0, f1), lambda T, f0=f0, f1=f1: X(T, "F", k, f0, f1), [fu], [gu], C["cp"], k, "cp_%d_%d" % (k, u), C["cpe"] * HW / 32)
-            elif way == "g":
-                op("g", lambda g, T, f0=f0, f1=f1: g.affine_select(X(T, "F2", k, f0, f1), X(T, "F", k, f0, f1), [[0, 16 * HW]], OP.is_ge, 0.0, 0, 0), [fu], [gu], None, 200 + 32 * HW, k)
+            S(lambda g, T, y0=y0, y1=y1, f0=f0, f1=f1: g.scalar.activation(X(T, "F", k, f0, f1), T.TB[:, TBW * s:TBW * s + TW].indirect(X(T, "OF", k, y0, y1)), AF.Copy),
+              ["XB%d" % s, kt("OFF")], [fu], GA * 16 * HW + 40, k)
+            op("g", lambda g, T, f0=f0, f1=f1: g.affine_select(X(T, "F2", k, f0, f1), X(T, "F", k, f0, f1), [[0, 16 * HW]], OP.is_ge, 0.0, 0, 0), [fu], [gu], None, 200 + 32 * HW, k)
         dts = ["D%d.%d" % (k, u) for u in range(SUB)]
         for u in range(SUB):
             f0, f1, y0, y1 = 16 * HW * u, 16 * HW * (u + 1), HW * u, HW * (u + 1)
             fu, gu, du = "F%d.%d" % (k, u), "G%d.%d" % (k, u), dts[u]
-            way = route(s, k, t, u)
-            if way in ("ts", "tv"):
-                db = "d%d" % (k % NDB)
-                if way == "ts":
-                    S(lambda g, T, y0=y0, y1=y1, f0=f0, f1=f1: g.scalar.activation(X(T, "F2", k, f0, f1), X(T, "F", k, f0, f1).indirect(X(T, "PO", k, y0, y1)), AF.Copy),
-                      [fu, kt("PO")], [gu], GA * 16 * HW + 40, k)
-                else:
-                    V(lambda g, T, y0=y0, y1=y1, f0=f0, f1=f1: g.vector.tensor_copy(X(T, "F2", k, f0, f1), X(T, "F", k, f0, f1).indirect(X(T, "PO", k, y0, y1))),
-                      [fu, kt("PO")], [gu], GA * 16 * HW + 45, k)
-                TE(lambda g, T, f0=f0, f1=f1, db=db: group(g, [(T["P_" + db][:, 0:16 * HW], T.IM1[:], X(T, "F", k, f0, f1)), (T["P_" + db][:, 0:16 * HW], T.ID[:], X(T, "F2", k, f0, f1))]),
-                   [fu, gu, "ID", "IM1"], ["P" + db], 32 * HW, k, db)
-                S(lambda g, T, f0=f0, f1=f1, db=db: g.scalar.activation(X(T, "D", k, f0, f1), T["P_" + db][:, 0:16 * HW], AF.Abs), ["P" + db], [du], 16 * HW, k, db)
-            else:
-                V(lambda g, T, y0=y0, y1=y1, f0=f0, f1=f1: g.vector.tensor_tensor(X(T, "D", k, f0, f1), X(T, "F", k, f0, f1).indirect(X(T, "PO", k, y0, y1)), X(T, "F2", k, f0, f1), OP.subtract),
-                  [fu, gu, kt("PO")], [du], GA * 16 * HW + 45, k)
-                S(lambda g, T, f0=f0, f1=f1: g.scalar.activation(X(T, "D", k, f0, f1), X(T, "D", k, f0, f1), AF.Abs), [du], [du], 16 * HW, k)
+            V(lambda g, T, y0=y0, y1=y1, f0=f0, f1=f1: g.vector.tensor_tensor(X(T, "D", k, f0, f1), X(T, "F", k, f0, f1).indirect(X(T, "OF", k, CN + y0, CN + y1)), X(T, "F2", k, f0, f1), OP.subtract),
+              [fu, gu, kt("PO")], [du], GA * 16 * HW + 45, k)
+            S(lambda g, T, f0=f0, f1=f1: g.scalar.activation(X(T, "D", k, f0, f1), X(T, "D", k, f0, f1), AF.Abs), [du], [du], 16 * HW, k)
             for q in range(NQ):
                 V(lambda g, T, f0=f0, f1=f1, y0=y0, y1=y1, q=q: g.vector.tensor_tensor(X(T, "C", k, f0 + q, f1, NQ), X(T, "D", k, f0 + q, f1, NQ), PL(T, REP * y0, REP * y1), OP.is_gt),
                   [du, kt("PL")], ["C%d.%d.%d" % (k, u, q)], REP * HW, k, lb)
 
-        def asum(g, T, w, x, als, first, final):
-            for a in als:
-                last = g.tensor.matmul(PS(T, PA, PA + CN), T[w][:, 15 - a:143 - a], X(T, x, k, a, None, 16), first and a == als[0], final and a == als[-1])
-            return last
-        TE(lambda g, T: asum(g, T, "WB", "D", range(16), True, False), dts + ["WB"], [kt("PA")], 16 * CN, k, ab)
+        def asum(T, w, x, als):
+            return [(PS(T, PA, PA + CN), T[w][:, 15 - a:143 - a], X(T, x, k, a, None, 16)) for a in als]
+        TE(lambda g, T: group(g, asum(T, "WB", "D", range(16)), True, False), dts + ["WB"] + ["LF%d.0" % j for j in range(NCH) if s + k + t == 0], [kt("PA")], 16 * CN, k, ab)
         for q in range(NQ):
-            TE(lambda g, T, q=q: asum(g, T, "WK", "C", range(q, 16, NQ), False, q == NQ - 1), ["C%d.%d.%d" % (k, u, q) for u in range(SUB)] + ["WK"], [kt("PA")], REP * CN, k, ab)
+            TE(lambda g, T, q=q: group(g, asum(T, "WK", "C", range(q, 16, NQ)), False, q == NQ - 1),
+               ["C%d.%d.%d" % (k, u, q) for u in range(SUB)] + ["WK"], [kt("PA")], REP * CN, k, ab)
         ns = "NS%d.%d" % (k, t)
         S(lambda g, T, t=t: g.scalar.activation(X(T, "NS", k, CN * t, CN * (t + 1)), PS(T, PA, PA + CN), AF.Sign, bias=-8.0 * BIG), [kt("PA")], [ns], CN, k, ab)
         S(lambda g, T: g.scalar.activation(X(T, "RL", k), PS(T, PA, PA + CN), AF.Relu, bias=-8.0 * BIG), [kt("PA")], [kt("RL")], CN, k, ab)
-        TE(lambda g, T, t=t, cur=cur, five=five: group(g, [(PS(T, PB, PB + CN), T.CST[:], T.ONES[:, 0:CN]), (PS(T, PB, PB + CN), T[five][:], X(T, cur, k)),
+        TE(lambda g, T, t=t, cur=cur, five=five: group(g, [(PS(T, PB, PB + CN), T.CST[:], T.ONES[:, 0:CN]), (PS(T, PB, PB + CN), T[five][:], cur(T)),
                                                            (PS(T, PB, PB + CN), T.WS[:], X(T, "NS", k, CN * t, CN * (t + 1))), (PS(T, PB, PB + CN), T.IDF[:], X(T, "RL", k))]),
-           [ns, kt("RL"), "WS", "IDF", "CST", "ONES", five, kt(cur)], [kt("PB")], 6 * CN + mm5, k, ab)
-        V(lambda g, T, keep=keep: g.vector.tensor_tensor(X(T, "O2", k), PS(T, PB, PB + CN), X(T, keep, k), OP.max), [kt("PB"), kt(keep)], [kt("O2")], CN, k, ab)
-        V(lambda g, T: g.vector.tensor_scalar(X(T, "CI", k), X(T, "O2", k), 2047, None, OP.bitwise_and), [kt("O2")], [kt("CI")], CN, k)
+           [ns, kt("RL"), "WS", "IDF", "CST", "ONES", five, kt(tags[0])], [kt("PB")], 6 * CN + mm5, k, ab)
+        V(lambda g, T, keep=keep: g.vector.tensor_tensor(X(T, "O2", k), PS(T, PB, PB + CN), keep(T), OP.max), [kt("PB"), kt(tags[1])], [kt("O2")], CN, k, ab)
         if t < NST - 1:
-            V(lambda g, T: g.vector.tensor_copy(X(T, "OFF", k), X(T, "CI", k)), [kt("CI")], [kt("OFF")], CN, k)
+            V(lambda g, T: g.vector.tensor_scalar(X(T, "CI", k), X(T, "O2", k), 2047, None, OP.bitwise_and), [kt("O2")], [kt("CI")], CN, k)
+            V(lambda g, T: g.vector.tensor_copy(X(T, "OF", k, 0, CN), X(T, "CI", k)), [kt("CI")], [kt("OFF")], CN, k)
             V(lambda g, T: g.vector.tensor_copy(X(T, "C16", k), X(T, "CI", k)), [kt("CI")], [kt("C16")], CN, k)
+    V(lambda g, T: g.vector.tensor_scalar(message(T, "c", k, s, 0), X(T, "O2", k), 2047, None, OP.bitwise_and), [kt("O2")], [ks("CO")], CN, k)
+    op("g", ("c", k, s), [ks("CO")], [ks("csent")], None, C["send"], k)
+    op("hop", "c", [ks("csent")], [ks("CL")], None, C["hop"], k, "cl_%d_%d" % (k, s))
+    V(lambda g, T: g.vector.tensor_copy(X(T, "LN", k), listed(T, s + 1)), [ks("LF", s + 1)], [kt("LN")], NB, k)
+    V(lambda g, T: g.vector.tensor_copy(saved(T, s + 1).indirect(X(T, "LN", k)), message(T, "c", k, s, 1)), [ks("CL"), kt("LN")], [ks("CW", s + 1)], C["sc"] * CN + 45, k)
 
     TE(lambda g, T: group(g, [(PS(T, PN, PN + 3 * NB), T.WB[:, 15 - a:143 - a], X(T, "NS", k, a, None, 16)) for a in range(16)]),
        ["NS%d.%d" % (k, t) for t in range(NST)] + ["WB"], [kt("PN")], 1024, k, ab)
-    S(lambda g, T: g.scalar.activation(X(T, "FM", k, 0, 3 * NB), PS(T, PN, PN + 3 * NB), AF.Relu, bias=-15.0, scale=-1.0), [kt("PN")], [kt("FM")], 3 * NB, k, ab)
+    if ON["FM"] == "s":
+        S(lambda g, T: g.scalar.activation(X(T, "FM", k, 0, 3 * NB), PS(T, PN, PN + 3 * NB), AF.Relu, bias=-15.0, scale=-1.0), [kt("PN")], [kt("FM")], 3 * NB, k, ab)
+    else:
+        V(lambda g, T: g.vector.tensor_scalar(X(T, "FM", k, 0, 3 * NB), PS(T, PN, PN + 3 * NB), -15.0, None, OP.is_lt), [kt("PN")], [kt("FM")], 3 * NB, k, ab)
 
     def msum(g, T):
         for at, w in ((PMA, "RH"), (PMB, "R1")):
             last = group(g, [(PS(T, at, at + NB), T[w][:], X(T, "FM", k, t * NB, (t + 1) * NB)) for t in range(NST)])
         return last
     TE(msum, [kt("FM"), "RH", "R1"], [kt("PM")], 384, k, ab)
-    S(lambda g, T: g.scalar.activation(X(T, "RR", k, 0, 3 * NB), PS(T, PN + 2 * NB, PN + 5 * NB), AF.Identity, bias=191.75), [kt("PN"), kt("PM")], [kt("RR")], 3 * NB, k, ab)
+    if ON["RR"] == "s":
+        S(lambda g, T: g.scalar.activation(X(T, "RR", k, 0, 3 * NB), PS(T, PN + 2 * NB, PN + 5 * NB), AF.Identity, bias=191.75), [kt("PN"), kt("PM")], [kt("RR")], 3 * NB, k, ab)
+    else:
+        V(lambda g, T: g.vector.tensor_scalar(X(T, "RR", k, 0, 3 * NB), PS(T, PN + 2 * NB, PN + 5 * NB), 191.75, None, OP.add), [kt("PN"), kt("PM")], [kt("RR")], 3 * NB, k, ab)
 
-    def newv(g, T):
-        terms = [(PS(T, PXY, PXY + 9 * NB), T.ID[:], T.XYC[:, 0:9 * NB])]
-        terms += [(PS(T, PXY, PXY + V4), T.IM64[:], X(T, "E", k)), (PS(T, PXY + V4, PXY + 2 * V4), T.I64[:], X(T, "E", k))]
-        terms += [(PS(T, PXY, PXY + V4), T.ID[:], x) for x in old(T, 0, V4)]
-        terms += [(PS(T, PXY + 2 * V4, PXY + 9 * NB), T.ID[:], X(T, "FM", k, t * NB, (t + 1) * NB)) for t in range(NST)]
+    def early(g, T):
+        terms = [(PL(T, 0, 9 * NB), T.ID[:], T.XYC[:, 0:9 * NB])]
+        terms += laid(PL, T, 0, "IM64", "E", 0, home) + laid(PL, T, V4, "I64", "E", 0, home) + old(PL, T, 0, "ID", home)
         if s:
-            terms += [(PS(T, PXY + 2 * V4, PXY + 9 * NB), T.ID[:], X(T, "HL", k, h0 + 2 * V4, h0 + 9 * NB))]
+            terms += [(PL(T, 2 * V4, 9 * NB), T.ID[:], X(T, "HP", k, h0 + 2 * V4, h0 + 9 * NB))]
+        return group(g, terms, True, False)
+    TE(early, xyc + ["ID", "IM64", "I64", kt("E"), st], [kt("PL")], 64 * (18 if home else 6 + (s == 0)), k, lb)
+    TE(lambda g, T: group(g, [(PL(T, 2 * V4, 9 * NB), T.ID[:], X(T, "FM", k, t * NB, (t + 1) * NB)) for t in range(NST)], False, False), ["ID", kt("FM"), kt("PM")], [kt("PL")], 192, k, lb)
+
+    def late(g, T):
+        terms = []
         for o in range(4):
-            x, y = PS(T, PXY + NB * o, PXY + NB * (o + 1)), PS(T, PXY + V4 + NB * o, PXY + V4 + NB * (o + 1))
+            x, y = one(PL, T, 0, o, home), one(PL, T, V4, o, home)
             terms += [(y, T.IMH[:], X(T, "RR", k, 0, NB)), (x, T.IM2[:], X(T, "RR", k, NB, 2 * NB)), (x, T.ID[:], X(T, "RR", k, 2 * NB, 3 * NB))]
-        return group(g, terms)
-    TE(newv, xyc + ["ID", "IM64", "I64", "IMH", "IM2", kt("E"), kt("FM"), kt("RR"), st], [kt("XY")], 64 * (17 + 2 * npart), k, ab)
-    hp, hl = "HP%d.%d" % (k, s), "HL%d.%d" % (k, s)
-    g0 = HPW * s
-    S(lambda g, T: g.scalar.activation(X(T, "HP", k, g0, g0 + 9 * NB), PS(T, PXY, PXY + 9 * NB), AF.Relu), [kt("XY")], [hp], 9 * NB, k, ab)
-    op("g", ("send", k, s), [hp], ["snt%d.%d" % (k, s)], None, 600, k)
-    op("hop", "hop", ["snt%d.%d" % (k, s)], [hl], None, C["hop"], k, "hl_%d_%d" % (k, s))
-    V(lambda g, T: g.vector.tensor_copy(X(T, "CW", k).indirect(X(T, "LU", k)), X(T, "CI", k)), [kt("CI"), kt("LU")], [kt("CW")], C["sc"] * CN + 45, k)
-    if s == NSL - 1:
-        dma("qs", lambda T: T.yg[:, 4 * lo:4 * (lo + CN)], lambda T: X(T, "CW", k), [kt("CW")], [], 2500, k, None, 500)
-        V(lambda g, T: g.vector.tensor_tensor(X(T, "YV", k), X(T, "HL", k, g0, g0 + V4), X(T, "HL", k, g0 + V4, g0 + 2 * V4), OP.add), [hl], [kt("YV")], 32, k)
-        S(lambda g, T: g.scalar.activation(X(T, "YM", k), X(T, "HL", k, g0 + 2 * V4, g0 + 2 * V4 + NB), AF.Copy), [hl], [kt("YM")], NB, k)
+        return group(g, terms, False, True)
+    TE(late, ["ID", "IMH", "IM2", kt("RR")], [kt("PL")], 768, k, lb)
+    hp, g0 = ks("HP"), HPW * s
+    if ON["HP"] == "s":
+        S(lambda g, T: g.scalar.activation(X(T, "HP", k, g0, g0 + 9 * NB), PL(T, 0, 9 * NB), AF.Relu), [kt("PL")], [hp], 9 * NB, k, lb)
+    else:
+        V(lambda g, T: g.vector.tensor_scalar(X(T, "HP", k, g0, g0 + 9 * NB), PL(T, 0, 9 * NB), 0.0, None, OP.max), [kt("PL")], [hp], 9 * NB, k, lb)
+    if home:
+        dma("qa" if k == NCH - 1 else "qs", lambda T: T.yg[:, 4 * lo:4 * (lo + CN)], lambda T: saved(T, NSL), [ks("CW", NSL)], [], 2500, k, 500)
+        V(lambda g, T: g.vector.tensor_tensor(X(T, "YV", k), X(T, "HP", k, g0, g0 + V4), X(T, "HP", k, g0 + V4, g0 + 2 * V4), OP.add), [hp], [kt("YV")], 32, k)
+        S(lambda g, T: g.scalar.activation(X(T, "YM", k), X(T, "HP", k, g0 + 2 * V4, g0 + 2 * V4 + NB), AF.Copy), [hp], [kt("YM")], NB, k)
         for o in range(4):
-            dma("qa" if k == NCH - 1 and o > 1 else "qs", lambda T, o=o: T.yv[o::4, lo:lo + CN], lambda T, o=o: X(T, "YV", k, NB * o, NB * (o + 1)), [kt("YV")], [], 2000, k)
-        dma("qa" if k == NCH - 1 else "qs", lambda T: T.ym[:, lo:lo + CN], lambda T: X(T, "YM", k), [kt("YM")], [], 2000, k)
+            dma("qs", lambda T, o=o: T.yv[o::4, lo:lo + CN], lambda T, o=o: X(T, "YV", k, NB * o, NB * (o + 1)), [kt("YV")], [], 2000, k)
+        dma("qs", lambda T: T.ym[:, lo:lo + CN], lambda T: X(T, "YM", k), [kt("YM")], [], 2000, k)
 
 
 def depend(ops):
@@ -324,7 +366,10 @@ def plan(ops, deps, C):
     tail = [0.0] * n
     for i in range(n - 1, -1, -1):
         tail[i] = ops[i]["cost"] + ops[i]["eng"] + max([tail[j] + sem for j in succ[i]] + [0.0])
-    prio = [tail[i] - LAG * o["k"] if o["r"] or o["q"] not in ("qs", "qa") else 1e9 - i for i, o in enumerate(ops)]
+    x, prio = SEED, []
+    for i, o in enumerate(ops):
+        x = (x * 1103515245 + 12345) % 2 ** 31
+        prio.append(1e9 - i if o["q"] in ("qs", "qa") and not o["r"] else tail[i] - LAG * o["k"] + AMP * x / 2 ** 31)
     left = [len(d) for d in deps]
     ready_at, fin = [0.0] * n, [0.0] * n
     free, bankfree, bankq = {}, {}, {}
@@ -381,8 +426,14 @@ def get_plan():
 get_plan()
 
 
-def helpers(topo, core, nxt, group):
-    return [c for c in topo.cores_of(core) if c not in group and topo.die(c) == topo.die(core) and topo.may_write(c, nxt)]
+def helpers(topo, cores, r):
+    own, n = cores[r], len(cores)
+    free = [c for c in topo.cores_of(own) if c not in cores]
+    ports = [c for c in free if topo.may_write(c, cores[(r - 1) % n])]
+    port = [c for c in ports if topo.die(c) == topo.die(own)]
+    far = [c for c in ports if c not in port]
+    rest = [c for c in free if c not in ports and topo.die(c) != topo.die(own)]
+    return port, {1: far[0], 2: rest[0], 3: far[-1]}
 
 
 def bits(topo, a, b):
@@ -391,60 +442,58 @@ def bits(topo, a, b):
 
 def rank_program(g, core, T, topo):
     cores = list(T.cores)
-    n = len(cores)
     rank = T.rank_of(core)
     if rank is not None:
         run_rank(g, core, T, topo, cores, rank)
         return
-    for r in range(n):
-        own, nxt, prv = cores[r], cores[(r + 1) % n], cores[(r + 3) % n]
-        hs = helpers(topo, own, nxt, cores)
-        if core in hs:
-            lims = [(name, dst) for name, dst, h in (("1", nxt, hs[0]), ("3", prv, hs[-1])) if h == core]
-            hand_on(g, core, T, topo, own, nxt, [k for k in range(NCH) if hs[k % len(hs)] == core], lims)
+    for r in range(len(cores)):
+        port, table = helpers(topo, cores, r)
+        if core in port or core in table.values():
+            hand_on(g, core, T, topo, cores, r, [k for k in range(NCH) if port[k % len(port)] == core], [s for s in table if table[s] == core])
 
 
-def hand_on(g, core, T, topo, own, nxt, ks, lims):
-    loc = 0
+def hand_on(g, core, T, topo, cores, r, ks, slots):
+    own, n, loc = cores[r], len(cores), 0
 
     def remote(out, in_, sem, dst):
         rid, pid = topo.addr(dst, core)
         g.remote_dma(out, in_, T.sem[sem], T.sem.loc, pid, rid, topo.mask(core, dst))
         return bits(topo, core, dst)
 
-    if lims:
-        g.wait_ge(T.sem.lh, bits(topo, own, core))
-    for name, dst in lims:
-        loc += remote(T["LS" + name][:], T.LIMP[:], "ls" + name, dst)
-    for s in range(NSL):
-        for k in ks:
-            g.wait_ge(T.sem["hr_%d_%d" % (k, s)], bits(topo, own, core))
-            a, b = HPW * s, HPW * s + 9 * NB
-            loc += remote(X(T, "HL", k, a, b), X(T, "HP", k, a, b), "hl_%d_%d" % (k, s), nxt)
-    if loc:
-        g.wait_ge(T.sem.loc, loc)
+    ops, order = get_plan()[:2]
+    for i in order:
+        if ops[i]["q"] != "g" or not isinstance(ops[i]["fn"], tuple):
+            continue
+        kind, k, s = ops[i]["fn"]
+        if kind == "t" and s in slots:
+            g.wait_ge(T.sem["tr%d" % s], bits(topo, own, core))
+            loc += remote(T.TB[:, TBW * s:TBW * (s + 1)], T.TB[:, TBW * s:TBW * (s + 1)], "tl%d" % s, cores[(r - s) % n])
+        elif kind != "t" and k in ks:
+            g.wait_ge(T.sem["%sr_%d_%d" % (kind, k, s)], bits(topo, own, core))
+            loc += remote(message(T, kind, k, s, 1), message(T, kind, k, s, 0), "%sl_%d_%d" % (kind, k, s), cores[(r - 1) % n])
+    g.wait_ge(T.sem.loc, loc)
 
 
 def run_rank(g, core, T, topo, cores, rank):
     n = len(cores)
-    nxt, opp, prv = cores[(rank + 1) % n], cores[(rank + 2) % n], cores[(rank + 3) % n]
-    hs, hprev, hnext = helpers(topo, core, nxt, cores), helpers(topo, prv, core, cores), helpers(topo, nxt, opp, cores)
+    port, table = helpers(topo, cores, rank)
     ops, order, deps, _f = get_plan()
     eng = {"v": g.vector, "s": g.scalar, "t": g.tensor, "g": g, "qs": g.sync, "qa": g.scalar}
     semname = {"v": "v", "s": "s", "t": "t", "g": "gc"}
     count = {"v": 0, "s": 0, "t": 0, "g": 0}
-    done, waited, banks, loc, dmas = {}, {}, {}, [0], {}
+    done, waited, banks, loc, dmas = {}, {}, {}, [0], []
+    place = {i: at for at, i in enumerate(order)}
 
-    def queue(q):
-        return "s" if q == "qa" else q
-
-    def wait(q, d):
-        if d in done:
-            sem, val = done[d]
-            key = (queue(q), sem)
-            if waited.get(key, 0) < val:
+    def wait(q, ds):
+        known = waited.setdefault("s" if q == "qa" else q, {})
+        for d in sorted((d for d in ds if d in done), key=lambda d: -place[d]):
+            sem, val, before = done[d]
+            if known.get(sem, 0) < val:
                 eng[q].wait_ge(T.sem[sem], val)
-                waited[key] = val
+                known[sem] = val
+                for x in before:
+                    known[x] = max(known.get(x, 0), before[x])
+        return dict(known)
 
     def remote(out, in_, sem, dst):
         rid, pid = topo.addr(dst, core)
@@ -455,37 +504,37 @@ def run_rank(g, core, T, topo, cores, rank):
         o = ops[i]
         q = o["q"]
         if q == "hop":
-            src = hprev[o["k"] % len(hprev)] if o["fn"] == "hop" else {"ls1": hprev[0], "ls2": opp, "ls3": hnext[-1]}[o["sem"]]
-            done[i] = (o["sem"], bits(topo, src, core))
+            if o["fn"] == "t":
+                s = int(o["sem"][-1])
+                src = helpers(topo, cores, (rank + s) % n)[1][s]
+            else:
+                near = helpers(topo, cores, (rank + 1) % n)[0]
+                src = near[o["k"] % len(near)]
+            done[i] = (o["sem"], bits(topo, src, core), {})
             continue
-        for d in sorted(deps[i], reverse=True):
-            if not (q == "t" and ops[d]["q"] == "t"):
-                wait(q, d)
+        need = [d for d in deps[i] if not (q == "t" and ops[d]["q"] == "t")]
         if o["bank"]:
-            for qq, d in banks.get(o["bank"], {}).items():
-                if qq != q:
-                    wait(q, d)
+            need += [d for qq, d in banks.get(o["bank"], {}).items() if qq != q]
             banks.setdefault(o["bank"], {})[q] = i
+        before = wait(q, need)
         if q in ("qs", "qa"):
             out, in_ = o["fn"]
             eng[q].dma_start(out(T), in_(T)).then_inc(T.sem[o["sem"]], 16)
-            dmas[o["sem"]] = dmas.get(o["sem"], 0) + 16
-            done[i] = (o["sem"], dmas[o["sem"]])
-        elif o["fn"] == "limsend":
-            for h in sorted({hs[0], hs[-1]}):
-                remote(T.LIMP[:], T.LIMP[:], "lh", h)
-            remote(T.LS2[:], T.LIMP[:], "ls2", opp)
+            dmas.append(o["sem"])
+            done[i] = (o["sem"], 16, before)
         elif q == "g" and isinstance(o["fn"], tuple):
-            _x, k, s = o["fn"]
-            a, b = HPW * s, HPW * s + 9 * NB
-            remote(X(T, "HP", k, a, b), X(T, "HP", k, a, b), "hr_%d_%d" % (k, s), hs[k % len(hs)])
+            kind, k, s = o["fn"]
+            if kind == "t":
+                remote(T.TB[:, TBW * s:TBW * (s + 1)], T.TB[:, 0:TBW], "tr%d" % s, table[s])
+            else:
+                remote(message(T, kind, k, s, 0), message(T, kind, k, s, 0), "%sr_%d_%d" % (kind, k, s), port[k % len(port)])
         else:
             ins = o["fn"](g, T)
             count[q] += 1
             ins.then_inc(T.sem[semname[q]], 1)
-            done[i] = (semname[q], count[q])
+            done[i] = (semname[q], count[q], before)
     for q in ("v", "s", "t", "g"):
         g.wait_ge(T.sem[semname[q]], count[q])
     g.wait_ge(T.sem.loc, loc[0])
     for sem in dmas:
-        g.wait_ge(T.sem[sem], dmas[sem])
+        g.wait_ge(T.sem[sem], 16)

@@ -10,10 +10,12 @@ NSL, NST = 4, 3
 BIG = 2 ** 14
 V4 = 4 * NB
 HPW = 40
-CWW = 4 * CN + 8
+CWW = (4 * CN + NB) * NCH
+TEAMS = ((0, 1), (2, 3))
+CREWS = ((0,), (1,), (2,), (3,))
 TW, TBW = 2048, 3072
 
-PER = {"PGI": (256, "int32"), "CW": (CWW * (NSL + 1), "float32"), "SC": (16, "bfloat16"), "E": (16, "bfloat16"), "LU": (4, "uint16"), "LN": (4, "uint16"),
+PER = {"PGI": (256, "int32"), "SC": (16, "bfloat16"), "E": (16, "bfloat16"), "LU": (4, "uint16"), "LN": (4, "uint16"),
        "CF": (128, "float32"), "C16": (64, "float16"), "OF": (128, "uint16"),
        "RL": (64, "float32"), "O2": (64, "int32"), "CI": (64, "int32"), "CO": (64 * NSL, "int32"), "CL": (64 * NSL, "int32"),
        "NS": (192, "bfloat16"), "FM": (16, "bfloat16"), "RR": (16, "bfloat16"),
@@ -25,8 +27,10 @@ ONE = {"TB": (TBW * NSL, "bfloat16"), "LIM": (256, "bfloat16"), "LIMP": (256, "b
        "WS": (128, "bfloat16"), "I8K": (128, "bfloat16"), "IDF": (128, "float32"),
        "I2": (128, "bfloat16"), "I3": (128, "bfloat16"), "I4": (128, "bfloat16"), "IM1": (128, "bfloat16"), "IM2": (128, "bfloat16"), "IMH": (128, "bfloat16"),
        "I64": (128, "bfloat16"), "IM64": (128, "bfloat16"), "I5H": (128, "float16"), "I5F": (128, "float32"),
-       "POS": (64, "bfloat16"), "BI": (16, "int32"), "BL": (4, "int32"), "B4": (16, "bfloat16"), "LL": (4, "uint16"),
-       "KO": (64, "bfloat16"), "RST": (64, "bfloat16"), "XYC": (40, "bfloat16"), "VI": (64, "int32"), "VB": (64, "bfloat16")}
+       "POS": (128, "bfloat16"), "BI": (4, "int32"), "BL": (4, "int32"), "B4": (16, "bfloat16"), "LL": (4, "uint16"),
+       "KO": (64, "bfloat16"), "RST": (64, "bfloat16"), "VI": (64, "int32"), "VB": (64, "bfloat16"), "CW": (CWW * (NSL + 1), "float32")}
+for _m in set(len(_t) for _t in TEAMS + CREWS):
+    ONE["XY%d" % _m] = (9 * NB * _m, "bfloat16")
 SCRATCH = {}
 for _n in PER:
     SCRATCH[_n] = ("sbuf", [128, PER[_n][0] * NCH], PER[_n][1])
@@ -38,7 +42,7 @@ for _k in range(NCH):
 SEMAPHORES = ["v", "s", "t", "gc", "loc"] + ["%s%d" % (_b, _s) for _b in ("tr", "tl") for _s in range(1, NSL)]
 SEMAPHORES += ["%s_%d_%d" % (_b, _k, _s) for _b in ("cr", "cl") for _k in range(NCH) for _s in range(NSL)]
 SEMAPHORES += ["%s_1_%d" % (_b, _s) for _b in ("wr", "wl") for _s in range(NSL)]
-PA, PB, PK1, PLU, PN, PMA, PMB, PK0 = 0, 64, 128, 144, 148, 160, 164, 192
+PA, PB, PK1, PLU, PN, PK0 = 0, 64, 128, 192, 208, 320
 
 
 def group(g, terms, first=True, final=True):
@@ -52,20 +56,32 @@ def X(T, name, k, a=0, b=None, step=1):
     return T[name][:, w * k + a:w * k + (w if b is None else b):step]
 
 
-def cursors(T, s, k, a, b):
-    return T.CW[:, CWW * (NCH * s + k) + a:CWW * (NCH * s + k) + b]
+def saved(T, s, k, m=1):
+    return T.CW[:, CWW * s + 4 * CN * k:CWW * s + 4 * CN * (k + m)]
+
+
+def lists(T, s, k, m):
+    return T.CW[:, CWW * s + 4 * CN * NCH + NB * k:CWW * s + 4 * CN * NCH + NB * (k + m)]
 
 
 def message(T, kind, k, s, landed):
     if kind == "w":
-        return cursors(T, s + landed, 0, 0, CWW * NCH)
-    return X(T, "CL" if landed else "CO", k, CN * s, CN * (s + 1))
+        return T.CW[:, CWW * (s + landed):CWW * (s + landed + 1)]
+    m = [len(crew) for crew in CREWS if crew[0] == k][0]
+    return T["CL" if landed else "CO"][:, CN * (NSL * k + m * s):CN * (NSL * k + m * (s + 1))]
 
 
-COST = {"ga": 1.4, "sc": 4.0, "tc": 0.45, "hop": 3500.0, "sem": 140.0, "vo": 20.0, "so": 50.0, "pm": 1.0, "send": 500.0}
+COST = {"ga": 1.25, "sc": 4.0, "tc": 0.4, "hop": 3300.0, "sem": 160.0, "vo": 15.0, "so": 70.0, "pm": 1.0, "send": 600.0}
 AMP, SEED = 0.0, 1
-SHORT, LAG = 600, 1500.0
-ON = {"E": "v", "FM": "v", "RR": "v", "HP": "v", "C32": "s", "LF": "s"}
+DIRECT = (0, 1, 2, 3)
+AFTER, WH = 3, 22000
+LAST = NCH - 1
+SHORT, LAG, GAP = 600, 1500.0, 1000.0
+ON = {"E": "v", "FM": "v", "RR": "v", "HP": "v", "C32": "s", "LF": "v"}
+
+
+def copier(s, k, t, u):
+    return "v" if (t, k, u) == (0, 0, 0) else "s" if (t, k, u) == (NST - 1, NCH - 1, SUB - 1) else "g"
 
 
 def build(C):
@@ -113,15 +129,17 @@ def build(C):
     V(lambda g, T: g.vector.memset(T.ONES[:], 1.0), [], ["ONES"], 64)
     G(lambda g, T: g.affine_select(T.ID[:], T.ONES[:], [[-1, 128]], OP.is_equal, 0.0, 0, 1), ["ONES"], ["ID"], 128)
     G(lambda g, T: g.iota(T.KO[:], [[0, NB * NCH], [-1, 4]], 0, 0, allow_small_or_imprecise_dtypes=True), [], ["KO"], 64)
-    G(lambda g, T: g.iota(T.BI[:], [[0, NCH], [4, NB]], 0, 4 * NB), [], ["BI"], 16)
-    G(lambda g, T: g.iota(T.POS[:], [[0, SUB], [16, HW]], 0, 0, allow_small_or_imprecise_dtypes=True), [], ["POS"], 64)
+    G(lambda g, T: g.iota(T.BI[:], [[4, NB]], 0, 4 * NB), [], ["BI"], 4)
+    G(lambda g, T: g.iota(T.POS[:], [[0, SUB * 2], [16, HW]], 0, 0, allow_small_or_imprecise_dtypes=True), [], ["POS"], 128)
     G(lambda g, T: g.affine_select(T.BO0[:], T.ONES[:], [[-16, 8], [0, 16]], OP.is_ge, 0.0, 0, 1), ["ONES"], ["BO0"], 128)
     G(lambda g, T: g.affine_select(T.BO[:], T.BO0[:], [[16, 8], [0, 16]], OP.is_ge, 0.0, 15, -1), ["BO0"], ["BO"], 128)
     G(lambda g, T: g.iota(T.RI[:], [[1, 128]], 0, -1), [], ["RI"], 128)
     V(lambda g, T: g.vector.memset(T.RST[:], 0.0), [], ["RST"], 16)
     V(lambda g, T: g.vector.memset(T.RST[:, 0:V4 * NCH:4], -1024.0), [], ["RST"], 16)
     V(lambda g, T: g.vector.tensor_scalar(T.BI[:], T.BI[:], 4 * CN - 1, None, OP.bitwise_and), ["BI"], ["BI"], 4)
-    V(lambda g, T: g.vector.tensor_copy(T.B4[:], T.BI[:]), ["BI"], ["B4"], 4)
+    for team in CREWS:
+        for k in team:
+            V(lambda g, T, k=k, at=4 * CN * (k - team[0]): g.vector.tensor_scalar(T.B4[:, NB * k:NB * (k + 1)], T.BI[:, 0:NB], at, None, OP.add), ["BI"], ["B4.%d" % k], 4)
     V(lambda g, T: g.vector.tensor_scalar(T.BL[:], T.BI[:, 0:NB], 2, None, OP.logical_shift_right), ["BI"], ["BL"], 4)
     V(lambda g, T: g.vector.tensor_copy(T.LL[:], T.BL[:]), ["BL"], ["LL"], 4)
     for name, f in (("I4", 4), ("IM1", -1), ("I2", 2), ("I3", 3), ("I5F", 5), ("I5H", 5), ("IM2", -2), ("IMH", -0.5), ("I64", 64), ("IM64", -64), ("I8K", 8 * BIG), ("IDF", 1)):
@@ -135,9 +153,9 @@ def build(C):
     scaled("R1", "RH", 2)
     scaled("CST", "ONES", 1.0 / 128)
     V(lambda g, T: g.vector.tensor_tensor(T.WS[:], T.NBO[:], T.I8K[:], OP.add), ["NBO", "I8K"], ["WS"], 256)
-    xyc = [fill("XYC", 0, V4, 193.0), fill("XYC", V4, 2 * V4, 40.0), fill("XYC", 2 * V4, 40, 0.0)]
-    for k in range(NCH):
-        V(lambda g, T, k=k: g.vector.memset(cursors(T, 0, k, 4 * CN, CWW), 0.0), [], ["LF%d.0" % k], 8)
+    xyc = {}
+    for m in sorted(set(len(team) for team in TEAMS + CREWS)):
+        xyc[m] = [fill("XY%d" % m, 0, V4 * m, 193.0), fill("XY%d" % m, V4 * m, 2 * V4 * m, 40.0), fill("XY%d" % m, 2 * V4 * m, 9 * NB * m, 0.0)]
     allk = lambda b: ["%s%d" % (b, k) for k in range(NCH)]
     W4 = V4 * NCH
     keys = lambda T: [(T.P_a0[:, PK0:PK0 + W4], T.ID[:], T.KO[:])] + [(T.P_a0[:, PK0 + o:PK0 + W4:4], T.I4[:], T.VB[:, V4 * o:V4 * (o + 1)]) for o in range(4)]
@@ -147,36 +165,51 @@ def build(C):
     TE(lambda g, T: group(g, keys(T) + [(T.P_a0[:, PK0 + o:PK0 + W4:4], T.IM1[:], T.SC[:, 3:W4:4]) for o in range(4)]), ["IM1"] + allk("SC"), ["K0"], 64 * 9, 0, "a0")
     V(lambda g, T: g.vector.tensor_scalar(T.E[:], T.P_a0[:, PK0:PK0 + W4], -0.5, None, OP.is_gt), ["K0"], allk("E"), W4, 0, "a0")
     TE(lambda g, T: group(g, [(T.P_a0[:, PK0:PK0 + V4], T.ID[:], T.B4[:])] + [(T.P_a0[:, PK0:PK0 + V4], T[w][:], T.E[:, o:W4:4]) for o, w in ((1, "ID"), (2, "I2"), (3, "I3"))]),
-       ["I2", "I3", "B4"] + allk("E"), ["K0"], 256, 0, "a0")
+       ["I2", "I3"] + allk("B4.") + allk("E"), ["K0"], 256, 0, "a0")
     V(lambda g, T: g.vector.tensor_copy(T.LU[:], T.P_a0[:, PK0:PK0 + V4]), ["K0"], allk("LU"), V4, 0, "a0")
+    S(lambda g, T: g.scalar.activation(lists(T, 0, 0, NCH), T.P_a0[:, PK0:PK0 + V4], AF.Copy), ["K0"], ["LF%d.0" % k for k in range(NCH)], V4, 0, "a0")
     for k in range(NCH):
-        S(lambda g, T, k=k: g.scalar.activation(cursors(T, 0, k, 4 * CN, 4 * CN + NB), T.P_a0[:, PK0 + NB * k:PK0 + NB * (k + 1)], AF.Copy), ["K0"], ["LF%d.0" % k], NB, k, "a0")
-        V(lambda g, T, k=k: g.vector.tensor_copy(cursors(T, 0, k, 0, 4 * CN), X(T, "PGI", k)), ["PGI%d" % k], ["CW%d.0" % k], 256, k)
+        V(lambda g, T, k=k: g.vector.tensor_copy(saved(T, 0, k), X(T, "PGI", k)), ["PGI%d" % k], ["CW%d.0" % k], 256, k)
         S(lambda g, T, k=k: g.scalar.activation(T.LIMP[:, CN * k:CN * (k + 1)], T.LIM[:, CN * k:CN * (k + 1)].indirect(T.LL[:]), AF.Copy),
           ["LIM", "LL"], ["LIMP%d" % k], C["ga"] * CN + 40, k)
     for s in range(NSL):
-        if s < NSL - 1:
-            op("g", ("t", 0, s + 1), ["XB0", "PRE0"] + ["csent%d.%d" % (NCH - 1, s - 1)] * (s > 0), ["tsent%d" % s], None, C["send"])
-            op("hop", "t", ["tsent%d" % s], ["XB%d" % (s + 1), "PRE%d" % (s + 1)], None, 28000, 0, "tl%d" % (s + 1))
-        for k in range(NCH):
-            one_slice(s, k, 0, C, op, V, S, TE, dma, xyc)
-        both = lambda at: ["%s%d.%d" % (b, k, at) for b in ("CW", "LF") for k in range(NCH)]
-        op("g", ("w", 1, s), both(s), ["wsent%d" % s], None, C["send"])
-        op("hop", "w", ["wsent%d" % s], both(s + 1), None, 22000, 1, "wl_1_%d" % s)
-        for k in range(NCH):
-            one_slice(s, k, 1, C, op, V, S, TE, dma, xyc)
+        for team in TEAMS if s < NSL - 1 else TEAMS[:-1] + CREWS[TEAMS[-1][0]:]:
+            for crew in CREWS:
+                if crew[0] in team:
+                    fetch(s, crew, C, V, S)
+                    for k in crew:
+                        steps(s, k, team, crew, C, op, V, S, TE)
+                    if crew[0] == 0:
+                        ahead(s, C, op, V)
+                    leave(s, crew, C, op, V, dma)
+            first = len(ops)
+            values(s, team, C, V, S, TE, dma, xyc[len(team)])
+            if s == NSL - 1:
+                for o in ops[first:]:
+                    o["k"] = LAST
     return ops
 
 
-def one_slice(s, k, rest, C, op, V, S, TE, dma, xyc):
+def ahead(s, C, op, V):
+    if s < NSL - 1:
+        op("g", ("t", 0, s + 1), ["XB0", "PRE0"] + ["csent%d.%d" % (AFTER, s - 1)] * (s > 0), ["tsent%d" % s], None, C["send"])
+        op("hop", "t", ["tsent%d" % s], ["XB%d" % (s + 1), "PRE%d" % (s + 1)], None, 28000, 0, "tl%d" % (s + 1))
+    both = lambda at: ["%s%d.%d" % (b, k, at) for b in ("CW", "LF") for k in range(NCH)]
+    op("g", ("w", 1, s), both(s), ["wsent%d" % s], None, C["send"])
+    op("hop", "w", ["wsent%d" % s], both(s + 1), None, WH, 1, "wl_1_%d" % s)
+    V(lambda g, T: g.vector.tensor_copy(T.LN[:], lists(T, s + 1, 0, NCH)), ["LF%d.%d" % (k, s + 1) for k in range(NCH)], ["LN"], V4, 0)
+
+
+def values(s, team, C, V, S, TE, dma, xyc):
+    k, m = team[0], len(team)
     kt = lambda b: "%s%d" % (b, k)
-    ks = lambda b, at=s: "%s%d.%d" % (b, k, at)
-    lo = CN * k
-    st = ks("HP", s - 1) if s else "VB"
-    h0 = HPW * (s - 1)
+    each = lambda b: ["%s%d" % (b, j) for j in team]
+    nb, nv = NB * m, V4 * m
     ab, lb = "a%d" % k, "l%d" % k
-    GA = C["ga"]
     home = s == NSL - 1
+    pma, pmb = PN + 3 * nb, PN + 4 * nb
+    k0, m0 = [(x[0], len(x)) for x in TEAMS if k in x][0]
+    kept = lambda sl: HPW * (m0 * sl - NSL * (k - k0))
 
     def PS(T, a, b, step=1):
         return T["P_" + ab][:, a:b:step]
@@ -184,82 +217,128 @@ def one_slice(s, k, rest, C, op, V, S, TE, dma, xyc):
     def PL(T, a, b, step=1):
         return T["P_" + lb][:, a:b:step]
 
-    def saved(T, at):
-        return cursors(T, at, k, 0, 4 * CN)
-
-    def listed(T, at):
-        return cursors(T, at, k, 4 * CN, 4 * CN + NB)
+    def Y(T, name, a, b, step=1):
+        return T[name][:, PER[name][0] * k + a:PER[name][0] * k + b:step]
 
     def one(P, T, at, o, by_order):
-        return P(T, at + NB * o, at + NB * (o + 1)) if by_order else P(T, at + o, at + V4, 4)
+        return P(T, at + nb * o, at + nb * (o + 1)) if by_order else P(T, at + o, at + nv, 4)
 
     def laid(P, T, at, w, name, a, by_order):
         if not by_order:
-            return [(P(T, at, at + V4), T[w][:], X(T, name, k, a, a + V4))]
-        return [(one(P, T, at, o, True), T[w][:], X(T, name, k, a + o, a + V4, 4)) for o in range(4)]
+            return [(P(T, at, at + nv), T[w][:], Y(T, name, a, a + nv))]
+        return [(one(P, T, at, o, True), T[w][:], Y(T, name, a + o, a + nv, 4)) for o in range(4)]
 
-    def old(P, T, at, w, by_order=False):
-        if s == 0:
-            return [(one(P, T, at, o, by_order), T[w][:], T.VB[:, V4 * o + NB * k:V4 * o + NB * (k + 1)]) for o in range(4)]
-        return laid(P, T, at, w, "HP", h0, by_order) + laid(P, T, at, w, "HP", h0 + V4, by_order)
+    def parts(P, T, at, w, sl, by_order=False):
+        if sl < 0:
+            return [(one(P, T, at, o, by_order), T[w][:], T.VB[:, V4 * o + NB * k:V4 * o + NB * k + nb]) for o in range(4)]
+        a = kept(sl) + V4 * (k - k0)
+        return laid(P, T, at, w, "HP", a, by_order) + laid(P, T, at, w, "HP", a + V4 * m0, by_order)
 
-    if s and not rest:
-        TE(lambda g, T: group(g, [(PS(T, PK1, PK1 + V4), T.ID[:], T.KO[:, 0:V4])] + old(PS, T, PK1, "I4")), ["ID", "I4", "KO", st], [kt("K1")], 64 * 3, k, ab)
-        V(lambda g, T: g.vector.tensor_tensor_scan(X(T, "SC", k), T.RST[:, 0:V4], PS(T, PK1, PK1 + V4), 0.0, OP.add, OP.max), [kt("K1"), "RST"], [kt("SC")], V4, k, ab)
-        TE(lambda g, T: group(g, [(PS(T, PK1, PK1 + V4), T.ID[:], T.KO[:, 0:V4])] + old(PS, T, PK1, "I4")
-                              + [(one(PS, T, PK1, o, False), T.IM1[:], X(T, "SC", k, 3, None, 4)) for o in range(4)]),
-           ["IM1", kt("SC"), st], [kt("K1")], 64 * 7, k, ab)
-        if ON["E"] == "s":
-            S(lambda g, T: g.scalar.activation(X(T, "E", k), PS(T, PK1, PK1 + V4), AF.Relu, bias=1.0), [kt("K1")], [kt("E")], V4, k, ab)
+    def small(name, out, in_, func, bias, scale, alu, c, r, w, n, bank):
+        if ON[name] == "s":
+            S(lambda g, T: g.scalar.activation(out(T), in_(T), func, bias=bias, scale=scale), r, w, n, k, bank)
         else:
-            V(lambda g, T: g.vector.tensor_scalar(X(T, "E", k), PS(T, PK1, PK1 + V4), -0.5, None, OP.is_gt), [kt("K1")], [kt("E")], V4, k, ab)
-        TE(lambda g, T: group(g, [(PS(T, PLU, PLU + NB), T.ID[:], T.B4[:, 0:NB])]
-                              + [(PS(T, PLU, PLU + NB), T[w][:], X(T, "E", k, o, None, 4)) for o, w in ((1, "ID"), (2, "I2"), (3, "I3"))]),
-           ["ID", "I2", "I3", "B4", kt("E")], [kt("PLU")], 256, k, ab)
-        V(lambda g, T: g.vector.tensor_copy(X(T, "LU", k), PS(T, PLU, PLU + NB)), [kt("PLU")], [kt("LU")], NB, k, ab)
-        if ON["LF"] == "s":
-            S(lambda g, T: g.scalar.activation(listed(T, s), PS(T, PLU, PLU + NB), AF.Copy), [kt("PLU")], [ks("LF")], NB, k, ab)
-        else:
-            V(lambda g, T: g.vector.tensor_copy(listed(T, s), PS(T, PLU, PLU + NB)), [kt("PLU")], [ks("LF")], NB, k, ab)
-    if not rest:
+            V(lambda g, T: g.vector.tensor_scalar(out(T), in_(T), c, None, alu), r, w, n, k, bank)
+
+    st, hp = ("HP%d.%d" % (k0, s - 1) if s else "VB"), "HP%d.%d" % (k, s)
+    g0, mt = kept(s) + HPW * (k - k0), kept(s - 1) + 2 * V4 * m0 + NB * (k - k0)
+    TE(lambda g, T: group(g, [(PS(T, PN, PN + 3 * nb), T.WB[:, 15 - a:143 - a], Y(T, "NS", a, NST * CN * m, 16)) for a in range(16)]),
+       ["NS%d.%d" % (j, t) for j in team for t in range(NST)] + ["WB"], [kt("PN")], 1024, k, ab)
+    small("FM", lambda T: Y(T, "FM", 0, 3 * nb), lambda T: PS(T, PN, PN + 3 * nb), AF.Relu, -15.0, -1.0, OP.is_lt, -15.0, [kt("PN")], [kt("FM")], 3 * nb, ab)
+
+    def msum(g, T):
+        for at, w in ((pma, "RH"), (pmb, "R1")):
+            last = group(g, [(PS(T, at, at + nb), T[w][:], Y(T, "FM", t * nb, (t + 1) * nb)) for t in range(NST)])
+        return last
+    TE(msum, [kt("FM"), "RH", "R1"], [kt("PM")], 384, k, ab)
+    small("RR", lambda T: Y(T, "RR", 0, 3 * nb), lambda T: PS(T, PN + 2 * nb, PN + 5 * nb), AF.Identity, 191.75, 1.0, OP.add, 191.75, [kt("PN"), kt("PM")], [kt("RR")], 3 * nb, ab)
+
+    def early(g, T):
+        terms = [(PL(T, 0, 9 * nb), T.ID[:], T["XY%d" % m][:])]
+        terms += laid(PL, T, 0, "IM64", "E", 0, home) + laid(PL, T, nv, "I64", "E", 0, home) + parts(PL, T, 0, "ID", s - 1, home)
+        if s:
+            terms += [(PL(T, 2 * nv, 9 * nb), T.ID[:], Y(T, "HP", mt, mt + nb))]
+        return group(g, terms, True, False)
+    TE(early, xyc + ["ID", "IM64", "I64", st] + each("E"), [kt("PL")], 64 * (18 if home else 6 + (s == 0)), k, lb)
+    TE(lambda g, T: group(g, [(PL(T, 2 * nv, 9 * nb), T.ID[:], Y(T, "FM", t * nb, (t + 1) * nb)) for t in range(NST)], False, False), ["ID", kt("FM"), kt("PM")], [kt("PL")], 192, k, lb)
+
+    def late(g, T):
+        terms = []
+        for o in range(4):
+            x, y = one(PL, T, 0, o, home), one(PL, T, nv, o, home)
+            terms += [(y, T.IMH[:], Y(T, "RR", 0, nb)), (x, T.IM2[:], Y(T, "RR", nb, 2 * nb)), (x, T.ID[:], Y(T, "RR", 2 * nb, 3 * nb))]
+        return group(g, terms, False, True)
+    TE(late, ["ID", "IMH", "IM2", kt("RR")], [kt("PL")], 768, k, lb)
+    small("HP", lambda T: Y(T, "HP", g0, g0 + 9 * nb), lambda T: PL(T, 0, 9 * nb), AF.Relu, 0.0, 1.0, OP.max, 0.0, [kt("PL")], [hp], 9 * nb, lb)
+    if home:
+        V(lambda g, T: g.vector.tensor_tensor(Y(T, "YV", 0, nv), Y(T, "HP", g0, g0 + nv), Y(T, "HP", g0 + nv, g0 + 2 * nv), OP.add), [hp], [kt("YV")], 2 * nv, k)
+        S(lambda g, T: g.scalar.activation(Y(T, "YM", 0, nb), Y(T, "HP", g0 + 2 * nv, g0 + 9 * nb), AF.Copy), [hp], [kt("YM")], nb, k)
+        for j in team:
+            for o in range(4):
+                dma("qs", lambda T, o=o, j=j: T.yv[o::4, CN * j:CN * (j + 1)], lambda T, o=o, j=j: Y(T, "YV", nb * o + NB * (j - k), nb * o + NB * (j - k + 1)), [kt("YV")], [], 2000, j)
+            dma("qs", lambda T, j=j: T.ym[:, CN * j:CN * (j + 1)], lambda T, j=j: X(T, "YM", j), [kt("YM")], [], 2000, j)
         return
-    if s == 0:
-        V(lambda g, T: g.vector.tensor_copy(X(T, "CF", k, 0, CN), X(T, "PGI", k).indirect(X(T, "LU", k))), [kt("PGI"), kt("LU")], [kt("C32")], GA * CN + 45, k)
-    elif ON["C32"] == "s":
-        S(lambda g, T: g.scalar.activation(X(T, "CF", k, 0, CN), saved(T, s).indirect(X(T, "LU", k)), AF.Copy), [ks("CW"), kt("LU")], [kt("C32")], GA * CN + 40, k)
-    else:
-        V(lambda g, T: g.vector.tensor_copy(X(T, "CF", k, 0, CN), saved(T, s).indirect(X(T, "LU", k))), [ks("CW"), kt("LU")], [kt("C32")], GA * CN + 45, k)
-    p0 = TBW * s + TW + 4 * lo
-    V(lambda g, T: g.vector.tensor_tensor(X(T, "CF", k, CN, 2 * CN), T.TB[:, p0:p0 + 4 * CN].indirect(X(T, "LU", k)), T.POS[:], OP.add),
-      ["PRE%d" % s, kt("LU"), "POS"], [kt("PF")], GA * CN + 45, k)
-    if s == 0:
-        V(lambda g, T: g.vector.tensor_copy(X(T, "OF", k, 0, CN), X(T, "CF", k, 0, CN)), [kt("C32")], [kt("OFF")], CN, k)
-        V(lambda g, T: g.vector.tensor_copy(X(T, "OF", k, CN, 2 * CN), X(T, "CF", k, CN, 2 * CN)), [kt("PF")], [kt("PO")], CN, k)
-    else:
-        V(lambda g, T: g.vector.tensor_copy(X(T, "OF", k), X(T, "CF", k)), [kt("C32"), kt("PF")], [kt("OFF"), kt("PO")], 2 * CN, k)
+    keys = lambda T: [(PS(T, PK1, PK1 + nv), T.ID[:], T.KO[:, 0:nv])] + parts(PS, T, PK1, "I4", s)
+    TE(lambda g, T: group(g, keys(T)), ["ID", "I4", "KO", hp], [kt("K1")], 64 * 3, k, ab)
+    V(lambda g, T: g.vector.tensor_tensor_scan(Y(T, "SC", 0, nv), T.RST[:, 0:nv], PS(T, PK1, PK1 + nv), 0.0, OP.add, OP.max), [kt("K1"), "RST"], each("SC"), nv, k, ab)
+    TE(lambda g, T: group(g, keys(T) + [(one(PS, T, PK1, o, False), T.IM1[:], Y(T, "SC", 3, nv, 4)) for o in range(4)]), ["IM1", hp] + each("SC"), [kt("K1")], 64 * 7, k, ab)
+    small("E", lambda T: Y(T, "E", 0, nv), lambda T: PS(T, PK1, PK1 + nv), AF.Relu, 1.0, 1.0, OP.is_gt, -0.5, [kt("K1")], each("E"), nv, ab)
+    TE(lambda g, T: group(g, [(PS(T, PLU, PLU + nb), T.ID[:], T.B4[:, NB * k:NB * k + nb])] + [(PS(T, PLU, PLU + nb), T[w][:], Y(T, "E", o, nv, 4)) for o, w in ((1, "ID"), (2, "I2"), (3, "I3"))]),
+       ["ID", "I2", "I3"] + each("B4.") + each("E"), [kt("PLU")], 256, k, ab)
+    V(lambda g, T: g.vector.tensor_copy(Y(T, "LU", 0, nb), PS(T, PLU, PLU + nb)), [kt("PLU")], each("LU"), nb, k, ab)
+    small("LF", lambda T: lists(T, s + 1, k, m), lambda T: PS(T, PLU, PLU + nb), AF.Identity, 0.0, 1.0, OP.add, 0.0, [kt("PLU")], ["LF%d.%d" % (j, s + 1) for j in team], nb, ab)
+
+
+def steps(s, k, team, crew, C, op, V, S, TE):
+    kt = lambda b: "%s%d" % (b, k)
+    ks = lambda b, at=s: "%s%d.%d" % (b, k, at)
+    lo = CN * k
+    ab, lb = "a%d" % k, "l%d" % k
+    GA = C["ga"]
+
+    def PS(T, a, b, step=1):
+        return T["P_" + ab][:, a:b:step]
+
+    def PL(T, a, b, step=1):
+        return T["P_" + lb][:, a:b:step]
+
+    def signs(T, t):
+        at = NST * CN * team[0] + CN * (len(team) * t + k - team[0])
+        return T.NS[:, at:at + CN]
+
+    def mine(T, name, half, a=0, b=CN):
+        at = 2 * CN * crew[0] + CN * (len(crew) * half + k - crew[0])
+        return T[name][:, at + a:at + b]
 
     def lrep(g, T):
         for e in range(REP):
             last = g.tensor.matmul(PL(T, e, REP * CN, REP), T.ID[:], T.LIMP[:, lo:lo + CN], True, True)
         return last
-    TE(lrep, [kt("LIMP"), "ID"], [kt("PL")], REP * CN, k, lb)
+    if s == 0 or k in [x[0] for x in TEAMS]:
+        TE(lrep, [kt("LIMP"), "ID"], [kt("PL")], REP * CN, k, lb)
 
     for t in range(NST):
         if t == 0:
-            cur, keep, tags, five, mm5 = (lambda T: X(T, "CF", k, 0, CN)), (lambda T: X(T, "CF", k, 0, CN)), ("C32", "C32"), "I5F", 4 * CN
+            cur, keep, tags, five, mm5 = (lambda T: mine(T, "CF", 0)), (lambda T: mine(T, "CF", 0)), ("C32", "C32"), "I5F", 4 * CN
         else:
             cur, keep, tags, five, mm5 = (lambda T: X(T, "C16", k)), (lambda T: X(T, "CI", k)), ("C16", "CI"), "I5H", CN
         for u in range(SUB):
             f0, f1, y0, y1 = 16 * HW * u, 16 * HW * (u + 1), HW * u, HW * (u + 1)
             fu, gu = "F%d.%d" % (k, u), "G%d.%d" % (k, u)
-            S(lambda g, T, y0=y0, y1=y1, f0=f0, f1=f1: g.scalar.activation(X(T, "F", k, f0, f1), T.TB[:, TBW * s:TBW * s + TW].indirect(X(T, "OF", k, y0, y1)), AF.Copy),
+            S(lambda g, T, y0=y0, y1=y1, f0=f0, f1=f1: g.scalar.activation(X(T, "F", k, f0, f1), T.TB[:, TBW * s:TBW * s + TW].indirect(mine(T, "OF", 0, y0, y1)), AF.Copy),
               ["XB%d" % s, kt("OFF")], [fu], GA * 16 * HW + 40, k)
-            op("g", lambda g, T, f0=f0, f1=f1: g.affine_select(X(T, "F2", k, f0, f1), X(T, "F", k, f0, f1), [[0, 16 * HW]], OP.is_ge, 0.0, 0, 0), [fu], [gu], None, 200 + 32 * HW, k)
+            who = copier(s, k, t, u)
+            if who == "g":
+                op("g", lambda g, T, f0=f0, f1=f1: g.affine_select(X(T, "F2", k, f0, f1), X(T, "F", k, f0, f1), [[0, 16 * HW]], OP.is_ge, 0.0, 0, 0), [fu], [gu], None, 200 + 32 * HW, k)
+            elif who == "v":
+                V(lambda g, T, f0=f0, f1=f1: g.vector.tensor_copy(X(T, "F2", k, f0, f1), X(T, "F", k, f0, f1)), [fu], [gu], 8 * HW, k)
+            else:
+                S(lambda g, T, f0=f0, f1=f1: g.scalar.activation(X(T, "F2", k, f0, f1), X(T, "F", k, f0, f1), AF.Copy), [fu], [gu], 16 * HW, k)
         dts = ["D%d.%d" % (k, u) for u in range(SUB)]
         for u in range(SUB):
             f0, f1, y0, y1 = 16 * HW * u, 16 * HW * (u + 1), HW * u, HW * (u + 1)
             fu, gu, du = "F%d.%d" % (k, u), "G%d.%d" % (k, u), dts[u]
-            V(lambda g, T, y0=y0, y1=y1, f0=f0, f1=f1: g.vector.tensor_tensor(X(T, "D", k, f0, f1), X(T, "F", k, f0, f1).indirect(X(T, "OF", k, CN + y0, CN + y1)), X(T, "F2", k, f0, f1), OP.subtract),
+            V(lambda g, T, y0=y0, y1=y1, f0=f0, f1=f1: g.vector.tensor_tensor(X(T, "D", k, f0, f1), X(T, "F", k, f0, f1).indirect(mine(T, "OF", 1, y0, y1)), X(T, "F2", k, f0, f1), OP.subtract),
               [fu, gu, kt("PO")], [du], GA * 16 * HW + 45, k)
             S(lambda g, T, f0=f0, f1=f1: g.scalar.activation(X(T, "D", k, f0, f1), X(T, "D", k, f0, f1), AF.Abs), [du], [du], 16 * HW, k)
             for q in range(NQ):
@@ -273,67 +352,50 @@ def one_slice(s, k, rest, C, op, V, S, TE, dma, xyc):
             TE(lambda g, T, q=q: group(g, asum(T, "WK", "C", range(q, 16, NQ)), False, q == NQ - 1),
                ["C%d.%d.%d" % (k, u, q) for u in range(SUB)] + ["WK"], [kt("PA")], REP * CN, k, ab)
         ns = "NS%d.%d" % (k, t)
-        S(lambda g, T, t=t: g.scalar.activation(X(T, "NS", k, CN * t, CN * (t + 1)), PS(T, PA, PA + CN), AF.Sign, bias=-8.0 * BIG), [kt("PA")], [ns], CN, k, ab)
+        S(lambda g, T, t=t: g.scalar.activation(signs(T, t), PS(T, PA, PA + CN), AF.Sign, bias=-8.0 * BIG), [kt("PA")], [ns], CN, k, ab)
         S(lambda g, T: g.scalar.activation(X(T, "RL", k), PS(T, PA, PA + CN), AF.Relu, bias=-8.0 * BIG), [kt("PA")], [kt("RL")], CN, k, ab)
         TE(lambda g, T, t=t, cur=cur, five=five: group(g, [(PS(T, PB, PB + CN), T.CST[:], T.ONES[:, 0:CN]), (PS(T, PB, PB + CN), T[five][:], cur(T)),
-                                                           (PS(T, PB, PB + CN), T.WS[:], X(T, "NS", k, CN * t, CN * (t + 1))), (PS(T, PB, PB + CN), T.IDF[:], X(T, "RL", k))]),
+                                                           (PS(T, PB, PB + CN), T.WS[:], signs(T, t)), (PS(T, PB, PB + CN), T.IDF[:], X(T, "RL", k))]),
            [ns, kt("RL"), "WS", "IDF", "CST", "ONES", five, kt(tags[0])], [kt("PB")], 6 * CN + mm5, k, ab)
         V(lambda g, T, keep=keep: g.vector.tensor_tensor(X(T, "O2", k), PS(T, PB, PB + CN), keep(T), OP.max), [kt("PB"), kt(tags[1])], [kt("O2")], CN, k, ab)
         if t < NST - 1:
             V(lambda g, T: g.vector.tensor_scalar(X(T, "CI", k), X(T, "O2", k), 2047, None, OP.bitwise_and), [kt("O2")], [kt("CI")], CN, k)
-            V(lambda g, T: g.vector.tensor_copy(X(T, "OF", k, 0, CN), X(T, "CI", k)), [kt("CI")], [kt("OFF")], CN, k)
+            V(lambda g, T: g.vector.tensor_copy(mine(T, "OF", 0), X(T, "CI", k)), [kt("CI")], [kt("OFF")], CN, k)
             V(lambda g, T: g.vector.tensor_copy(X(T, "C16", k), X(T, "CI", k)), [kt("CI")], [kt("C16")], CN, k)
-    V(lambda g, T: g.vector.tensor_scalar(message(T, "c", k, s, 0), X(T, "O2", k), 2047, None, OP.bitwise_and), [kt("O2")], [ks("CO")], CN, k)
+
+
+def fetch(s, team, C, V, S):
+    k, m = team[0], len(team)
+    each = lambda b: ["%s%d" % (b, j) for j in team]
+    n, p0 = CN * m, TBW * s + TW + 4 * CN * k
+    lu = lambda T: T.LU[:, NB * k:NB * (k + m)]
+    half = lambda T, name, a, b: T[name][:, 2 * CN * k + n * a:2 * CN * k + n * b]
+    if s == 0:
+        V(lambda g, T: g.vector.tensor_copy(half(T, "CF", 0, 1), T.PGI[:, 4 * CN * k:4 * CN * (k + m)].indirect(lu(T))), each("PGI") + each("LU"), each("C32"), C["ga"] * n + 45, k)
+    else:
+        S(lambda g, T: g.scalar.activation(half(T, "CF", 0, 1), saved(T, s, k, m).indirect(lu(T)), AF.Copy), ["CW%d.%d" % (j, s) for j in team] + each("LU"), each("C32"), C["ga"] * n + 40, k)
+    V(lambda g, T: g.vector.tensor_tensor(half(T, "CF", 1, 2), T.TB[:, p0:p0 + 4 * n].indirect(lu(T)), T.POS[:, 0:n], OP.add), ["PRE%d" % s, "POS"] + each("LU"), each("PF"), C["ga"] * n + 45, k)
+    if s and k in DIRECT:
+        V(lambda g, T: g.vector.tensor_copy(half(T, "OF", 0, 1), saved(T, s, k, m).indirect(lu(T))), ["CW%d.%d" % (j, s) for j in team] + each("LU"), each("OFF"), C["ga"] * n + 45, k)
+        V(lambda g, T: g.vector.tensor_copy(half(T, "OF", 1, 2), half(T, "CF", 1, 2)), each("PF"), each("PO"), n, k)
+    elif s == 0 or m > 1:
+        V(lambda g, T: g.vector.tensor_copy(half(T, "OF", 0, 1), half(T, "CF", 0, 1)), each("C32"), each("OFF"), n, k)
+        V(lambda g, T: g.vector.tensor_copy(half(T, "OF", 1, 2), half(T, "CF", 1, 2)), each("PF"), each("PO"), n, k)
+    else:
+        V(lambda g, T: g.vector.tensor_copy(half(T, "OF", 0, 2), half(T, "CF", 0, 2)), each("C32") + each("PF"), each("OFF") + each("PO"), 2 * n, k)
+
+
+def leave(s, team, C, op, V, dma):
+    k, m = team[0], len(team)
+    ks = lambda b: "%s%d.%d" % (b, k, s)
+    nxt = ["CW%d.%d" % (j, s + 1) for j in team]
+    V(lambda g, T: g.vector.tensor_scalar(message(T, "c", k, s, 0), T.O2[:, CN * k:CN * (k + m)], 2047, None, OP.bitwise_and), ["O2%d" % j for j in team], [ks("CO")], CN * m, k)
     op("g", ("c", k, s), [ks("CO")], [ks("csent")], None, C["send"], k)
     op("hop", "c", [ks("csent")], [ks("CL")], None, C["hop"], k, "cl_%d_%d" % (k, s))
-    V(lambda g, T: g.vector.tensor_copy(X(T, "LN", k), listed(T, s + 1)), [ks("LF", s + 1)], [kt("LN")], NB, k)
-    V(lambda g, T: g.vector.tensor_copy(saved(T, s + 1).indirect(X(T, "LN", k)), message(T, "c", k, s, 1)), [ks("CL"), kt("LN")], [ks("CW", s + 1)], C["sc"] * CN + 45, k)
-
-    TE(lambda g, T: group(g, [(PS(T, PN, PN + 3 * NB), T.WB[:, 15 - a:143 - a], X(T, "NS", k, a, None, 16)) for a in range(16)]),
-       ["NS%d.%d" % (k, t) for t in range(NST)] + ["WB"], [kt("PN")], 1024, k, ab)
-    if ON["FM"] == "s":
-        S(lambda g, T: g.scalar.activation(X(T, "FM", k, 0, 3 * NB), PS(T, PN, PN + 3 * NB), AF.Relu, bias=-15.0, scale=-1.0), [kt("PN")], [kt("FM")], 3 * NB, k, ab)
-    else:
-        V(lambda g, T: g.vector.tensor_scalar(X(T, "FM", k, 0, 3 * NB), PS(T, PN, PN + 3 * NB), -15.0, None, OP.is_lt), [kt("PN")], [kt("FM")], 3 * NB, k, ab)
-
-    def msum(g, T):
-        for at, w in ((PMA, "RH"), (PMB, "R1")):
-            last = group(g, [(PS(T, at, at + NB), T[w][:], X(T, "FM", k, t * NB, (t + 1) * NB)) for t in range(NST)])
-        return last
-    TE(msum, [kt("FM"), "RH", "R1"], [kt("PM")], 384, k, ab)
-    if ON["RR"] == "s":
-        S(lambda g, T: g.scalar.activation(X(T, "RR", k, 0, 3 * NB), PS(T, PN + 2 * NB, PN + 5 * NB), AF.Identity, bias=191.75), [kt("PN"), kt("PM")], [kt("RR")], 3 * NB, k, ab)
-    else:
-        V(lambda g, T: g.vector.tensor_scalar(X(T, "RR", k, 0, 3 * NB), PS(T, PN + 2 * NB, PN + 5 * NB), 191.75, None, OP.add), [kt("PN"), kt("PM")], [kt("RR")], 3 * NB, k, ab)
-
-    def early(g, T):
-        terms = [(PL(T, 0, 9 * NB), T.ID[:], T.XYC[:, 0:9 * NB])]
-        terms += laid(PL, T, 0, "IM64", "E", 0, home) + laid(PL, T, V4, "I64", "E", 0, home) + old(PL, T, 0, "ID", home)
-        if s:
-            terms += [(PL(T, 2 * V4, 9 * NB), T.ID[:], X(T, "HP", k, h0 + 2 * V4, h0 + 9 * NB))]
-        return group(g, terms, True, False)
-    TE(early, xyc + ["ID", "IM64", "I64", kt("E"), st], [kt("PL")], 64 * (18 if home else 6 + (s == 0)), k, lb)
-    TE(lambda g, T: group(g, [(PL(T, 2 * V4, 9 * NB), T.ID[:], X(T, "FM", k, t * NB, (t + 1) * NB)) for t in range(NST)], False, False), ["ID", kt("FM"), kt("PM")], [kt("PL")], 192, k, lb)
-
-    def late(g, T):
-        terms = []
-        for o in range(4):
-            x, y = one(PL, T, 0, o, home), one(PL, T, V4, o, home)
-            terms += [(y, T.IMH[:], X(T, "RR", k, 0, NB)), (x, T.IM2[:], X(T, "RR", k, NB, 2 * NB)), (x, T.ID[:], X(T, "RR", k, 2 * NB, 3 * NB))]
-        return group(g, terms, False, True)
-    TE(late, ["ID", "IMH", "IM2", kt("RR")], [kt("PL")], 768, k, lb)
-    hp, g0 = ks("HP"), HPW * s
-    if ON["HP"] == "s":
-        S(lambda g, T: g.scalar.activation(X(T, "HP", k, g0, g0 + 9 * NB), PL(T, 0, 9 * NB), AF.Relu), [kt("PL")], [hp], 9 * NB, k, lb)
-    else:
-        V(lambda g, T: g.vector.tensor_scalar(X(T, "HP", k, g0, g0 + 9 * NB), PL(T, 0, 9 * NB), 0.0, None, OP.max), [kt("PL")], [hp], 9 * NB, k, lb)
-    if home:
-        dma("qa" if k == NCH - 1 else "qs", lambda T: T.yg[:, 4 * lo:4 * (lo + CN)], lambda T: saved(T, NSL), [ks("CW", NSL)], [], 2500, k, 500)
-        V(lambda g, T: g.vector.tensor_tensor(X(T, "YV", k), X(T, "HP", k, g0, g0 + V4), X(T, "HP", k, g0 + V4, g0 + 2 * V4), OP.add), [hp], [kt("YV")], 32, k)
-        S(lambda g, T: g.scalar.activation(X(T, "YM", k), X(T, "HP", k, g0 + 2 * V4, g0 + 2 * V4 + NB), AF.Copy), [hp], [kt("YM")], NB, k)
-        for o in range(4):
-            dma("qs", lambda T, o=o: T.yv[o::4, lo:lo + CN], lambda T, o=o: X(T, "YV", k, NB * o, NB * (o + 1)), [kt("YV")], [], 2000, k)
-        dma("qs", lambda T: T.ym[:, lo:lo + CN], lambda T: X(T, "YM", k), [kt("YM")], [], 2000, k)
+    V(lambda g, T: g.vector.tensor_copy(saved(T, s + 1, k, m).indirect(T.LN[:, NB * k:NB * (k + m)]), message(T, "c", k, s, 1)), [ks("CL"), "LN"], nxt, C["sc"] * CN * m + 45, k)
+    if s == NSL - 1:
+        for j in team:
+            dma("qa" if j == NCH - 1 else "qs", lambda T, j=j: T.yg[:, 4 * CN * j:4 * CN * (j + 1)], lambda T, j=j: saved(T, NSL, j), nxt, [], 2500, j, 500)
 
 
 def depend(ops):
@@ -369,7 +431,7 @@ def plan(ops, deps, C):
     x, prio = SEED, []
     for i, o in enumerate(ops):
         x = (x * 1103515245 + 12345) % 2 ** 31
-        prio.append(1e9 - i if o["q"] in ("qs", "qa") and not o["r"] else tail[i] - LAG * o["k"] + AMP * x / 2 ** 31)
+        prio.append(1e9 - i if o["q"] in ("qs", "qa") and not o["r"] else tail[i] - LAG * o["k"] - GAP * (o["k"] // 2) + AMP * x / 2 ** 31)
     left = [len(d) for d in deps]
     ready_at, fin = [0.0] * n, [0.0] * n
     free, bankfree, bankq = {}, {}, {}

from concourse.mybir import AluOpType, ActivationFunctionType

OP, AF = AluOpType, ActivationFunctionType
NCH, CN, NB = 4, 64, 4
SUB = 2
HW = CN // SUB
REP = 8
NQ = 16 // REP
NSL, NST = 4, 3
BIG = 2 ** 14
V4 = 4 * NB
HPW = 40
CWW = (4 * CN + NB) * NCH
TEAMS = ((0, 1), (2, 3))
CREWS = ((0,), (1,), (2,), (3,))
TW, TBW = 2048, 3072

PER = {"PGI": (256, "int32"), "SC": (16, "bfloat16"), "E": (16, "bfloat16"), "LU": (4, "uint16"), "LN": (4, "uint16"),
       "CF": (128, "float32"), "C16": (64, "float16"), "OF": (128, "uint16"),
       "RL": (64, "float32"), "O2": (64, "int32"), "CI": (64, "int32"), "CO": (64 * NSL, "int32"), "CL": (64 * NSL, "int32"),
       "NS": (192, "bfloat16"), "FM": (16, "bfloat16"), "RR": (16, "bfloat16"),
       "YV": (16, "float32"), "YM": (4, "float32"), "F": (1024, "bfloat16"), "F2": (1024, "bfloat16"), "D": (1024, "bfloat16"),
       "C": (1024, "bfloat16"), "HP": (HPW * NSL, "bfloat16")}
ONE = {"TB": (TBW * NSL, "bfloat16"), "LIM": (256, "bfloat16"), "LIMP": (256, "bfloat16"),
       "ONES": (128, "bfloat16"), "BO": (128, "bfloat16"), "BO0": (128, "bfloat16"), "ID": (128, "bfloat16"), "WB": (144, "bfloat16"), "WK": (144, "bfloat16"),
       "RI": (128, "int32"), "RH": (128, "bfloat16"), "R1": (128, "bfloat16"), "NBO": (128, "bfloat16"), "CST": (128, "bfloat16"),
       "WS": (128, "bfloat16"), "I8K": (128, "bfloat16"), "IDF": (128, "float32"),
       "I2": (128, "bfloat16"), "I3": (128, "bfloat16"), "I4": (128, "bfloat16"), "IM1": (128, "bfloat16"), "IM2": (128, "bfloat16"), "IMH": (128, "bfloat16"),
       "I64": (128, "bfloat16"), "IM64": (128, "bfloat16"), "I5H": (128, "float16"), "I5F": (128, "float32"),
       "POS": (128, "bfloat16"), "BI": (4, "int32"), "BL": (4, "int32"), "B4": (16, "bfloat16"), "LL": (4, "uint16"),
       "KO": (64, "bfloat16"), "RST": (64, "bfloat16"), "VI": (64, "int32"), "VB": (64, "bfloat16"), "CW": (CWW * (NSL + 1), "float32")}
for _m in set(len(_t) for _t in TEAMS + CREWS):
    ONE["XY%d" % _m] = (9 * NB * _m, "bfloat16")
SCRATCH = {}
for _n in PER:
    SCRATCH[_n] = ("sbuf", [128, PER[_n][0] * NCH], PER[_n][1])
for _n in ONE:
    SCRATCH[_n] = ("sbuf", [128, ONE[_n][0]], ONE[_n][1])
for _k in range(NCH):
    SCRATCH["P_a%d" % _k] = ("psum", [128, 512], "float32")
    SCRATCH["P_l%d" % _k] = ("psum", [128, 512], "float32")
SEMAPHORES = ["v", "s", "t", "gc", "loc"] + ["%s%d" % (_b, _s) for _b in ("tr", "tl") for _s in range(1, NSL)]
SEMAPHORES += ["%s_%d_%d" % (_b, _k, _s) for _b in ("cr", "cl") for _k in range(NCH) for _s in range(NSL)]
SEMAPHORES += ["%s_1_%d" % (_b, _s) for _b in ("wr", "wl") for _s in range(NSL)]
PA, PB, PK1, PLU, PN, PK0 = 0, 64, 128, 192, 208, 320


def group(g, terms, first=True, final=True):
    for n, (out, w, x) in enumerate(terms):
        last = g.tensor.matmul(out, w, x, first and n == 0, final and n == len(terms) - 1)
    return last


def X(T, name, k, a=0, b=None, step=1):
    w = PER[name][0]
    return T[name][:, w * k + a:w * k + (w if b is None else b):step]


def saved(T, s, k, m=1):
    return T.CW[:, CWW * s + 4 * CN * k:CWW * s + 4 * CN * (k + m)]


def lists(T, s, k, m):
    return T.CW[:, CWW * s + 4 * CN * NCH + NB * k:CWW * s + 4 * CN * NCH + NB * (k + m)]


def message(T, kind, k, s, landed):
    if kind == "w":
        return T.CW[:, CWW * (s + landed):CWW * (s + landed + 1)]
    m = [len(crew) for crew in CREWS if crew[0] == k][0]
    return T["CL" if landed else "CO"][:, CN * (NSL * k + m * s):CN * (NSL * k + m * (s + 1))]


COST = {"ga": 1.25, "sc": 4.0, "tc": 0.4, "hop": 3300.0, "sem": 160.0, "vo": 15.0, "so": 70.0, "pm": 1.0, "send": 600.0}
AMP, SEED = 0.0, 1
DIRECT = (0, 1, 2, 3)
AFTER, WH = 3, 22000
LAST = NCH - 1
SHORT, LAG, GAP = 600, 1500.0, 1000.0
ON = {"E": "v", "FM": "v", "RR": "v", "HP": "v", "C32": "s", "LF": "v"}


def copier(s, k, t, u):
    return "v" if (t, k, u) == (0, 0, 0) else "s" if (t, k, u) == (NST - 1, NCH - 1, SUB - 1) else "g"


def build(C):
    ops = []

    def op(q, fn, r=(), w=(), bank=None, cost=80.0, k=0, sem=None, eng=0.0):
        ops.append({"q": q, "fn": fn, "r": list(r), "w": list(w), "bank": bank, "cost": cost, "k": k, "sem": sem, "eng": eng, "i": len(ops)})

    def V(fn, r, w, n, k=0, bank=None):
        op("v", fn, r, w, bank, max(64, n) + C["vo"], k)

    def S(fn, r, w, n, k=0, bank=None):
        op("s", fn, r, w, bank, max(64, n) * (C["pm"] if bank else 1) + C["so"], k)

    def TE(fn, r, w, n, k=0, bank=None):
        op("t", fn, r, w, bank, n * C["tc"] + 15, k)

    def dma(q, out, in_, r, w, cost=3000.0, k=0, eng=100.0):
        sem = "d%d" % sum(1 for o in ops if o["q"] in ("qs", "qa"))
        if sem not in SEMAPHORES:
            SEMAPHORES.append(sem)
        op(q, (out, in_), r, w, None, cost, k, sem, eng)

    for k in range(NCH):
        for o in range(4):
            dma("qs" if o < 2 else "qa", lambda T, k=k, o=o: T.VI[:, V4 * o + NB * k:V4 * o + NB * (k + 1)], lambda T, o=o, k=k: T.vv[o::4, CN * k:CN * (k + 1)],
                [], ["VI%d.%d" % (k, o)], 2000, k)
    for k in range(NCH):
        dma("qa" if k else "qs", lambda T, k=k: X(T, "PGI", k), lambda T, k=k: T.pg[:, 4 * CN * k:4 * CN * (k + 1)], [], ["PGI%d" % k], 2000, k, 500)
        if k == 0:
            dma("qa", lambda T: T.TB[:, 0:TW], lambda T: T.xt[:], [], ["XB0"], 2000, k, 2000)
            dma("qs", lambda T: T.TB[:, TW:TBW], lambda T: T.pre[:], [], ["PRE0"], 2000, k, 1000)
            dma("qs", lambda T: T.LIM[:], lambda T: T.lim[:], [], ["LIM"], 2000, k, 300)

    def fill(name, a, b, val):
        V(lambda g, T: g.vector.memset(T[name][:, a:b], val), [], ["%s.%d" % (name, a)], 32)
        return "%s.%d" % (name, a)

    def scaled(name, src, f, n=64):
        V(lambda g, T: g.vector.tensor_scalar(T[name][:], T[src][:], float(f), None, OP.mult), [src], [name], n)

    def G(fn, r, w, n):
        op("g", fn, r, w, None, 200 + 2 * n)

    V(lambda g, T: g.vector.memset(T.ONES[:], 1.0), [], ["ONES"], 64)
    G(lambda g, T: g.affine_select(T.ID[:], T.ONES[:], [[-1, 128]], OP.is_equal, 0.0, 0, 1), ["ONES"], ["ID"], 128)
    G(lambda g, T: g.iota(T.KO[:], [[0, NB * NCH], [-1, 4]], 0, 0, allow_small_or_imprecise_dtypes=True), [], ["KO"], 64)
    G(lambda g, T: g.iota(T.BI[:], [[4, NB]], 0, 4 * NB), [], ["BI"], 4)
    G(lambda g, T: g.iota(T.POS[:], [[0, SUB * 2], [16, HW]], 0, 0, allow_small_or_imprecise_dtypes=True), [], ["POS"], 128)
    G(lambda g, T: g.affine_select(T.BO0[:], T.ONES[:], [[-16, 8], [0, 16]], OP.is_ge, 0.0, 0, 1), ["ONES"], ["BO0"], 128)
    G(lambda g, T: g.affine_select(T.BO[:], T.BO0[:], [[16, 8], [0, 16]], OP.is_ge, 0.0, 15, -1), ["BO0"], ["BO"], 128)
    G(lambda g, T: g.iota(T.RI[:], [[1, 128]], 0, -1), [], ["RI"], 128)
    V(lambda g, T: g.vector.memset(T.RST[:], 0.0), [], ["RST"], 16)
    V(lambda g, T: g.vector.memset(T.RST[:, 0:V4 * NCH:4], -1024.0), [], ["RST"], 16)
    V(lambda g, T: g.vector.tensor_scalar(T.BI[:], T.BI[:], 4 * CN - 1, None, OP.bitwise_and), ["BI"], ["BI"], 4)
    for team in CREWS:
        for k in team:
            V(lambda g, T, k=k, at=4 * CN * (k - team[0]): g.vector.tensor_scalar(T.B4[:, NB * k:NB * (k + 1)], T.BI[:, 0:NB], at, None, OP.add), ["BI"], ["B4.%d" % k], 4)
    V(lambda g, T: g.vector.tensor_scalar(T.BL[:], T.BI[:, 0:NB], 2, None, OP.logical_shift_right), ["BI"], ["BL"], 4)
    V(lambda g, T: g.vector.tensor_copy(T.LL[:], T.BL[:]), ["BL"], ["LL"], 4)
    for name, f in (("I4", 4), ("IM1", -1), ("I2", 2), ("I3", 3), ("I5F", 5), ("I5H", 5), ("IM2", -2), ("IMH", -0.5), ("I64", 64), ("IM64", -64), ("I8K", 8 * BIG), ("IDF", 1)):
        scaled(name, "ID", f, 128 if name[-1] == "F" else 64)
    V(lambda g, T: g.vector.memset(T.WB[:], 0.0), [], ["WB"], 72)
    V(lambda g, T: g.vector.tensor_copy(T.WB[:, 15:143:16], T.BO[:, 0:128:16]), ["BO"], ["WB"], 8)
    scaled("WK", "WB", BIG, 72)
    scaled("NBO", "BO", -(BIG // 2))
    V(lambda g, T: g.vector.tensor_scalar(T.RI[:], T.RI[:], 15, None, OP.bitwise_and), ["RI"], ["RI"], 128)
    V(lambda g, T: g.vector.tensor_scalar(T.RH[:], T.RI[:], 0, 0.5, OP.is_equal, OP.mult), ["RI"], ["RH"], 128)
    scaled("R1", "RH", 2)
    scaled("CST", "ONES", 1.0 / 128)
    V(lambda g, T: g.vector.tensor_tensor(T.WS[:], T.NBO[:], T.I8K[:], OP.add), ["NBO", "I8K"], ["WS"], 256)
    xyc = {}
    for m in sorted(set(len(team) for team in TEAMS + CREWS)):
        xyc[m] = [fill("XY%d" % m, 0, V4 * m, 193.0), fill("XY%d" % m, V4 * m, 2 * V4 * m, 40.0), fill("XY%d" % m, 2 * V4 * m, 9 * NB * m, 0.0)]
    allk = lambda b: ["%s%d" % (b, k) for k in range(NCH)]
    W4 = V4 * NCH
    keys = lambda T: [(T.P_a0[:, PK0:PK0 + W4], T.ID[:], T.KO[:])] + [(T.P_a0[:, PK0 + o:PK0 + W4:4], T.I4[:], T.VB[:, V4 * o:V4 * (o + 1)]) for o in range(4)]
    V(lambda g, T: g.vector.tensor_copy(T.VB[:], T.VI[:]), ["VI%d.%d" % (k, o) for k in range(NCH) for o in range(4)], ["VB"], W4)
    TE(lambda g, T: group(g, keys(T)), ["ID", "I4", "KO", "VB"], ["K0"], 64 * 5, 0, "a0")
    V(lambda g, T: g.vector.tensor_tensor_scan(T.SC[:], T.RST[:], T.P_a0[:, PK0:PK0 + W4], 0.0, OP.add, OP.max), ["K0", "RST"], allk("SC"), W4, 0, "a0")
    TE(lambda g, T: group(g, keys(T) + [(T.P_a0[:, PK0 + o:PK0 + W4:4], T.IM1[:], T.SC[:, 3:W4:4]) for o in range(4)]), ["IM1"] + allk("SC"), ["K0"], 64 * 9, 0, "a0")
    V(lambda g, T: g.vector.tensor_scalar(T.E[:], T.P_a0[:, PK0:PK0 + W4], -0.5, None, OP.is_gt), ["K0"], allk("E"), W4, 0, "a0")
    TE(lambda g, T: group(g, [(T.P_a0[:, PK0:PK0 + V4], T.ID[:], T.B4[:])] + [(T.P_a0[:, PK0:PK0 + V4], T[w][:], T.E[:, o:W4:4]) for o, w in ((1, "ID"), (2, "I2"), (3, "I3"))]),
       ["I2", "I3"] + allk("B4.") + allk("E"), ["K0"], 256, 0, "a0")
    V(lambda g, T: g.vector.tensor_copy(T.LU[:], T.P_a0[:, PK0:PK0 + V4]), ["K0"], allk("LU"), V4, 0, "a0")
    S(lambda g, T: g.scalar.activation(lists(T, 0, 0, NCH), T.P_a0[:, PK0:PK0 + V4], AF.Copy), ["K0"], ["LF%d.0" % k for k in range(NCH)], V4, 0, "a0")
    for k in range(NCH):
        V(lambda g, T, k=k: g.vector.tensor_copy(saved(T, 0, k), X(T, "PGI", k)), ["PGI%d" % k], ["CW%d.0" % k], 256, k)
        S(lambda g, T, k=k: g.scalar.activation(T.LIMP[:, CN * k:CN * (k + 1)], T.LIM[:, CN * k:CN * (k + 1)].indirect(T.LL[:]), AF.Copy),
          ["LIM", "LL"], ["LIMP%d" % k], C["ga"] * CN + 40, k)
    for s in range(NSL):
        for team in TEAMS if s < NSL - 1 else TEAMS[:-1] + CREWS[TEAMS[-1][0]:]:
            for crew in CREWS:
                if crew[0] in team:
                    fetch(s, crew, C, V, S)
                    for k in crew:
                        steps(s, k, team, crew, C, op, V, S, TE)
                    if crew[0] == 0:
                        ahead(s, C, op, V)
                    leave(s, crew, C, op, V, dma)
            first = len(ops)
            values(s, team, C, V, S, TE, dma, xyc[len(team)])
            if s == NSL - 1:
                for o in ops[first:]:
                    o["k"] = LAST
    return ops


def ahead(s, C, op, V):
    if s < NSL - 1:
        op("g", ("t", 0, s + 1), ["XB0", "PRE0"] + ["csent%d.%d" % (AFTER, s - 1)] * (s > 0), ["tsent%d" % s], None, C["send"])
        op("hop", "t", ["tsent%d" % s], ["XB%d" % (s + 1), "PRE%d" % (s + 1)], None, 28000, 0, "tl%d" % (s + 1))
    both = lambda at: ["%s%d.%d" % (b, k, at) for b in ("CW", "LF") for k in range(NCH)]
    op("g", ("w", 1, s), both(s), ["wsent%d" % s], None, C["send"])
    op("hop", "w", ["wsent%d" % s], both(s + 1), None, WH, 1, "wl_1_%d" % s)
    V(lambda g, T: g.vector.tensor_copy(T.LN[:], lists(T, s + 1, 0, NCH)), ["LF%d.%d" % (k, s + 1) for k in range(NCH)], ["LN"], V4, 0)


def values(s, team, C, V, S, TE, dma, xyc):
    k, m = team[0], len(team)
    kt = lambda b: "%s%d" % (b, k)
    each = lambda b: ["%s%d" % (b, j) for j in team]
    nb, nv = NB * m, V4 * m
    ab, lb = "a%d" % k, "l%d" % k
    home = s == NSL - 1
    pma, pmb = PN + 3 * nb, PN + 4 * nb
    k0, m0 = [(x[0], len(x)) for x in TEAMS if k in x][0]
    kept = lambda sl: HPW * (m0 * sl - NSL * (k - k0))

    def PS(T, a, b, step=1):
        return T["P_" + ab][:, a:b:step]

    def PL(T, a, b, step=1):
        return T["P_" + lb][:, a:b:step]

    def Y(T, name, a, b, step=1):
        return T[name][:, PER[name][0] * k + a:PER[name][0] * k + b:step]

    def one(P, T, at, o, by_order):
        return P(T, at + nb * o, at + nb * (o + 1)) if by_order else P(T, at + o, at + nv, 4)

    def laid(P, T, at, w, name, a, by_order):
        if not by_order:
            return [(P(T, at, at + nv), T[w][:], Y(T, name, a, a + nv))]
        return [(one(P, T, at, o, True), T[w][:], Y(T, name, a + o, a + nv, 4)) for o in range(4)]

    def parts(P, T, at, w, sl, by_order=False):
        if sl < 0:
            return [(one(P, T, at, o, by_order), T[w][:], T.VB[:, V4 * o + NB * k:V4 * o + NB * k + nb]) for o in range(4)]
        a = kept(sl) + V4 * (k - k0)
        return laid(P, T, at, w, "HP", a, by_order) + laid(P, T, at, w, "HP", a + V4 * m0, by_order)

    def small(name, out, in_, func, bias, scale, alu, c, r, w, n, bank):
        if ON[name] == "s":
            S(lambda g, T: g.scalar.activation(out(T), in_(T), func, bias=bias, scale=scale), r, w, n, k, bank)
        else:
            V(lambda g, T: g.vector.tensor_scalar(out(T), in_(T), c, None, alu), r, w, n, k, bank)

    st, hp = ("HP%d.%d" % (k0, s - 1) if s else "VB"), "HP%d.%d" % (k, s)
    g0, mt = kept(s) + HPW * (k - k0), kept(s - 1) + 2 * V4 * m0 + NB * (k - k0)
    TE(lambda g, T: group(g, [(PS(T, PN, PN + 3 * nb), T.WB[:, 15 - a:143 - a], Y(T, "NS", a, NST * CN * m, 16)) for a in range(16)]),
       ["NS%d.%d" % (j, t) for j in team for t in range(NST)] + ["WB"], [kt("PN")], 1024, k, ab)
    small("FM", lambda T: Y(T, "FM", 0, 3 * nb), lambda T: PS(T, PN, PN + 3 * nb), AF.Relu, -15.0, -1.0, OP.is_lt, -15.0, [kt("PN")], [kt("FM")], 3 * nb, ab)

    def msum(g, T):
        for at, w in ((pma, "RH"), (pmb, "R1")):
            last = group(g, [(PS(T, at, at + nb), T[w][:], Y(T, "FM", t * nb, (t + 1) * nb)) for t in range(NST)])
        return last
    TE(msum, [kt("FM"), "RH", "R1"], [kt("PM")], 384, k, ab)
    small("RR", lambda T: Y(T, "RR", 0, 3 * nb), lambda T: PS(T, PN + 2 * nb, PN + 5 * nb), AF.Identity, 191.75, 1.0, OP.add, 191.75, [kt("PN"), kt("PM")], [kt("RR")], 3 * nb, ab)

    def early(g, T):
        terms = [(PL(T, 0, 9 * nb), T.ID[:], T["XY%d" % m][:])]
        terms += laid(PL, T, 0, "IM64", "E", 0, home) + laid(PL, T, nv, "I64", "E", 0, home) + parts(PL, T, 0, "ID", s - 1, home)
        if s:
            terms += [(PL(T, 2 * nv, 9 * nb), T.ID[:], Y(T, "HP", mt, mt + nb))]
        return group(g, terms, True, False)
    TE(early, xyc + ["ID", "IM64", "I64", st] + each("E"), [kt("PL")], 64 * (18 if home else 6 + (s == 0)), k, lb)
    TE(lambda g, T: group(g, [(PL(T, 2 * nv, 9 * nb), T.ID[:], Y(T, "FM", t * nb, (t + 1) * nb)) for t in range(NST)], False, False), ["ID", kt("FM"), kt("PM")], [kt("PL")], 192, k, lb)

    def late(g, T):
        terms = []
        for o in range(4):
            x, y = one(PL, T, 0, o, home), one(PL, T, nv, o, home)
            terms += [(y, T.IMH[:], Y(T, "RR", 0, nb)), (x, T.IM2[:], Y(T, "RR", nb, 2 * nb)), (x, T.ID[:], Y(T, "RR", 2 * nb, 3 * nb))]
        return group(g, terms, False, True)
    TE(late, ["ID", "IMH", "IM2", kt("RR")], [kt("PL")], 768, k, lb)
    small("HP", lambda T: Y(T, "HP", g0, g0 + 9 * nb), lambda T: PL(T, 0, 9 * nb), AF.Relu, 0.0, 1.0, OP.max, 0.0, [kt("PL")], [hp], 9 * nb, lb)
    if home:
        V(lambda g, T: g.vector.tensor_tensor(Y(T, "YV", 0, nv), Y(T, "HP", g0, g0 + nv), Y(T, "HP", g0 + nv, g0 + 2 * nv), OP.add), [hp], [kt("YV")], 2 * nv, k)
        S(lambda g, T: g.scalar.activation(Y(T, "YM", 0, nb), Y(T, "HP", g0 + 2 * nv, g0 + 9 * nb), AF.Copy), [hp], [kt("YM")], nb, k)
        for j in team:
            for o in range(4):
                dma("qs", lambda T, o=o, j=j: T.yv[o::4, CN * j:CN * (j + 1)], lambda T, o=o, j=j: Y(T, "YV", nb * o + NB * (j - k), nb * o + NB * (j - k + 1)), [kt("YV")], [], 2000, j)
            dma("qs", lambda T, j=j: T.ym[:, CN * j:CN * (j + 1)], lambda T, j=j: X(T, "YM", j), [kt("YM")], [], 2000, j)
        return
    keys = lambda T: [(PS(T, PK1, PK1 + nv), T.ID[:], T.KO[:, 0:nv])] + parts(PS, T, PK1, "I4", s)
    TE(lambda g, T: group(g, keys(T)), ["ID", "I4", "KO", hp], [kt("K1")], 64 * 3, k, ab)
    V(lambda g, T: g.vector.tensor_tensor_scan(Y(T, "SC", 0, nv), T.RST[:, 0:nv], PS(T, PK1, PK1 + nv), 0.0, OP.add, OP.max), [kt("K1"), "RST"], each("SC"), nv, k, ab)
    TE(lambda g, T: group(g, keys(T) + [(one(PS, T, PK1, o, False), T.IM1[:], Y(T, "SC", 3, nv, 4)) for o in range(4)]), ["IM1", hp] + each("SC"), [kt("K1")], 64 * 7, k, ab)
    small("E", lambda T: Y(T, "E", 0, nv), lambda T: PS(T, PK1, PK1 + nv), AF.Relu, 1.0, 1.0, OP.is_gt, -0.5, [kt("K1")], each("E"), nv, ab)
    TE(lambda g, T: group(g, [(PS(T, PLU, PLU + nb), T.ID[:], T.B4[:, NB * k:NB * k + nb])] + [(PS(T, PLU, PLU + nb), T[w][:], Y(T, "E", o, nv, 4)) for o, w in ((1, "ID"), (2, "I2"), (3, "I3"))]),
       ["ID", "I2", "I3"] + each("B4.") + each("E"), [kt("PLU")], 256, k, ab)
    V(lambda g, T: g.vector.tensor_copy(Y(T, "LU", 0, nb), PS(T, PLU, PLU + nb)), [kt("PLU")], each("LU"), nb, k, ab)
    small("LF", lambda T: lists(T, s + 1, k, m), lambda T: PS(T, PLU, PLU + nb), AF.Identity, 0.0, 1.0, OP.add, 0.0, [kt("PLU")], ["LF%d.%d" % (j, s + 1) for j in team], nb, ab)


def steps(s, k, team, crew, C, op, V, S, TE):
    kt = lambda b: "%s%d" % (b, k)
    ks = lambda b, at=s: "%s%d.%d" % (b, k, at)
    lo = CN * k
    ab, lb = "a%d" % k, "l%d" % k
    GA = C["ga"]

    def PS(T, a, b, step=1):
        return T["P_" + ab][:, a:b:step]

    def PL(T, a, b, step=1):
        return T["P_" + lb][:, a:b:step]

    def signs(T, t):
        at = NST * CN * team[0] + CN * (len(team) * t + k - team[0])
        return T.NS[:, at:at + CN]

    def mine(T, name, half, a=0, b=CN):
        at = 2 * CN * crew[0] + CN * (len(crew) * half + k - crew[0])
        return T[name][:, at + a:at + b]

    def lrep(g, T):
        for e in range(REP):
            last = g.tensor.matmul(PL(T, e, REP * CN, REP), T.ID[:], T.LIMP[:, lo:lo + CN], True, True)
        return last
    if s == 0 or k in [x[0] for x in TEAMS]:
        TE(lrep, [kt("LIMP"), "ID"], [kt("PL")], REP * CN, k, lb)

    for t in range(NST):
        if t == 0:
            cur, keep, tags, five, mm5 = (lambda T: mine(T, "CF", 0)), (lambda T: mine(T, "CF", 0)), ("C32", "C32"), "I5F", 4 * CN
        else:
            cur, keep, tags, five, mm5 = (lambda T: X(T, "C16", k)), (lambda T: X(T, "CI", k)), ("C16", "CI"), "I5H", CN
        for u in range(SUB):
            f0, f1, y0, y1 = 16 * HW * u, 16 * HW * (u + 1), HW * u, HW * (u + 1)
            fu, gu = "F%d.%d" % (k, u), "G%d.%d" % (k, u)
            S(lambda g, T, y0=y0, y1=y1, f0=f0, f1=f1: g.scalar.activation(X(T, "F", k, f0, f1), T.TB[:, TBW * s:TBW * s + TW].indirect(mine(T, "OF", 0, y0, y1)), AF.Copy),
              ["XB%d" % s, kt("OFF")], [fu], GA * 16 * HW + 40, k)
            who = copier(s, k, t, u)
            if who == "g":
                op("g", lambda g, T, f0=f0, f1=f1: g.affine_select(X(T, "F2", k, f0, f1), X(T, "F", k, f0, f1), [[0, 16 * HW]], OP.is_ge, 0.0, 0, 0), [fu], [gu], None, 200 + 32 * HW, k)
            elif who == "v":
                V(lambda g, T, f0=f0, f1=f1: g.vector.tensor_copy(X(T, "F2", k, f0, f1), X(T, "F", k, f0, f1)), [fu], [gu], 8 * HW, k)
            else:
                S(lambda g, T, f0=f0, f1=f1: g.scalar.activation(X(T, "F2", k, f0, f1), X(T, "F", k, f0, f1), AF.Copy), [fu], [gu], 16 * HW, k)
        dts = ["D%d.%d" % (k, u) for u in range(SUB)]
        for u in range(SUB):
            f0, f1, y0, y1 = 16 * HW * u, 16 * HW * (u + 1), HW * u, HW * (u + 1)
            fu, gu, du = "F%d.%d" % (k, u), "G%d.%d" % (k, u), dts[u]
            V(lambda g, T, y0=y0, y1=y1, f0=f0, f1=f1: g.vector.tensor_tensor(X(T, "D", k, f0, f1), X(T, "F", k, f0, f1).indirect(mine(T, "OF", 1, y0, y1)), X(T, "F2", k, f0, f1), OP.subtract),
              [fu, gu, kt("PO")], [du], GA * 16 * HW + 45, k)
            S(lambda g, T, f0=f0, f1=f1: g.scalar.activation(X(T, "D", k, f0, f1), X(T, "D", k, f0, f1), AF.Abs), [du], [du], 16 * HW, k)
            for q in range(NQ):
                V(lambda g, T, f0=f0, f1=f1, y0=y0, y1=y1, q=q: g.vector.tensor_tensor(X(T, "C", k, f0 + q, f1, NQ), X(T, "D", k, f0 + q, f1, NQ), PL(T, REP * y0, REP * y1), OP.is_gt),
                  [du, kt("PL")], ["C%d.%d.%d" % (k, u, q)], REP * HW, k, lb)

        def asum(T, w, x, als):
            return [(PS(T, PA, PA + CN), T[w][:, 15 - a:143 - a], X(T, x, k, a, None, 16)) for a in als]
        TE(lambda g, T: group(g, asum(T, "WB", "D", range(16)), True, False), dts + ["WB"] + ["LF%d.0" % j for j in range(NCH) if s + k + t == 0], [kt("PA")], 16 * CN, k, ab)
        for q in range(NQ):
            TE(lambda g, T, q=q: group(g, asum(T, "WK", "C", range(q, 16, NQ)), False, q == NQ - 1),
               ["C%d.%d.%d" % (k, u, q) for u in range(SUB)] + ["WK"], [kt("PA")], REP * CN, k, ab)
        ns = "NS%d.%d" % (k, t)
        S(lambda g, T, t=t: g.scalar.activation(signs(T, t), PS(T, PA, PA + CN), AF.Sign, bias=-8.0 * BIG), [kt("PA")], [ns], CN, k, ab)
        S(lambda g, T: g.scalar.activation(X(T, "RL", k), PS(T, PA, PA + CN), AF.Relu, bias=-8.0 * BIG), [kt("PA")], [kt("RL")], CN, k, ab)
        TE(lambda g, T, t=t, cur=cur, five=five: group(g, [(PS(T, PB, PB + CN), T.CST[:], T.ONES[:, 0:CN]), (PS(T, PB, PB + CN), T[five][:], cur(T)),
                                                           (PS(T, PB, PB + CN), T.WS[:], signs(T, t)), (PS(T, PB, PB + CN), T.IDF[:], X(T, "RL", k))]),
           [ns, kt("RL"), "WS", "IDF", "CST", "ONES", five, kt(tags[0])], [kt("PB")], 6 * CN + mm5, k, ab)
        V(lambda g, T, keep=keep: g.vector.tensor_tensor(X(T, "O2", k), PS(T, PB, PB + CN), keep(T), OP.max), [kt("PB"), kt(tags[1])], [kt("O2")], CN, k, ab)
        if t < NST - 1:
            V(lambda g, T: g.vector.tensor_scalar(X(T, "CI", k), X(T, "O2", k), 2047, None, OP.bitwise_and), [kt("O2")], [kt("CI")], CN, k)
            V(lambda g, T: g.vector.tensor_copy(mine(T, "OF", 0), X(T, "CI", k)), [kt("CI")], [kt("OFF")], CN, k)
            V(lambda g, T: g.vector.tensor_copy(X(T, "C16", k), X(T, "CI", k)), [kt("CI")], [kt("C16")], CN, k)


def fetch(s, team, C, V, S):
    k, m = team[0], len(team)
    each = lambda b: ["%s%d" % (b, j) for j in team]
    n, p0 = CN * m, TBW * s + TW + 4 * CN * k
    lu = lambda T: T.LU[:, NB * k:NB * (k + m)]
    half = lambda T, name, a, b: T[name][:, 2 * CN * k + n * a:2 * CN * k + n * b]
    if s == 0:
        V(lambda g, T: g.vector.tensor_copy(half(T, "CF", 0, 1), T.PGI[:, 4 * CN * k:4 * CN * (k + m)].indirect(lu(T))), each("PGI") + each("LU"), each("C32"), C["ga"] * n + 45, k)
    else:
        S(lambda g, T: g.scalar.activation(half(T, "CF", 0, 1), saved(T, s, k, m).indirect(lu(T)), AF.Copy), ["CW%d.%d" % (j, s) for j in team] + each("LU"), each("C32"), C["ga"] * n + 40, k)
    V(lambda g, T: g.vector.tensor_tensor(half(T, "CF", 1, 2), T.TB[:, p0:p0 + 4 * n].indirect(lu(T)), T.POS[:, 0:n], OP.add), ["PRE%d" % s, "POS"] + each("LU"), each("PF"), C["ga"] * n + 45, k)
    if s and k in DIRECT:
        V(lambda g, T: g.vector.tensor_copy(half(T, "OF", 0, 1), saved(T, s, k, m).indirect(lu(T))), ["CW%d.%d" % (j, s) for j in team] + each("LU"), each("OFF"), C["ga"] * n + 45, k)
        V(lambda g, T: g.vector.tensor_copy(half(T, "OF", 1, 2), half(T, "CF", 1, 2)), each("PF"), each("PO"), n, k)
    elif s == 0 or m > 1:
        V(lambda g, T: g.vector.tensor_copy(half(T, "OF", 0, 1), half(T, "CF", 0, 1)), each("C32"), each("OFF"), n, k)
        V(lambda g, T: g.vector.tensor_copy(half(T, "OF", 1, 2), half(T, "CF", 1, 2)), each("PF"), each("PO"), n, k)
    else:
        V(lambda g, T: g.vector.tensor_copy(half(T, "OF", 0, 2), half(T, "CF", 0, 2)), each("C32") + each("PF"), each("OFF") + each("PO"), 2 * n, k)


def leave(s, team, C, op, V, dma):
    k, m = team[0], len(team)
    ks = lambda b: "%s%d.%d" % (b, k, s)
    nxt = ["CW%d.%d" % (j, s + 1) for j in team]
    V(lambda g, T: g.vector.tensor_scalar(message(T, "c", k, s, 0), T.O2[:, CN * k:CN * (k + m)], 2047, None, OP.bitwise_and), ["O2%d" % j for j in team], [ks("CO")], CN * m, k)
    op("g", ("c", k, s), [ks("CO")], [ks("csent")], None, C["send"], k)
    op("hop", "c", [ks("csent")], [ks("CL")], None, C["hop"], k, "cl_%d_%d" % (k, s))
    V(lambda g, T: g.vector.tensor_copy(saved(T, s + 1, k, m).indirect(T.LN[:, NB * k:NB * (k + m)]), message(T, "c", k, s, 1)), [ks("CL"), "LN"], nxt, C["sc"] * CN * m + 45, k)
    if s == NSL - 1:
        for j in team:
            dma("qa" if j == NCH - 1 else "qs", lambda T, j=j: T.yg[:, 4 * CN * j:4 * CN * (j + 1)], lambda T, j=j: saved(T, NSL, j), nxt, [], 2500, j, 500)


def depend(ops):
    lastw, readers = {}, {}
    deps = [set() for _ in ops]
    for o in ops:
        i = o["i"]
        for r in o["r"]:
            if r in lastw:
                deps[i].add(lastw[r])
        for w in o["w"]:
            if w in lastw:
                deps[i].add(lastw[w])
            deps[i].update(readers.get(w, ()))
        for r in o["r"]:
            readers.setdefault(r, set()).add(i)
        for w in o["w"]:
            lastw[w] = i
            readers[w] = set()
        deps[i].discard(i)
    return deps


def plan(ops, deps, C):
    n, sem = len(ops), C["sem"]
    succ = [[] for _ in range(n)]
    for i in range(n):
        for d in deps[i]:
            succ[d].append(i)
    tail = [0.0] * n
    for i in range(n - 1, -1, -1):
        tail[i] = ops[i]["cost"] + ops[i]["eng"] + max([tail[j] + sem for j in succ[i]] + [0.0])
    x, prio = SEED, []
    for i, o in enumerate(ops):
        x = (x * 1103515245 + 12345) % 2 ** 31
        prio.append(1e9 - i if o["q"] in ("qs", "qa") and not o["r"] else tail[i] - LAG * o["k"] - GAP * (o["k"] // 2) + AMP * x / 2 ** 31)
    left = [len(d) for d in deps]
    ready_at, fin = [0.0] * n, [0.0] * n
    free, bankfree, bankq = {}, {}, {}
    avail = [i for i in range(n) if left[i] == 0]
    order = []
    while len(order) < n:
        best = None
        for i in avail:
            o = ops[i]
            at = ready_at[i]
            if o["q"] != "hop":
                at = max(at, free.get("s" if o["q"] == "qa" else o["q"], 0.0))
            b = o["bank"]
            if b and bankq.get(b) not in (None, o["q"]):
                at = max(at, bankfree[b] + sem)
            key = (at, o["cost"] > SHORT, -prio[i], i)
            if best is None or key < best:
                best = key
        i, at = best[3], best[0]
        o = ops[i]
        avail.remove(i)
        if o["q"] in ("qs", "qa"):
            free["s" if o["q"] == "qa" else "qs"] = at + 100
            free["dma"] = max(free.get("dma", 0.0), at) + o["eng"]
            fin[i] = free["dma"] + o["cost"]
        else:
            fin[i] = at + o["cost"]
            if o["q"] != "hop":
                free[o["q"]] = fin[i]
        if o["bank"]:
            bankq[o["bank"]] = o["q"]
            bankfree[o["bank"]] = fin[i]
        order.append(i)
        for j in succ[i]:
            left[j] -= 1
            ready_at[j] = max(ready_at[j], fin[i] + sem)
            if left[j] == 0:
                avail.append(j)
    return order, fin


_PLAN = []


def get_plan():
    if not _PLAN:
        ops = build(COST)
        deps = depend(ops)
        order, fin = plan(ops, deps, COST)
        _PLAN.extend([ops, order, deps, fin])
    return _PLAN


get_plan()


def helpers(topo, cores, r):
    own, n = cores[r], len(cores)
    free = [c for c in topo.cores_of(own) if c not in cores]
    ports = [c for c in free if topo.may_write(c, cores[(r - 1) % n])]
    port = [c for c in ports if topo.die(c) == topo.die(own)]
    far = [c for c in ports if c not in port]
    rest = [c for c in free if c not in ports and topo.die(c) != topo.die(own)]
    return port, {1: far[0], 2: rest[0], 3: far[-1]}


def bits(topo, a, b):
    return len(topo.engines(a, b))


def rank_program(g, core, T, topo):
    cores = list(T.cores)
    rank = T.rank_of(core)
    if rank is not None:
        run_rank(g, core, T, topo, cores, rank)
        return
    for r in range(len(cores)):
        port, table = helpers(topo, cores, r)
        if core in port or core in table.values():
            hand_on(g, core, T, topo, cores, r, [k for k in range(NCH) if port[k % len(port)] == core], [s for s in table if table[s] == core])


def hand_on(g, core, T, topo, cores, r, ks, slots):
    own, n, loc = cores[r], len(cores), 0

    def remote(out, in_, sem, dst):
        rid, pid = topo.addr(dst, core)
        g.remote_dma(out, in_, T.sem[sem], T.sem.loc, pid, rid, topo.mask(core, dst))
        return bits(topo, core, dst)

    ops, order = get_plan()[:2]
    for i in order:
        if ops[i]["q"] != "g" or not isinstance(ops[i]["fn"], tuple):
            continue
        kind, k, s = ops[i]["fn"]
        if kind == "t" and s in slots:
            g.wait_ge(T.sem["tr%d" % s], bits(topo, own, core))
            loc += remote(T.TB[:, TBW * s:TBW * (s + 1)], T.TB[:, TBW * s:TBW * (s + 1)], "tl%d" % s, cores[(r - s) % n])
        elif kind != "t" and k in ks:
            g.wait_ge(T.sem["%sr_%d_%d" % (kind, k, s)], bits(topo, own, core))
            loc += remote(message(T, kind, k, s, 1), message(T, kind, k, s, 0), "%sl_%d_%d" % (kind, k, s), cores[(r - 1) % n])
    g.wait_ge(T.sem.loc, loc)


def run_rank(g, core, T, topo, cores, rank):
    n = len(cores)
    port, table = helpers(topo, cores, rank)
    ops, order, deps, _f = get_plan()
    eng = {"v": g.vector, "s": g.scalar, "t": g.tensor, "g": g, "qs": g.sync, "qa": g.scalar}
    semname = {"v": "v", "s": "s", "t": "t", "g": "gc"}
    count = {"v": 0, "s": 0, "t": 0, "g": 0}
    done, waited, banks, loc, dmas = {}, {}, {}, [0], []
    place = {i: at for at, i in enumerate(order)}

    def wait(q, ds):
        known = waited.setdefault("s" if q == "qa" else q, {})
        for d in sorted((d for d in ds if d in done), key=lambda d: -place[d]):
            sem, val, before = done[d]
            if known.get(sem, 0) < val:
                eng[q].wait_ge(T.sem[sem], val)
                known[sem] = val
                for x in before:
                    known[x] = max(known.get(x, 0), before[x])
        return dict(known)

    def remote(out, in_, sem, dst):
        rid, pid = topo.addr(dst, core)
        g.remote_dma(out, in_, T.sem[sem], T.sem.loc, pid, rid, topo.mask(core, dst))
        loc[0] += bits(topo, core, dst)

    for i in order:
        o = ops[i]
        q = o["q"]
        if q == "hop":
            if o["fn"] == "t":
                s = int(o["sem"][-1])
                src = helpers(topo, cores, (rank + s) % n)[1][s]
            else:
                near = helpers(topo, cores, (rank + 1) % n)[0]
                src = near[o["k"] % len(near)]
            done[i] = (o["sem"], bits(topo, src, core), {})
            continue
        need = [d for d in deps[i] if not (q == "t" and ops[d]["q"] == "t")]
        if o["bank"]:
            need += [d for qq, d in banks.get(o["bank"], {}).items() if qq != q]
            banks.setdefault(o["bank"], {})[q] = i
        before = wait(q, need)
        if q in ("qs", "qa"):
            out, in_ = o["fn"]
            eng[q].dma_start(out(T), in_(T)).then_inc(T.sem[o["sem"]], 16)
            dmas.append(o["sem"])
            done[i] = (o["sem"], 16, before)
        elif q == "g" and isinstance(o["fn"], tuple):
            kind, k, s = o["fn"]
            if kind == "t":
                remote(T.TB[:, TBW * s:TBW * (s + 1)], T.TB[:, 0:TBW], "tr%d" % s, table[s])
            else:
                remote(message(T, kind, k, s, 0), message(T, kind, k, s, 0), "%sr_%d_%d" % (kind, k, s), port[k % len(port)])
        else:
            ins = o["fn"](g, T)
            count[q] += 1
            ins.then_inc(T.sem[semname[q]], 1)
            done[i] = (semname[q], count[q], before)
    for q in ("v", "s", "t", "g"):
        g.wait_ge(T.sem[semname[q]], count[q])
    g.wait_ge(T.sem.loc, loc[0])
    for sem in dmas:
        g.wait_ge(T.sem[sem], 16)
